import numpy as np
import ml_dtypes


def mxq(x, axis, fmt="e4m3"):
    dtype, down = {"e4m3": (ml_dtypes.float8_e4m3fn, 7), "e5m2": (ml_dtypes.float8_e5m2, 14)}[fmt]
    v = np.moveaxis(np.asarray(x, np.float32).astype(ml_dtypes.bfloat16).astype(np.float64), axis, -1)
    blocks = v.reshape(v.shape[:-1] + (-1, 32))
    amax = np.abs(blocks).max(-1, keepdims=True)
    byte = np.maximum(np.where(amax > 0, np.frexp(amax)[1] - 1 + 127, 0) - down, 1)
    scale = np.exp2(byte - 127.0)
    codes = (blocks / scale).astype(np.float32).astype(dtype).astype(np.float64)
    return np.moveaxis((codes * scale).reshape(v.shape), -1, axis)


WIDE = False


def mx_kscale(k):
    if not WIDE:
        return np.ones(k)
    levels = np.array([18, -18])
    if k % 512:
        return np.exp2(np.random.permutation(np.resize(levels, k // 32))).repeat(32)
    a = np.empty((k // 512, 16))
    for p in range(k // 512):
        a[p, :8] = np.random.permutation(np.resize(levels, 8))
        for g in range(8):
            far = levels[np.abs(levels - a[p, g]) >= 10]
            a[p, g + 8] = far[np.random.randint(len(far))]
    return np.exp2(a.ravel()).repeat(32)


def f64(x):
    return np.asarray(x).astype(np.float64)


def striped(idx):
    return np.tile(np.asarray(idx).reshape(-1, 16).T, (8, 1)).astype(np.uint16)


def unstriped(offs):
    return offs[:16].T.reshape(-1).astype(np.int64)


B, N, T, D, R, TU = 1, 512, 2048, 512, 512, 2048


def setup_inputs():
    n = np.random.standard_normal
    idx = np.random.permutation(T)[:B * N]
    uidx = np.random.permutation(TU)[:B * R]
    s = mx_kscale(D)[:, None]
    z = np.ones(TU)
    z[uidx] = mx_kscale(B * R)
    u = np.ones(T)
    u[idx] = mx_kscale(B * N)
    r = np.random.uniform(0.5, 2.0, T) * u
    ur = np.random.uniform(0.5, 2.0, TU) * z
    return {
        "uT": (n((D, TU)) * s / ur).astype(np.float32),
        "vT": (n((D, T)) * (1.00 / np.sqrt(D)) / s / r).astype(np.float32),
        "y": n((B, R, N)).astype(np.float32),
        "us": ur[uidx].reshape(B, R, 1).astype(np.float32),
        "ts": np.tile(r, (128, 1)).astype(np.float32),
        "offs": striped(idx),
        "uoffs": striped(uidx),
    }


def reference(uT, vT, y, us, ts, offs, uoffs):
    idx = unstriped(offs)
    pick = lambda x: x[:, idx].reshape(x.shape[0], B, N).transpose(1, 0, 2)
    uidx = unstriped(uoffs)
    w = pick(f64(vT))
    x = f64(uT)[:, uidx].reshape(D, B, R).transpose(1, 0, 2)
    a = mxq(x, 1, "e4m3").transpose(0, 2, 1) @ mxq(w, 1, "e4m3")
    sc = f64(us) * pick(f64(ts))[:, :1, :]
    a = a * sc
    q = a - f64(y)
    g = q / (1.0 + q * q)
    h = sc * g
    dv = mxq(x, 2, "e4m3") @ mxq(h, 1, "e5m2")
    gv = np.zeros((D, T))
    gv[:, idx] = dv.transpose(1, 0, 2).reshape(D, B * N)
    du = mxq(w, 2, "e4m3") @ mxq(h, 2, "e5m2").transpose(0, 2, 1)
    gu = np.zeros((D, TU))
    gu[:, uidx] = du.transpose(1, 0, 2).reshape(D, B * R)
    return gv, gu

@@ -1,0 +1,239 @@
+from contextlib import ExitStack
+
+import concourse.mybir as mybir
+from concourse.masks import make_identity
+
+F32 = mybir.dt.float32
+BF16 = mybir.dt.bfloat16
+U32 = mybir.dt.uint32
+I32 = mybir.dt.int32
+U16 = mybir.dt.uint16
+U8 = mybir.dt.uint8
+E4M3 = mybir.dt.float8_e4m3fn_x4
+E5M2 = mybir.dt.float8_e5m2_x4
+ACT = mybir.ActivationFunctionType
+MULT = mybir.AluOpType.mult
+SUB = mybir.AluOpType.subtract
+
+P = 128
+PACK = 4
+L = 512
+T = 2048
+FLOPS = 3 * 2 * L * L * L
+BYTES = 4 * (4 * L * T + L * L + L + T) + 2 * 2 * P * 32
+
+
+def tile_attend_gmf_cau_vu_kernel(tc, uT, vT, y, us, ts, offs, uoffs, out_0, out_1):
+    nc = tc.nc
+    with ExitStack() as ctx:
+        lists = ctx.enter_context(tc.tile_pool(name="lists", bufs=1))
+        sb = ctx.enter_context(tc.tile_pool(name="sb", bufs=1))
+        ps = ctx.enter_context(tc.psum_pool(name="ps", bufs=1))
+
+        cell_list = lists.tile([P, L // 16], U16, name="cell_list")
+        gene_list = lists.tile([P, L // 16], U16, name="gene_list")
+        banks = [ps.tile([P, L], F32, name=f"bank{b}") for b in range(8)]
+
+        def f32_tile(name, width):
+            return sb.tile([P, width], F32, name=name, align_bytes=64)
+
+        def bf16_tile(name):
+            return sb.tile([P, L * PACK], BF16, name=name, align_bytes=64)
+
+        def mx_tiles(name):
+            return (sb.tile([P, L], U32, name=name + "_codes", align_bytes=64),
+                    sb.tile([P, L], U8, name=name + "_scales", align_bytes=64))
+
+        def quantize(dst, src, fmt, c0=0, c1=L):
+            nc.vector.quantize_mx(out=dst[0][:, c0:c1].bitcast(fmt), scales=dst[1][:, c0:c1],
+                                  in_=src[:, PACK * c0:PACK * c1])
+
+        def product(out, lhs, lhs_fmt, m0, rhs, rhs_fmt, n0, n1):
+            nc.tensor.matmul_mx(out=out, lhsT=lhs[0][:, m0:m0 + P].bitcast(lhs_fmt), lhsT_scale=lhs[1][:, m0:m0 + P],
+                                rhs=rhs[0][:, n0:n1].bitcast(rhs_fmt), rhs_scale=rhs[1][:, n0:n1],
+                                start=True, stop=True)
+
+        ident = f32_tile("ident", P)
+        ts_table = f32_tile("ts_table", T)
+        nc.vector.memset(ts_table[:].bitcast(I32), 0)
+        make_identity(nc, ident[:])
+
+        u_planes = [f32_tile(f"u_plane{t}", T) for t in range(PACK)]
+        v_planes = [f32_tile(f"v_plane{t}", T) for t in range(PACK)]
+        us_rows = f32_tile("us_rows", PACK)
+        y_rows = f32_tile("y_rows", PACK * L)
+        uT_rows = uT.rearrange("(p t) c -> p t c", t=PACK)
+        vT_rows = vT.rearrange("(p t) c -> p t c", t=PACK)
+        nc.sync.dma_start(gene_list[:], uoffs)
+        nc.sync.dma_start(u_planes[0][:], uT_rows[:, 0, :])
+        nc.sync.dma_start(cell_list[:], offs)
+        for t in range(1, PACK):
+            nc.sync.dma_start(u_planes[t][:], uT_rows[:, t, :])
+        nc.scalar.dma_start(ts_table[0:1, :], ts[0:1, :])
+        nc.scalar.dma_start(us_rows[:], us.rearrange("b (p s) o -> p (b s o)", s=PACK))
+        for t in range(PACK):
+            nc.sync.dma_start(v_planes[t][:], vT_rows[:, t, :])
+        nc.sync.dma_start(y_rows[:], y.rearrange("b (p s) i -> p (b s i)", s=PACK))
+
+        cell_windows = [f32_tile(f"cell_window{k}", T) for k in range(3)]
+        gene_windows = [f32_tile(f"gene_window{k}", T) for k in range(2)]
+        for window in cell_windows + gene_windows:
+            nc.vector.memset(window[:].bitcast(I32), 0)
+
+        warm = f32_tile("warm", 8)
+        nc.scalar.activation(warm[:, 0:1], ident[:, 0:1], ACT.Abs_reciprocal_sqrt, bias=1.0)
+
+        def turn(dst, src_words, first, step, bank):
+            for s in range(PACK):
+                a = first(s)
+                nc.tensor.transpose(bank[:, s * P:(s + 1) * P], src_words[:, a:a + step * (P - 1) + 1:step], ident[:])
+            return bank[:].bitcast(BF16)
+
+        x_d = bf16_tile("x_d")
+        x_r = bf16_tile("x_r")
+        x_words = x_d[:].bitcast(F32)
+        for t in range(PACK):
+            nc.vector.tensor_copy(x_d[:].rearrange("p (s m t) -> p m s t", s=PACK, t=PACK)[:, :, :, t],
+                                  u_planes[t][:].indirect(gene_list[:]))
+            if t % 2 == 1:
+                u = t // 2
+                turned = turn(None, x_words, lambda s: 2 * P * s + u, 2, banks[4 + u])
+                nc.scalar.copy(x_r[:, u * 1024:(u + 1) * 1024].rearrange("q (e p s) -> q e p s", e=2, s=PACK),
+                               turned.rearrange("q (s p e) -> q e p s", s=PACK, e=2))
+        xq_d = mx_tiles("xq_d")
+        xq_r = mx_tiles("xq_r")
+        quantize(xq_d, x_d, E4M3)
+
+        ts_listed = f32_tile("ts_listed", L)
+        ts_column = f32_tile("ts_column", PACK)
+        sc = f32_tile("sc", PACK * L)
+        nc.vector.tensor_copy(ts_listed[:], ts_table[:].indirect(cell_list[:]))
+        for b in range(PACK):
+            nc.tensor.transpose(banks[6][:, b * P:(b + 1) * P], ts_listed[:, b * P:(b + 1) * P], ident[:])
+        nc.scalar.copy(ts_column[:], banks[6][:, 0:L:P])
+        for b in range(PACK):
+            nc.tensor.transpose(banks[7][:, b * P:(b + 1) * P], ts_column[:, b:b + 1].to_broadcast([P, P]), ident[:])
+        for s in range(PACK):
+            nc.scalar.activation(sc[:].rearrange("p (b s j) -> p s b j", b=PACK, s=PACK)[:, s],
+                                 banks[7][:].rearrange("p (b j) -> p b j", b=PACK), ACT.Copy, scale=us_rows[:, s:s + 1])
+        quantize(xq_r, x_r, E4M3)
+
+        w_d = bf16_tile("w_d")
+        w_i = bf16_tile("w_i")
+        w_words = w_d[:].bitcast(F32)
+        wq_d = mx_tiles("wq_d")
+        wq_i = mx_tiles("wq_i")
+
+        def turn_w(u, bank):
+            turned = turn(None, w_words, lambda s: 2 * s + u, 8, bank)
+            nc.scalar.copy(w_i[:, u * 1024:(u + 1) * 1024].rearrange("q (e p s) -> q e p s", e=2, s=PACK),
+                           turned.rearrange("q (s p e) -> q e p s", s=PACK, e=2))
+
+        for t in range(PACK - 1):
+            nc.vector.tensor_copy(w_d[:, t:L * PACK:PACK], v_planes[t][:].indirect(cell_list[:]))
+            if t == 1:
+                turn_w(0, banks[4])
+        half = L // 2
+        for k in range(2):
+            nc.vector.tensor_copy(w_d[:, k * 1024 + 3:(k + 1) * 1024:PACK],
+                                  v_planes[3][:].indirect(cell_list[:, k * 16:(k + 1) * 16]))
+        for k in range(2):
+            quantize(wq_d, w_d, E4M3, k * half, (k + 1) * half)
+        for b in range(PACK):
+            for s in range(PACK):
+                product(banks[b][:, s * P:(s + 1) * P], xq_d, E4M3, s * P, wq_d, E4M3, b * P, (b + 1) * P)
+
+        q = f32_tile("q", PACK * L)
+        num = f32_tile("num", PACK * L)
+        inv = f32_tile("inv", PACK * L)
+        h_r = bf16_tile("h_r")
+        hq_r = mx_tiles("hq_r")
+        y_chunks = y_rows[:].rearrange("p (s b j) -> p b s j", s=PACK, b=PACK)
+
+        def chunk(tile_, b):
+            return tile_[:, b * L:(b + 1) * L]
+
+        def scaled(b):
+            nc.vector.tensor_tensor(chunk(q, b), banks[b][:], chunk(sc, b), MULT)
+
+        def residual(b):
+            view = chunk(q, b).rearrange("p (s j) -> p s j", s=PACK)
+            nc.vector.tensor_tensor(view, view, y_chunks[:, b], SUB)
+
+        def numerator(b):
+            nc.vector.tensor_tensor(chunk(num, b), chunk(q, b), chunk(sc, b), MULT)
+
+        def square(b):
+            nc.scalar.activation(chunk(inv, b).rearrange("p (j s) -> p j s", s=PACK),
+                                 chunk(q, b).rearrange("p (s j) -> p j s", s=PACK), ACT.Square)
+
+        def root(b):
+            nc.scalar.activation(chunk(inv, b), chunk(inv, b), ACT.Abs_reciprocal_sqrt, bias=1.0)
+
+        def unroot(b):
+            nc.scalar.activation(chunk(inv, b), chunk(inv, b), ACT.Square)
+
+        def weight(b):
+            nc.vector.tensor_tensor(chunk(h_r, b).rearrange("p (j s) -> p j s", s=PACK),
+                                    chunk(num, b).rearrange("p (s j) -> p j s", s=PACK),
+                                    chunk(inv, b).rearrange("p (j s) -> p j s", s=PACK), MULT)
+
+        scaled(0)
+        residual(0)
+        square(0)
+        root(0)
+        for b in range(1, PACK):
+            scaled(b)
+            numerator(b - 1)
+            residual(b)
+            square(b)
+            unroot(b - 1)
+            root(b)
+        numerator(PACK - 1)
+        unroot(PACK - 1)
+        turn_w(1, banks[0])
+        for b in range(PACK):
+            weight(b)
+            if b > 0:
+                quantize(hq_r, h_r, E5M2, (b - 1) * P, b * P)
+        quantize(wq_i, w_i, E4M3)
+        quantize(hq_r, h_r, E5M2, (PACK - 1) * P, L)
+
+        dv_banks = [banks[6], banks[7], banks[1], banks[2]]
+        du_banks = [banks[3], banks[4], banks[5], banks[0]]
+        dv = [f32_tile(f"dv{t}", L) for t in range(PACK)]
+        du = [f32_tile(f"du{t}", L) for t in range(PACK)]
+        for t in range(PACK):
+            product(dv_banks[t][:], xq_r, E4M3, t * P, hq_r, E5M2, 0, L)
+        for t in range(PACK):
+            nc.scalar.copy(dv[t][:], dv_banks[t][:])
+
+        h_i = bf16_tile("h_i")
+        hq_i = mx_tiles("hq_i")
+        h_words = h_r[:].bitcast(F32)
+        for u in range(2):
+            turned = turn(None, h_words, lambda s: 2 * s + u, 8, banks[6 + u])
+            nc.scalar.copy(h_i[:].rearrange("q (p u e s) -> q u p e s", u=2, e=2, s=PACK)[:, u],
+                           turned.rearrange("q (s p e) -> q p e s", s=PACK, e=2))
+
+        out_0_rows = out_0.rearrange("(p t) c -> p t c", t=PACK)
+        out_1_rows = out_1.rearrange("(p t) c -> p t c", t=PACK)
+
+        def place(windows, offsets, values, rows, t):
+            window = windows[t % len(windows)]
+            nc.vector.tensor_copy(window[:].indirect(offsets[:]), values[t][:])
+            nc.sync.dma_start(rows[:, t, :], window[:])
+
+        place(cell_windows, cell_list, dv, out_0_rows, 0)
+        place(cell_windows, cell_list, dv, out_0_rows, 1)
+        quantize(hq_i, h_i, E5M2)
+        for t in range(PACK):
+            product(du_banks[t][:], wq_i, E4M3, t * P, hq_i, E5M2, 0, L)
+        for t in range(PACK):
+            nc.scalar.copy(du[t][:], du_banks[t][:])
+        place(cell_windows, cell_list, dv, out_0_rows, 2)
+        place(gene_windows, gene_list, du, out_1_rows, 0)
+        place(gene_windows, gene_list, du, out_1_rows, 1)
+        place(cell_windows, cell_list, dv, out_0_rows, 3)
+        place(gene_windows, gene_list, du, out_1_rows, 2)
+        place(gene_windows, gene_list, du, out_1_rows, 3)

@@ -34,18 +34,18 @@ def tile_attend_gmf_cau_vu_kernel(tc, uT, vT, y, us, ts, offs, uoffs, out_0, out
         gene_list = lists.tile([P, L // 16], U16, name="gene_list")
         banks = [ps.tile([P, L], F32, name=f"bank{b}") for b in range(8)]
 
-        def f32_tile(name, width):
-            return sb.tile([P, width], F32, name=name, align_bytes=64)
+        def f32_tile(name, width, tag=None):
+            return sb.tile([P, width], F32, name=name, tag=tag or name, align_bytes=64)
 
         def bf16_tile(name):
             return sb.tile([P, L * PACK], BF16, name=name, align_bytes=64)
 
-        def mx_tiles(name):
-            return (sb.tile([P, L], U32, name=name + "_codes", align_bytes=64),
-                    sb.tile([P, L], U8, name=name + "_scales", align_bytes=64))
+        def mx_tiles(name, width=L):
+            return (sb.tile([P, width], U32, name=name + "_codes", tag=name + "_codes", align_bytes=64),
+                    sb.tile([P, width], U8, name=name + "_scales", align_bytes=64))
 
-        def quantize(dst, src, fmt, c0=0, c1=L):
-            nc.vector.quantize_mx(out=dst[0][:, c0:c1].bitcast(fmt), scales=dst[1][:, c0:c1],
+        def quantize(dst, src, fmt, c0=0, c1=L, shift=0):
+            nc.vector.quantize_mx(out=dst[0][:, shift + c0:shift + c1].bitcast(fmt), scales=dst[1][:, shift + c0:shift + c1],
                                   in_=src[:, PACK * c0:PACK * c1])
 
         def product(out, lhs, lhs_fmt, m0, rhs, rhs_fmt, n0, n1):
@@ -64,21 +64,22 @@ def tile_attend_gmf_cau_vu_kernel(tc, uT, vT, y, us, ts, offs, uoffs, out_0, out
         y_rows = f32_tile("y_rows", PACK * L)
         uT_rows = uT.rearrange("(p t) c -> p t c", t=PACK)
         vT_rows = vT.rearrange("(p t) c -> p t c", t=PACK)
-        nc.sync.dma_start(gene_list[:], uoffs)
         nc.sync.dma_start(u_planes[0][:], uT_rows[:, 0, :])
+        nc.sync.dma_start(gene_list[:], uoffs)
         nc.sync.dma_start(cell_list[:], offs)
-        for t in range(1, PACK):
+        nc.sync.dma_start(u_planes[1][:], uT_rows[:, 1, :])
+        nc.sync.dma_start(ts_table[0:1, :], ts[0:1, :])
+        nc.sync.dma_start(us_rows[:], us.rearrange("b (p s) o -> p (b s o)", s=PACK))
+        for t in range(2, PACK):
             nc.sync.dma_start(u_planes[t][:], uT_rows[:, t, :])
-        nc.scalar.dma_start(ts_table[0:1, :], ts[0:1, :])
-        nc.scalar.dma_start(us_rows[:], us.rearrange("b (p s) o -> p (b s o)", s=PACK))
         for t in range(PACK):
             nc.sync.dma_start(v_planes[t][:], vT_rows[:, t, :])
         nc.sync.dma_start(y_rows[:], y.rearrange("b (p s) i -> p (b s i)", s=PACK))
 
-        cell_windows = [f32_tile(f"cell_window{k}", T) for k in range(3)]
-        gene_windows = [f32_tile(f"gene_window{k}", T) for k in range(2)]
+        cell_windows = [f32_tile(f"cell_window{k}", T) for k in range(4)]
+        gene_windows = [f32_tile("gene_window0", T)]
         for window in cell_windows + gene_windows:
-            nc.vector.memset(window[:].bitcast(I32), 0)
+            nc.gpsimd.memset(window[:], 0.0)
 
         warm = f32_tile("warm", 8)
         nc.scalar.activation(warm[:, 0:1], ident[:, 0:1], ACT.Abs_reciprocal_sqrt, bias=1.0)
@@ -102,7 +103,6 @@ def tile_attend_gmf_cau_vu_kernel(tc, uT, vT, y, us, ts, offs, uoffs, out_0, out
                                turned.rearrange("q (s p e) -> q e p s", s=PACK, e=2))
         xq_d = mx_tiles("xq_d")
         xq_r = mx_tiles("xq_r")
-        quantize(xq_d, x_d, E4M3)
 
         ts_listed = f32_tile("ts_listed", L)
         ts_column = f32_tile("ts_column", PACK)
@@ -116,7 +116,6 @@ def tile_attend_gmf_cau_vu_kernel(tc, uT, vT, y, us, ts, offs, uoffs, out_0, out
         for s in range(PACK):
             nc.scalar.activation(sc[:].rearrange("p (b s j) -> p s b j", b=PACK, s=PACK)[:, s],
                                  banks[7][:].rearrange("p (b j) -> p b j", b=PACK), ACT.Copy, scale=us_rows[:, s:s + 1])
-        quantize(xq_r, x_r, E4M3)
 
         w_d = bf16_tile("w_d")
         w_i = bf16_tile("w_i")
@@ -129,25 +128,35 @@ def tile_attend_gmf_cau_vu_kernel(tc, uT, vT, y, us, ts, offs, uoffs, out_0, out
             nc.scalar.copy(w_i[:, u * 1024:(u + 1) * 1024].rearrange("q (e p s) -> q e p s", e=2, s=PACK),
                            turned.rearrange("q (s p e) -> q e p s", s=PACK, e=2))
 
+        half = L // 2
         for t in range(PACK - 1):
             nc.vector.tensor_copy(w_d[:, t:L * PACK:PACK], v_planes[t][:].indirect(cell_list[:]))
             if t == 1:
                 turn_w(0, banks[4])
-        half = L // 2
+
+        quantize(xq_d, x_d, E4M3)
         for k in range(2):
             nc.vector.tensor_copy(w_d[:, k * 1024 + 3:(k + 1) * 1024:PACK],
                                   v_planes[3][:].indirect(cell_list[:, k * 16:(k + 1) * 16]))
-        for k in range(2):
             quantize(wq_d, w_d, E4M3, k * half, (k + 1) * half)
         for b in range(PACK):
             for s in range(PACK):
                 product(banks[b][:, s * P:(s + 1) * P], xq_d, E4M3, s * P, wq_d, E4M3, b * P, (b + 1) * P)
 
+        quantize(xq_r, x_r, E4M3)
+        quantize(wq_i, w_i, E4M3, 0, half)
+
+        gene_windows += [f32_tile("gene_window1", T, "xq_d_codes"), f32_tile("gene_window2", T, "wq_d_codes")]
+        for window in gene_windows[1:]:
+            nc.gpsimd.memset(window[:], 0.0)
+
         q = f32_tile("q", PACK * L)
         num = f32_tile("num", PACK * L)
         inv = f32_tile("inv", PACK * L)
         h_r = bf16_tile("h_r")
-        hq_r = mx_tiles("hq_r")
+        hq_r = mx_tiles("hq_r", half + L)
+        nc.gpsimd.memset(hq_r[0][:, 0:half], 0)
+        nc.gpsimd.memset(hq_r[1][:, 0:half], 0)
         y_chunks = y_rows[:].rearrange("p (s b j) -> p b s j", s=PACK, b=PACK)
 
         def chunk(tile_, b):
@@ -178,62 +187,88 @@ def tile_attend_gmf_cau_vu_kernel(tc, uT, vT, y, us, ts, offs, uoffs, out_0, out
                                     chunk(num, b).rearrange("p (s j) -> p j s", s=PACK),
                                     chunk(inv, b).rearrange("p (j s) -> p j s", s=PACK), MULT)
 
-        scaled(0)
-        residual(0)
-        square(0)
-        root(0)
-        for b in range(1, PACK):
-            scaled(b)
-            numerator(b - 1)
-            residual(b)
-            square(b)
-            unroot(b - 1)
-            root(b)
-        numerator(PACK - 1)
-        unroot(PACK - 1)
-        turn_w(1, banks[0])
-        for b in range(PACK):
-            weight(b)
-            if b > 0:
-                quantize(hq_r, h_r, E5M2, (b - 1) * P, b * P)
-        quantize(wq_i, w_i, E4M3)
-        quantize(hq_r, h_r, E5M2, (PACK - 1) * P, L)
-
-        dv_banks = [banks[6], banks[7], banks[1], banks[2]]
-        du_banks = [banks[3], banks[4], banks[5], banks[0]]
+        early_banks = [banks[6], banks[7], banks[4]]
+        dv_banks = [banks[5], banks[1], banks[2], banks[1]]
+        du_banks = [banks[0], banks[6], banks[7], banks[4]]
         dv = [f32_tile(f"dv{t}", L) for t in range(PACK)]
         du = [f32_tile(f"du{t}", L) for t in range(PACK)]
-        for t in range(PACK):
-            product(dv_banks[t][:], xq_r, E4M3, t * P, hq_r, E5M2, 0, L)
-        for t in range(PACK):
-            nc.scalar.copy(dv[t][:], dv_banks[t][:])
-
-        h_i = bf16_tile("h_i")
-        hq_i = mx_tiles("hq_i")
-        h_words = h_r[:].bitcast(F32)
-        for u in range(2):
-            turned = turn(None, h_words, lambda s: 2 * s + u, 8, banks[6 + u])
-            nc.scalar.copy(h_i[:].rearrange("q (p u e s) -> q u p e s", u=2, e=2, s=PACK)[:, u],
-                           turned.rearrange("q (s p e) -> q p e s", s=PACK, e=2))
-
         out_0_rows = out_0.rearrange("(p t) c -> p t c", t=PACK)
         out_1_rows = out_1.rearrange("(p t) c -> p t c", t=PACK)
+
+        first_halves = [dv[0][:, 0:half], dv[1][:, 0:half], chunk(num, 2)[:, 0:half]]
+
+        def place_half(t, k):
+            nc.vector.tensor_copy(cell_windows[t][:].indirect(cell_list[:, k * 16:(k + 1) * 16]),
+                                  dv[t][:, half:L] if k else first_halves[t])
 
         def place(windows, offsets, values, rows, t):
             window = windows[t % len(windows)]
             nc.vector.tensor_copy(window[:].indirect(offsets[:]), values[t][:])
             nc.sync.dma_start(rows[:, t, :], window[:])
 
-        place(cell_windows, cell_list, dv, out_0_rows, 0)
-        place(cell_windows, cell_list, dv, out_0_rows, 1)
+        scaled(0)
+        scaled(1)
+        residual(0)
+        square(0)
+        root(0)
+        scaled(2)
+        residual(1)
+        square(1)
+        unroot(0)
+        root(1)
+        scaled(3)
+        residual(2)
+        square(2)
+        unroot(1)
+        numerator(0)
+        residual(3)
+        numerator(1)
+        weight(0)
+        weight(1)
+        numerator(2)
+        quantize(hq_r, h_r, E5M2, 0, half, half)
+        root(2)
+        square(3)
+        for t in range(3):
+            product(early_banks[t][:], xq_r, E4M3, t * P, hq_r, E5M2, 0, L)
+        unroot(2)
+        root(3)
+        nc.scalar.copy(dv[0][:, 0:half], early_banks[0][:, half:L])
+        unroot(3)
+        nc.scalar.copy(first_halves[1], early_banks[1][:, half:L])
+        numerator(3)
+        weight(2)
+        nc.scalar.copy(first_halves[2], early_banks[2][:, half:L])
+        weight(3)
+        quantize(hq_r, h_r, E5M2, half, 3 * P, half)
+        quantize(hq_r, h_r, E5M2, 3 * P, L, half)
+        for t in range(3):
+            product(dv_banks[t][:], xq_r, E4M3, t * P, hq_r, E5M2, half, half + L)
+        for t in range(3):
+            nc.scalar.copy(dv[t][:, half:L], dv_banks[t][:, half:L])
+        for t in range(3):
+            place_half(t, 0)
+
+        h_i = bf16_tile("h_i")
+        hq_i = mx_tiles("hq_i")
+        h_words = h_r[:].bitcast(F32)
+        for u in range(2):
+            turned = turn(None, h_words, lambda s: 2 * s + u, 8, dv_banks[u])
+            nc.scalar.copy(h_i[:].rearrange("q (p u e s) -> q u p e s", u=2, e=2, s=PACK)[:, u],
+                           turned.rearrange("q (s p e) -> q p e s", s=PACK, e=2))
         quantize(hq_i, h_i, E5M2)
+        product(dv_banks[3][:], xq_r, E4M3, 3 * P, hq_r, E5M2, half, half + L)
+        nc.scalar.copy(dv[3][:], dv_banks[3][:])
+        turn_w(1, dv_banks[2])
+        quantize(wq_i, w_i, E4M3, half, L)
         for t in range(PACK):
             product(du_banks[t][:], wq_i, E4M3, t * P, hq_i, E5M2, 0, L)
         for t in range(PACK):
             nc.scalar.copy(du[t][:], du_banks[t][:])
-        place(cell_windows, cell_list, dv, out_0_rows, 2)
-        place(gene_windows, gene_list, du, out_1_rows, 0)
-        place(gene_windows, gene_list, du, out_1_rows, 1)
+
+        for t in range(3):
+            place_half(t, 1)
+            nc.sync.dma_start(out_0_rows[:, t, :], cell_windows[t][:])
         place(cell_windows, cell_list, dv, out_0_rows, 3)
-        place(gene_windows, gene_list, du, out_1_rows, 2)
-        place(gene_windows, gene_list, du, out_1_rows, 3)
+        for t in range(PACK):
+            place(gene_windows, gene_list, du, out_1_rows, t)

@@ -40,8 +40,8 @@ def tile_attend_gmf_cau_vu_kernel(tc, uT, vT, y, us, ts, offs, uoffs, out_0, out
         def bf16_tile(name):
             return sb.tile([P, L * PACK], BF16, name=name, align_bytes=64)
 
-        def mx_tiles(name, width=L):
-            return (sb.tile([P, width], U32, name=name + "_codes", tag=name + "_codes", align_bytes=64),
+        def mx_tiles(name, width=L, tag=None):
+            return (sb.tile([P, width], U32, name=name + "_codes", tag=tag or name + "_codes", align_bytes=64),
                     sb.tile([P, width], U8, name=name + "_scales", align_bytes=64))
 
         def quantize(dst, src, fmt, c0=0, c1=L, shift=0):
@@ -76,10 +76,10 @@ def tile_attend_gmf_cau_vu_kernel(tc, uT, vT, y, us, ts, offs, uoffs, out_0, out
             nc.sync.dma_start(v_planes[t][:], vT_rows[:, t, :])
         nc.sync.dma_start(y_rows[:], y.rearrange("b (p s) i -> p (b s i)", s=PACK))
 
-        cell_windows = [f32_tile(f"cell_window{k}", T) for k in range(4)]
-        gene_windows = [f32_tile("gene_window0", T)]
+        cell_windows = [f32_tile(f"cell_window{k}", T) for k in range(3)]
+        gene_windows = [f32_tile(f"gene_window{k}", T) for k in range(2)]
         for window in cell_windows + gene_windows:
-            nc.gpsimd.memset(window[:], 0.0)
+            nc.vector.memset(window[:].bitcast(I32), 0)
 
         warm = f32_tile("warm", 8)
         nc.scalar.activation(warm[:, 0:1], ident[:, 0:1], ACT.Abs_reciprocal_sqrt, bias=1.0)
@@ -102,11 +102,13 @@ def tile_attend_gmf_cau_vu_kernel(tc, uT, vT, y, us, ts, offs, uoffs, out_0, out
                 nc.scalar.copy(x_r[:, u * 1024:(u + 1) * 1024].rearrange("q (e p s) -> q e p s", e=2, s=PACK),
                                turned.rearrange("q (s p e) -> q e p s", s=PACK, e=2))
         xq_d = mx_tiles("xq_d")
-        xq_r = mx_tiles("xq_r")
 
         ts_listed = f32_tile("ts_listed", L)
         ts_column = f32_tile("ts_column", PACK)
         sc = f32_tile("sc", PACK * L)
+        q = f32_tile("q", PACK * L)
+        num = f32_tile("num", PACK * L)
+        inv = f32_tile("inv", PACK * L)
         nc.vector.tensor_copy(ts_listed[:], ts_table[:].indirect(cell_list[:]))
         for b in range(PACK):
             nc.tensor.transpose(banks[6][:, b * P:(b + 1) * P], ts_listed[:, b * P:(b + 1) * P], ident[:])
@@ -114,14 +116,13 @@ def tile_attend_gmf_cau_vu_kernel(tc, uT, vT, y, us, ts, offs, uoffs, out_0, out
         for b in range(PACK):
             nc.tensor.transpose(banks[7][:, b * P:(b + 1) * P], ts_column[:, b:b + 1].to_broadcast([P, P]), ident[:])
         for s in range(PACK):
-            nc.scalar.activation(sc[:].rearrange("p (b s j) -> p s b j", b=PACK, s=PACK)[:, s],
-                                 banks[7][:].rearrange("p (b j) -> p b j", b=PACK), ACT.Copy, scale=us_rows[:, s:s + 1])
+            nc.scalar.activation(inv[:, s * L:(s + 1) * L], banks[7][:], ACT.Copy, scale=us_rows[:, s:s + 1])
+        nc.scalar.copy(sc[:].rearrange("p (i s) -> p i s", s=PACK), inv[:].rearrange("p (s i) -> p i s", s=PACK))
 
         w_d = bf16_tile("w_d")
         w_i = bf16_tile("w_i")
         w_words = w_d[:].bitcast(F32)
         wq_d = mx_tiles("wq_d")
-        wq_i = mx_tiles("wq_i")
 
         def turn_w(u, bank):
             turned = turn(None, w_words, lambda s: 2 * s + u, 8, bank)
@@ -143,38 +144,34 @@ def tile_attend_gmf_cau_vu_kernel(tc, uT, vT, y, us, ts, offs, uoffs, out_0, out
             for s in range(PACK):
                 product(banks[b][:, s * P:(s + 1) * P], xq_d, E4M3, s * P, wq_d, E4M3, b * P, (b + 1) * P)
 
+        xq_r = mx_tiles("xq_r", tag="v_plane3")
         quantize(xq_r, x_r, E4M3)
-        quantize(wq_i, w_i, E4M3, 0, half)
 
-        gene_windows += [f32_tile("gene_window1", T, "xq_d_codes"), f32_tile("gene_window2", T, "wq_d_codes")]
-        for window in gene_windows[1:]:
-            nc.gpsimd.memset(window[:], 0.0)
-
-        q = f32_tile("q", PACK * L)
-        num = f32_tile("num", PACK * L)
-        inv = f32_tile("inv", PACK * L)
         h_r = bf16_tile("h_r")
         hq_r = mx_tiles("hq_r", half + L)
         nc.gpsimd.memset(hq_r[0][:, 0:half], 0)
         nc.gpsimd.memset(hq_r[1][:, 0:half], 0)
-        y_chunks = y_rows[:].rearrange("p (s b j) -> p b s j", s=PACK, b=PACK)
+        y_chunks = y_rows[:].rearrange("p (s b j) -> p b j s", s=PACK, b=PACK)
 
         def chunk(tile_, b):
             return tile_[:, b * L:(b + 1) * L]
 
+        for b in range(PACK):
+            nc.scalar.copy(chunk(q, b).rearrange("p (j s) -> p j s", s=PACK), y_chunks[:, b])
+
         def scaled(b):
-            nc.vector.tensor_tensor(chunk(q, b), banks[b][:], chunk(sc, b), MULT)
+            nc.vector.tensor_tensor(chunk(num, b).rearrange("p (j s) -> p j s", s=PACK),
+                                    banks[b][:].rearrange("p (s j) -> p j s", s=PACK),
+                                    chunk(sc, b).rearrange("p (j s) -> p j s", s=PACK), MULT)
 
         def residual(b):
-            view = chunk(q, b).rearrange("p (s j) -> p s j", s=PACK)
-            nc.vector.tensor_tensor(view, view, y_chunks[:, b], SUB)
+            nc.vector.tensor_tensor(chunk(q, b), chunk(num, b), chunk(q, b), SUB)
 
         def numerator(b):
             nc.vector.tensor_tensor(chunk(num, b), chunk(q, b), chunk(sc, b), MULT)
 
         def square(b):
-            nc.scalar.activation(chunk(inv, b).rearrange("p (j s) -> p j s", s=PACK),
-                                 chunk(q, b).rearrange("p (s j) -> p j s", s=PACK), ACT.Square)
+            nc.scalar.activation(chunk(inv, b), chunk(q, b), ACT.Square)
 
         def root(b):
             nc.scalar.activation(chunk(inv, b), chunk(inv, b), ACT.Abs_reciprocal_sqrt, bias=1.0)
@@ -183,19 +180,18 @@ def tile_attend_gmf_cau_vu_kernel(tc, uT, vT, y, us, ts, offs, uoffs, out_0, out
             nc.scalar.activation(chunk(inv, b), chunk(inv, b), ACT.Square)
 
         def weight(b):
-            nc.vector.tensor_tensor(chunk(h_r, b).rearrange("p (j s) -> p j s", s=PACK),
-                                    chunk(num, b).rearrange("p (s j) -> p j s", s=PACK),
-                                    chunk(inv, b).rearrange("p (j s) -> p j s", s=PACK), MULT)
+            nc.vector.tensor_tensor(chunk(h_r, b), chunk(num, b), chunk(inv, b), MULT)
 
         early_banks = [banks[6], banks[7], banks[4]]
-        dv_banks = [banks[5], banks[1], banks[2], banks[1]]
-        du_banks = [banks[0], banks[6], banks[7], banks[4]]
+        dv_banks = [banks[1], banks[2], banks[3], banks[5]]
+        du_banks = [banks[6], banks[5], banks[7], banks[4]]
+        h_banks = [banks[5], banks[0]]
         dv = [f32_tile(f"dv{t}", L) for t in range(PACK)]
         du = [f32_tile(f"du{t}", L) for t in range(PACK)]
         out_0_rows = out_0.rearrange("(p t) c -> p t c", t=PACK)
         out_1_rows = out_1.rearrange("(p t) c -> p t c", t=PACK)
 
-        first_halves = [dv[0][:, 0:half], dv[1][:, 0:half], chunk(num, 2)[:, 0:half]]
+        first_halves = [dv[0][:, 0:half], chunk(num, 3)[:, 0:half], chunk(num, 3)[:, half:L]]
 
         def place_half(t, k):
             nc.vector.tensor_copy(cell_windows[t][:].indirect(cell_list[:, k * 16:(k + 1) * 16]),
@@ -235,40 +231,43 @@ def tile_attend_gmf_cau_vu_kernel(tc, uT, vT, y, us, ts, offs, uoffs, out_0, out
         root(3)
         nc.scalar.copy(dv[0][:, 0:half], early_banks[0][:, half:L])
         unroot(3)
-        nc.scalar.copy(first_halves[1], early_banks[1][:, half:L])
         numerator(3)
+        place_half(0, 0)
         weight(2)
-        nc.scalar.copy(first_halves[2], early_banks[2][:, half:L])
         weight(3)
         quantize(hq_r, h_r, E5M2, half, 3 * P, half)
         quantize(hq_r, h_r, E5M2, 3 * P, L, half)
-        for t in range(3):
-            product(dv_banks[t][:], xq_r, E4M3, t * P, hq_r, E5M2, half, half + L)
-        for t in range(3):
-            nc.scalar.copy(dv[t][:, half:L], dv_banks[t][:, half:L])
-        for t in range(3):
+        wq_i = [mx_tiles("wq_i0", half, tag="inv"), mx_tiles("wq_i1", half)]
+        quantize(wq_i[0], w_i, E4M3, 0, half)
+        for t in range(1, 3):
+            nc.scalar.copy(first_halves[t], early_banks[t][:, half:L])
             place_half(t, 0)
 
         h_i = bf16_tile("h_i")
         hq_i = mx_tiles("hq_i")
         h_words = h_r[:].bitcast(F32)
         for u in range(2):
-            turned = turn(None, h_words, lambda s: 2 * s + u, 8, dv_banks[u])
+            turned = turn(None, h_words, lambda s: 2 * s + u, 8, h_banks[u])
             nc.scalar.copy(h_i[:].rearrange("q (p u e s) -> q u p e s", u=2, e=2, s=PACK)[:, u],
                            turned.rearrange("q (s p e) -> q p e s", s=PACK, e=2))
         quantize(hq_i, h_i, E5M2)
-        product(dv_banks[3][:], xq_r, E4M3, 3 * P, hq_r, E5M2, half, half + L)
-        nc.scalar.copy(dv[3][:], dv_banks[3][:])
-        turn_w(1, dv_banks[2])
-        quantize(wq_i, w_i, E4M3, half, L)
-        for t in range(PACK):
-            product(du_banks[t][:], wq_i, E4M3, t * P, hq_i, E5M2, 0, L)
-        for t in range(PACK):
-            nc.scalar.copy(du[t][:], du_banks[t][:])
-
         for t in range(3):
+            product(dv_banks[t][:], xq_r, E4M3, t * P, hq_r, E5M2, half, half + L)
+            nc.scalar.copy(dv[t][:, half:L], dv_banks[t][:, half:L])
             place_half(t, 1)
             nc.sync.dma_start(out_0_rows[:, t, :], cell_windows[t][:])
-        place(cell_windows, cell_list, dv, out_0_rows, 3)
-        for t in range(PACK):
+
+        def gene_block(t):
+            product(du_banks[t][:], wq_i[t // 2], E4M3, (t % 2) * P, hq_i, E5M2, 0, L)
+            nc.scalar.copy(du[t][:], du_banks[t][:])
             place(gene_windows, gene_list, du, out_1_rows, t)
+
+        gene_block(0)
+        gene_block(1)
+        product(dv_banks[3][:], xq_r, E4M3, 3 * P, hq_r, E5M2, half, half + L)
+        nc.scalar.copy(dv[3][:], dv_banks[3][:])
+        place(cell_windows, cell_list, dv, out_0_rows, 3)
+        turn_w(1, dv_banks[2])
+        quantize(wq_i[1], w_i, E4M3, half, L, -half)
+        gene_block(2)
+        gene_block(3)

@@ -13,7 +13,6 @@ E4M3 = mybir.dt.float8_e4m3fn_x4
 E5M2 = mybir.dt.float8_e5m2_x4
 ACT = mybir.ActivationFunctionType
 MULT = mybir.AluOpType.mult
-SUB = mybir.AluOpType.subtract
 
 P = 128
 PACK = 4
@@ -68,7 +67,7 @@ def tile_attend_gmf_cau_vu_kernel(tc, uT, vT, y, us, ts, offs, uoffs, out_0, out
         nc.sync.dma_start(gene_list[:], uoffs)
         nc.sync.dma_start(cell_list[:], offs)
         nc.sync.dma_start(u_planes[1][:], uT_rows[:, 1, :])
-        nc.sync.dma_start(ts_table[0:1, :], ts[0:1, :])
+        nc.scalar.dma_start(ts_table[0:1, :], ts[0:1, :])
         nc.sync.dma_start(us_rows[:], us.rearrange("b (p s) o -> p (b s o)", s=PACK))
         for t in range(2, PACK):
             nc.sync.dma_start(u_planes[t][:], uT_rows[:, t, :])
@@ -76,198 +75,161 @@ def tile_attend_gmf_cau_vu_kernel(tc, uT, vT, y, us, ts, offs, uoffs, out_0, out
             nc.sync.dma_start(v_planes[t][:], vT_rows[:, t, :])
         nc.sync.dma_start(y_rows[:], y.rearrange("b (p s) i -> p (b s i)", s=PACK))
 
-        cell_windows = [f32_tile(f"cell_window{k}", T) for k in range(3)]
-        gene_windows = [f32_tile(f"gene_window{k}", T) for k in range(2)]
-        for window in cell_windows + gene_windows:
-            nc.vector.memset(window[:].bitcast(I32), 0)
-
         warm = f32_tile("warm", 8)
         nc.scalar.activation(warm[:, 0:1], ident[:, 0:1], ACT.Abs_reciprocal_sqrt, bias=1.0)
 
-        def turn(dst, src_words, first, step, bank):
+        def block(tile_, b, width=L):
+            return tile_[:, b * width:(b + 1) * width]
+
+        def turn(src_words, u, bank, dealt=False):
             for s in range(PACK):
-                a = first(s)
-                nc.tensor.transpose(bank[:, s * P:(s + 1) * P], src_words[:, a:a + step * (P - 1) + 1:step], ident[:])
+                a, step = (2 * P * s + u, 2) if dealt else (2 * s + u, 8)
+                nc.tensor.transpose(block(bank, s, P), src_words[:, a:a + step * (P - 1) + 1:step], ident[:])
             return bank[:].bitcast(BF16)
+
+        def turn_table(dst, src, u, bank, dealt=False):
+            turned = turn(src[:].bitcast(F32), u, bank, dealt)
+            nc.scalar.copy(block(dst, u, 1024).rearrange("q (e p s) -> q e p s", e=2, s=PACK),
+                           turned.rearrange("q (s p e) -> q e p s", s=PACK, e=2))
+
+        ts_listed = f32_tile("ts_listed", L)
+        neg_ts = f32_tile("neg_ts", PACK)
+        us_all = f32_tile("us_all", L)
+        neg_sc = f32_tile("neg_sc", PACK * L)
+        nc.vector.tensor_copy(ts_listed[:], ts_table[:].indirect(cell_list[:]))
+        for s in range(PACK):
+            nc.tensor.transpose(block(banks[0], s, P), us_rows[:, s:s + 1].to_broadcast([P, P]), ident[:])
+        nc.scalar.copy(us_all[:].rearrange("q (p s) -> q p s", s=PACK), banks[0][:].rearrange("q (s p) -> q p s", s=PACK))
+        for b in range(PACK):
+            nc.tensor.transpose(block(banks[6], b, P), block(ts_listed, b, P), ident[:])
+        nc.scalar.activation(neg_ts[:], banks[6][:, 0:L:P], ACT.Copy, scale=-1.0)
+        for b in range(PACK):
+            nc.tensor.transpose(block(banks[7], b, P), neg_ts[:, b:b + 1].to_broadcast([P, P]), ident[:])
+        for m in range(PACK):
+            nc.scalar.activation(neg_sc[:].rearrange("p (b m j) -> p b m j", b=PACK, m=PACK)[:, :, m, :],
+                                 banks[7][:].rearrange("p (b j) -> p b j", b=PACK), ACT.Copy, scale=us_rows[:, m:m + 1])
 
         x_d = bf16_tile("x_d")
         x_r = bf16_tile("x_r")
-        x_words = x_d[:].bitcast(F32)
         for t in range(PACK):
-            nc.vector.tensor_copy(x_d[:].rearrange("p (s m t) -> p m s t", s=PACK, t=PACK)[:, :, :, t],
-                                  u_planes[t][:].indirect(gene_list[:]))
+            nc.vector.tensor_copy(x_d[:].rearrange("p (s m t) -> p m s t", s=PACK, t=PACK)[:, :, :, t], u_planes[t][:].indirect(gene_list[:]))
             if t % 2 == 1:
-                u = t // 2
-                turned = turn(None, x_words, lambda s: 2 * P * s + u, 2, banks[4 + u])
-                nc.scalar.copy(x_r[:, u * 1024:(u + 1) * 1024].rearrange("q (e p s) -> q e p s", e=2, s=PACK),
-                               turned.rearrange("q (s p e) -> q e p s", s=PACK, e=2))
-        xq_d = mx_tiles("xq_d")
-
-        ts_listed = f32_tile("ts_listed", L)
-        ts_column = f32_tile("ts_column", PACK)
-        sc = f32_tile("sc", PACK * L)
-        q = f32_tile("q", PACK * L)
-        num = f32_tile("num", PACK * L)
-        inv = f32_tile("inv", PACK * L)
-        nc.vector.tensor_copy(ts_listed[:], ts_table[:].indirect(cell_list[:]))
-        for b in range(PACK):
-            nc.tensor.transpose(banks[6][:, b * P:(b + 1) * P], ts_listed[:, b * P:(b + 1) * P], ident[:])
-        nc.scalar.copy(ts_column[:], banks[6][:, 0:L:P])
-        for b in range(PACK):
-            nc.tensor.transpose(banks[7][:, b * P:(b + 1) * P], ts_column[:, b:b + 1].to_broadcast([P, P]), ident[:])
-        for s in range(PACK):
-            nc.scalar.activation(inv[:, s * L:(s + 1) * L], banks[7][:], ACT.Copy, scale=us_rows[:, s:s + 1])
-        nc.scalar.copy(sc[:].rearrange("p (i s) -> p i s", s=PACK), inv[:].rearrange("p (s i) -> p i s", s=PACK))
+                turn_table(x_r, x_d, t // 2, banks[4 + t // 2], dealt=True)
 
         w_d = bf16_tile("w_d")
         w_i = bf16_tile("w_i")
-        w_words = w_d[:].bitcast(F32)
+        xq_d = mx_tiles("xq_d")
+        late_codes = sb.tile([P, L + L // 2], U32, name="late_codes", tag="v_plane3", align_bytes=64)
+        late_scales = sb.tile([P, L + L // 2], U8, name="late_scales", align_bytes=64)
+        xq_r = (late_codes[:, 0:L], late_scales[:, 0:L])
         wq_d = mx_tiles("wq_d")
-
-        def turn_w(u, bank):
-            turned = turn(None, w_words, lambda s: 2 * s + u, 8, bank)
-            nc.scalar.copy(w_i[:, u * 1024:(u + 1) * 1024].rearrange("q (e p s) -> q e p s", e=2, s=PACK),
-                           turned.rearrange("q (s p e) -> q e p s", s=PACK, e=2))
-
+        wq_i = [(late_codes[:, L:], late_scales[:, L:]), mx_tiles("wq_i1", L // 2)]
         half = L // 2
-        for t in range(PACK - 1):
+        for t in range(2):
             nc.vector.tensor_copy(w_d[:, t:L * PACK:PACK], v_planes[t][:].indirect(cell_list[:]))
-            if t == 1:
-                turn_w(0, banks[4])
-
+        turn_table(w_i, w_d, 0, banks[4])
         quantize(xq_d, x_d, E4M3)
+        nc.vector.tensor_copy(w_d[:, 2:L * PACK:PACK], v_planes[2][:].indirect(cell_list[:]))
         for k in range(2):
             nc.vector.tensor_copy(w_d[:, k * 1024 + 3:(k + 1) * 1024:PACK],
                                   v_planes[3][:].indirect(cell_list[:, k * 16:(k + 1) * 16]))
             quantize(wq_d, w_d, E4M3, k * half, (k + 1) * half)
         for b in range(PACK):
-            for s in range(PACK):
-                product(banks[b][:, s * P:(s + 1) * P], xq_d, E4M3, s * P, wq_d, E4M3, b * P, (b + 1) * P)
-
-        xq_r = mx_tiles("xq_r", tag="v_plane3")
+            for m in range(PACK):
+                product(block(banks[b], m, P), xq_d, E4M3, m * P, wq_d, E4M3, b * P, (b + 1) * P)
         quantize(xq_r, x_r, E4M3)
+        quantize(wq_i[0], w_i, E4M3, 0, half)
 
+        cell_windows = [f32_tile(f"cell_window{k}", T) for k in range(3)]
+        for window in cell_windows:
+            nc.vector.memset(window[:].bitcast(I32), 0)
+
+        neg_a = f32_tile("neg_a", PACK * L)
+        num = f32_tile("num", PACK * L)
+        inv = f32_tile("inv", PACK * L)
+        last_root = f32_tile("last_root", L)
+        h_cells = bf16_tile("h_cells")
         h_r = bf16_tile("h_r")
         hq_r = mx_tiles("hq_r", half + L)
         nc.gpsimd.memset(hq_r[0][:, 0:half], 0)
         nc.gpsimd.memset(hq_r[1][:, 0:half], 0)
-        y_chunks = y_rows[:].rearrange("p (s b j) -> p b j s", s=PACK, b=PACK)
-
-        def chunk(tile_, b):
-            return tile_[:, b * L:(b + 1) * L]
+        q_banks = banks[4:8]
 
         for b in range(PACK):
-            nc.scalar.copy(chunk(q, b).rearrange("p (j s) -> p j s", s=PACK), y_chunks[:, b])
+            nc.vector.tensor_tensor(block(neg_a, b), banks[b][:], block(neg_sc, b), MULT)
+            for m in range(PACK):
+                nc.tensor.matmul(block(q_banks[b], m, P), y_rows[:, m * L + b * P:m * L + (b + 1) * P], ident[:],
+                                 start=(m == 0), stop=False, is_transpose=True)
+            for m in range(PACK):
+                nc.tensor.matmul(block(q_banks[b], m, P), neg_a[:, b * L + m * P:b * L + (m + 1) * P], ident[:],
+                                 start=False, stop=(m == PACK - 1), is_transpose=True)
 
-        def scaled(b):
-            nc.vector.tensor_tensor(chunk(num, b).rearrange("p (j s) -> p j s", s=PACK),
-                                    banks[b][:].rearrange("p (s j) -> p j s", s=PACK),
-                                    chunk(sc, b).rearrange("p (j s) -> p j s", s=PACK), MULT)
+        gene_windows = [f32_tile("gene_window0", T, tag="neg_sc"), f32_tile("gene_window1", T, tag="neg_a")]
 
-        def residual(b):
-            nc.vector.tensor_tensor(chunk(q, b), chunk(num, b), chunk(q, b), SUB)
+        def weigh(b):
+            root = last_root[:] if b == PACK - 1 else block(inv, b)
+            neg_q = q_banks[b][:].rearrange("j (s p) -> j p s", s=PACK)
+            nc.scalar.activation(block(inv, b).rearrange("j (p s) -> j p s", s=PACK), neg_q, ACT.Square)
+            nc.vector.scalar_tensor_tensor(block(num, b).rearrange("j (p s) -> j p s", s=PACK), neg_q, neg_ts[:, b:b + 1],
+                                           us_all[:].rearrange("j (p s) -> j p s", s=PACK), MULT, MULT)
+            nc.scalar.activation(root, block(inv, b), ACT.Abs_reciprocal_sqrt, bias=1.0)
+            nc.scalar.activation(block(inv, b), root, ACT.Square)
+            nc.vector.tensor_tensor(block(h_cells, b), block(num, b), block(inv, b), MULT)
+            words = block(h_cells[:].bitcast(F32), b, half)
+            bank = banks[b % 2]
+            for u in range(2):
+                nc.tensor.transpose(block(bank, u, P), words[:, u:half:2], ident[:])
+            nc.scalar.copy(block(h_r[:].bitcast(F32), b, half).rearrange("q (j u) -> q j u", u=2),
+                           bank[:, 0:half].rearrange("q (u j) -> q j u", u=2))
 
-        def numerator(b):
-            nc.vector.tensor_tensor(chunk(num, b), chunk(q, b), chunk(sc, b), MULT)
-
-        def square(b):
-            nc.scalar.activation(chunk(inv, b), chunk(q, b), ACT.Square)
-
-        def root(b):
-            nc.scalar.activation(chunk(inv, b), chunk(inv, b), ACT.Abs_reciprocal_sqrt, bias=1.0)
-
-        def unroot(b):
-            nc.scalar.activation(chunk(inv, b), chunk(inv, b), ACT.Square)
-
-        def weight(b):
-            nc.vector.tensor_tensor(chunk(h_r, b), chunk(num, b), chunk(inv, b), MULT)
-
-        early_banks = [banks[6], banks[7], banks[4]]
-        dv_banks = [banks[1], banks[2], banks[3], banks[5]]
-        du_banks = [banks[6], banks[5], banks[7], banks[4]]
-        h_banks = [banks[5], banks[0]]
-        dv = [f32_tile(f"dv{t}", L) for t in range(PACK)]
+        dv = [f32_tile(f"dv{t}", L) for t in range(3)]
         du = [f32_tile(f"du{t}", L) for t in range(PACK)]
         out_0_rows = out_0.rearrange("(p t) c -> p t c", t=PACK)
         out_1_rows = out_1.rearrange("(p t) c -> p t c", t=PACK)
 
-        first_halves = [dv[0][:, 0:half], chunk(num, 3)[:, 0:half], chunk(num, 3)[:, half:L]]
+        def cell_half(t, k, bank, stage):
+            product(bank[:], xq_r, E4M3, t * P, hq_r, E5M2, k * half, k * half + L)
+            nc.scalar.copy(stage, bank[:, half:L])
+            nc.vector.tensor_copy(cell_windows[t][:].indirect(cell_list[:, k * 16:(k + 1) * 16]), stage)
 
-        def place_half(t, k):
-            nc.vector.tensor_copy(cell_windows[t][:].indirect(cell_list[:, k * 16:(k + 1) * 16]),
-                                  dv[t][:, half:L] if k else first_halves[t])
+        def place(window, offsets, bank, stage, rows):
+            nc.scalar.copy(stage, bank[:])
+            nc.vector.tensor_copy(window[:].indirect(offsets[:]), stage)
+            nc.sync.dma_start(rows, window[:])
 
-        def place(windows, offsets, values, rows, t):
-            window = windows[t % len(windows)]
-            nc.vector.tensor_copy(window[:].indirect(offsets[:]), values[t][:])
-            nc.sync.dma_start(rows[:, t, :], window[:])
+        def gene_block(t, bank):
+            product(bank[:], wq_i[t // 2], E4M3, (t % 2) * P, hq_i, E5M2, 0, L)
+            place(gene_windows[t % 2], gene_list, bank, du[t][:], out_1_rows[:, t, :])
 
-        scaled(0)
-        scaled(1)
-        residual(0)
-        square(0)
-        root(0)
-        scaled(2)
-        residual(1)
-        square(1)
-        unroot(0)
-        root(1)
-        scaled(3)
-        residual(2)
-        square(2)
-        unroot(1)
-        numerator(0)
-        residual(3)
-        numerator(1)
-        weight(0)
-        weight(1)
-        numerator(2)
+        weigh(0)
+        weigh(1)
+        for window in gene_windows:
+            nc.vector.memset(window[:].bitcast(I32), 0)
         quantize(hq_r, h_r, E5M2, 0, half, half)
-        root(2)
-        square(3)
-        for t in range(3):
-            product(early_banks[t][:], xq_r, E4M3, t * P, hq_r, E5M2, 0, L)
-        unroot(2)
-        root(3)
-        nc.scalar.copy(dv[0][:, 0:half], early_banks[0][:, half:L])
-        unroot(3)
-        numerator(3)
-        place_half(0, 0)
-        weight(2)
-        weight(3)
-        quantize(hq_r, h_r, E5M2, half, 3 * P, half)
-        quantize(hq_r, h_r, E5M2, 3 * P, L, half)
-        wq_i = [mx_tiles("wq_i0", half, tag="inv"), mx_tiles("wq_i1", half)]
-        quantize(wq_i[0], w_i, E4M3, 0, half)
-        for t in range(1, 3):
-            nc.scalar.copy(first_halves[t], early_banks[t][:, half:L])
-            place_half(t, 0)
+        cell_half(0, 0, banks[2], dv[0][:, 0:half])
+        weigh(2)
+        weigh(3)
+        cell_half(1, 0, banks[3], last_root[:, 0:half])
+        quantize(hq_r, h_r, E5M2, half, L, half)
+        cell_half(2, 0, banks[1], dv[2][:, 0:half])
 
         h_i = bf16_tile("h_i")
         hq_i = mx_tiles("hq_i")
-        h_words = h_r[:].bitcast(F32)
+        for t in range(2):
+            cell_half(t, 1, banks[2 + t], dv[t][:, half:L])
+            nc.sync.dma_start(out_0_rows[:, t, :], cell_windows[t][:])
         for u in range(2):
-            turned = turn(None, h_words, lambda s: 2 * s + u, 8, h_banks[u])
+            turned = turn(h_r[:].bitcast(F32), u, banks[4 + u])
             nc.scalar.copy(h_i[:].rearrange("q (p u e s) -> q u p e s", u=2, e=2, s=PACK)[:, u],
                            turned.rearrange("q (s p e) -> q p e s", s=PACK, e=2))
         quantize(hq_i, h_i, E5M2)
-        for t in range(3):
-            product(dv_banks[t][:], xq_r, E4M3, t * P, hq_r, E5M2, half, half + L)
-            nc.scalar.copy(dv[t][:, half:L], dv_banks[t][:, half:L])
-            place_half(t, 1)
-            nc.sync.dma_start(out_0_rows[:, t, :], cell_windows[t][:])
-
-        def gene_block(t):
-            product(du_banks[t][:], wq_i[t // 2], E4M3, (t % 2) * P, hq_i, E5M2, 0, L)
-            nc.scalar.copy(du[t][:], du_banks[t][:])
-            place(gene_windows, gene_list, du, out_1_rows, t)
-
-        gene_block(0)
-        gene_block(1)
-        product(dv_banks[3][:], xq_r, E4M3, 3 * P, hq_r, E5M2, half, half + L)
-        nc.scalar.copy(dv[3][:], dv_banks[3][:])
-        place(cell_windows, cell_list, dv, out_0_rows, 3)
-        turn_w(1, dv_banks[2])
+        cell_half(2, 1, banks[5], dv[2][:, half:L])
+        nc.sync.dma_start(out_0_rows[:, 2, :], cell_windows[2][:])
+        gene_block(0, banks[6])
+        gene_block(1, banks[7])
+        product(banks[0][:], xq_r, E4M3, 3 * P, hq_r, E5M2, half, half + L)
+        place(cell_windows[0], cell_list, banks[0], du[0][:], out_0_rows[:, 3, :])
+        turn_table(w_i, w_d, 1, banks[4])
         quantize(wq_i[1], w_i, E4M3, half, L, -half)
-        gene_block(2)
-        gene_block(3)
+        gene_block(2, banks[2])
+        gene_block(3, banks[3])

@@ -13,11 +13,13 @@ E4M3 = mybir.dt.float8_e4m3fn_x4
 E5M2 = mybir.dt.float8_e5m2_x4
 ACT = mybir.ActivationFunctionType
 MULT = mybir.AluOpType.mult
+ADD = mybir.AluOpType.add
 
 P = 128
 PACK = 4
 L = 512
 T = 2048
+NEAR = 2
 FLOPS = 3 * 2 * L * L * L
 BYTES = 4 * (4 * L * T + L * L + L + T) + 2 * 2 * P * 32
 
@@ -60,20 +62,22 @@ def tile_attend_gmf_cau_vu_kernel(tc, uT, vT, y, us, ts, offs, uoffs, out_0, out
         u_planes = [f32_tile(f"u_plane{t}", T) for t in range(PACK)]
         v_planes = [f32_tile(f"v_plane{t}", T) for t in range(PACK)]
         us_rows = f32_tile("us_rows", PACK)
-        y_rows = f32_tile("y_rows", PACK * L)
+        y_halves = [f32_tile(f"y_half{k}", 2 * L) for k in range(2)]
         uT_rows = uT.rearrange("(p t) c -> p t c", t=PACK)
         vT_rows = vT.rearrange("(p t) c -> p t c", t=PACK)
         nc.sync.dma_start(u_planes[0][:], uT_rows[:, 0, :])
         nc.sync.dma_start(gene_list[:], uoffs)
         nc.sync.dma_start(cell_list[:], offs)
+        nc.sync.dma_start(us_rows[:], us.rearrange("b (p s) o -> p (b s o)", s=PACK))
         nc.sync.dma_start(u_planes[1][:], uT_rows[:, 1, :])
         nc.scalar.dma_start(ts_table[0:1, :], ts[0:1, :])
-        nc.sync.dma_start(us_rows[:], us.rearrange("b (p s) o -> p (b s o)", s=PACK))
         for t in range(2, PACK):
             nc.sync.dma_start(u_planes[t][:], uT_rows[:, t, :])
         for t in range(PACK):
             nc.sync.dma_start(v_planes[t][:], vT_rows[:, t, :])
-        nc.sync.dma_start(y_rows[:], y.rearrange("b (p s) i -> p (b s i)", s=PACK))
+        y_rows = y.rearrange("b (p s) i -> p (b s) i", s=PACK)
+        for k in range(2):
+            nc.sync.dma_start(y_halves[k][:].rearrange("p (s i) -> p s i", s=PACK), y_rows[:, :, k * L // 2:(k + 1) * L // 2])
 
         warm = f32_tile("warm", 8)
         nc.scalar.activation(warm[:, 0:1], ident[:, 0:1], ACT.Abs_reciprocal_sqrt, bias=1.0)
@@ -108,22 +112,29 @@ def tile_attend_gmf_cau_vu_kernel(tc, uT, vT, y, us, ts, offs, uoffs, out_0, out
         for m in range(PACK):
             nc.scalar.activation(neg_sc[:].rearrange("p (b m j) -> p b m j", b=PACK, m=PACK)[:, :, m, :],
                                  banks[7][:].rearrange("p (b j) -> p b j", b=PACK), ACT.Copy, scale=us_rows[:, m:m + 1])
+        neg_sc_woven = f32_tile("neg_sc_woven", NEAR * L)
+        for b in range(NEAR):
+            nc.scalar.copy(block(neg_sc_woven, b).rearrange("p (j s) -> p j s", s=PACK), block(neg_sc, b).rearrange("p (s j) -> p j s", s=PACK))
 
+        x_planes = bf16_tile("x_planes")
         x_d = bf16_tile("x_d")
         x_r = bf16_tile("x_r")
         for t in range(PACK):
-            nc.vector.tensor_copy(x_d[:].rearrange("p (s m t) -> p m s t", s=PACK, t=PACK)[:, :, :, t], u_planes[t][:].indirect(gene_list[:]))
+            if t < 2:
+                nc.vector.tensor_copy(block(x_planes, t), u_planes[t][:].indirect(gene_list[:]))
+            else:
+                nc.vector.tensor_copy(x_d[:].rearrange("p (s m t) -> p m s t", s=PACK, t=PACK)[:, :, :, t], u_planes[t][:].indirect(gene_list[:]))
+            if t == 1:
+                nc.scalar.copy(x_d[:].rearrange("p (s m t) -> p s m t", s=PACK, t=PACK)[:, :, :, t - 1:t + 1],
+                               block(x_planes, t // 2, 2 * L).rearrange("p (e m s) -> p s m e", e=2, s=PACK))
             if t % 2 == 1:
                 turn_table(x_r, x_d, t // 2, banks[4 + t // 2], dealt=True)
 
         w_d = bf16_tile("w_d")
         w_i = bf16_tile("w_i")
-        xq_d = mx_tiles("xq_d")
-        late_codes = sb.tile([P, L + L // 2], U32, name="late_codes", tag="v_plane3", align_bytes=64)
-        late_scales = sb.tile([P, L + L // 2], U8, name="late_scales", align_bytes=64)
-        xq_r = (late_codes[:, 0:L], late_scales[:, 0:L])
+        xq_d = mx_tiles("xq_d", tag="v_plane0")
+        xq_r = mx_tiles("xq_r", tag="v_plane3")
         wq_d = mx_tiles("wq_d")
-        wq_i = [(late_codes[:, L:], late_scales[:, L:]), mx_tiles("wq_i1", L // 2)]
         half = L // 2
         for t in range(2):
             nc.vector.tensor_copy(w_d[:, t:L * PACK:PACK], v_planes[t][:].indirect(cell_list[:]))
@@ -137,17 +148,19 @@ def tile_attend_gmf_cau_vu_kernel(tc, uT, vT, y, us, ts, offs, uoffs, out_0, out
         for b in range(PACK):
             for m in range(PACK):
                 product(block(banks[b], m, P), xq_d, E4M3, m * P, wq_d, E4M3, b * P, (b + 1) * P)
+
         quantize(xq_r, x_r, E4M3)
-        quantize(wq_i[0], w_i, E4M3, 0, half)
 
         cell_windows = [f32_tile(f"cell_window{k}", T) for k in range(3)]
-        for window in cell_windows:
+        gene_windows = [f32_tile(f"gene_window{k}", T, tag=f"u_plane{k + 1}") for k in range(2)]
+        for window in cell_windows + gene_windows:
             nc.vector.memset(window[:].bitcast(I32), 0)
 
         neg_a = f32_tile("neg_a", PACK * L)
         num = f32_tile("num", PACK * L)
         inv = f32_tile("inv", PACK * L)
-        last_root = f32_tile("last_root", L)
+        square = f32_tile("square", 2 * L)
+        root = f32_tile("root", 2 * L)
         h_cells = bf16_tile("h_cells")
         h_r = bf16_tile("h_r")
         hq_r = mx_tiles("hq_r", half + L)
@@ -155,34 +168,56 @@ def tile_attend_gmf_cau_vu_kernel(tc, uT, vT, y, us, ts, offs, uoffs, out_0, out
         nc.gpsimd.memset(hq_r[1][:, 0:half], 0)
         q_banks = banks[4:8]
 
-        for b in range(PACK):
+        neg_q = f32_tile("neg_q", NEAR * L)
+
+        def y_chunk(b):
+            return y_halves[b // 2][:].rearrange("p (s b j) -> p b s j", s=PACK, b=2)[:, b % 2]
+
+        def woven(ap):
+            return ap.rearrange("p (j s) -> p j s", s=PACK)
+
+        def scale_near(b):
+            nc.scalar.copy(woven(block(neg_q, b)), y_chunk(b).rearrange("p s j -> p j s"))
+            nc.vector.tensor_tensor(woven(block(neg_a, b)), banks[b][:].rearrange("p (s j) -> p j s", s=PACK),
+                                    woven(block(neg_sc_woven, b)), MULT)
+
+        def residual_near(b):
+            nc.vector.tensor_tensor(block(neg_q, b), block(neg_a, b), block(neg_q, b), ADD)
+
+        def damping(b, first):
+            nc.scalar.activation(woven(block(square, b % 2)), first, ACT.Square)
+            nc.scalar.activation(block(root, b % 2), block(square, b % 2), ACT.Abs_reciprocal_sqrt, bias=1.0)
+            nc.scalar.activation(block(inv, b), block(root, b % 2), ACT.Square)
+
+        def weigh_near(b):
+            damping(b, woven(block(neg_q, b)))
+            nc.vector.tensor_tensor(block(num, b), block(neg_q, b), block(neg_sc_woven, b), MULT)
+            nc.vector.tensor_tensor(block(h_r, b), block(num, b), block(inv, b), MULT)
+
+        def scale_far(b):
             nc.vector.tensor_tensor(block(neg_a, b), banks[b][:], block(neg_sc, b), MULT)
             for m in range(PACK):
-                nc.tensor.matmul(block(q_banks[b], m, P), y_rows[:, m * L + b * P:m * L + (b + 1) * P], ident[:],
+                nc.tensor.matmul(block(q_banks[b], m, P), y_chunk(b)[:, m, :], ident[:],
                                  start=(m == 0), stop=False, is_transpose=True)
             for m in range(PACK):
                 nc.tensor.matmul(block(q_banks[b], m, P), neg_a[:, b * L + m * P:b * L + (m + 1) * P], ident[:],
                                  start=False, stop=(m == PACK - 1), is_transpose=True)
 
-        gene_windows = [f32_tile("gene_window0", T, tag="neg_sc"), f32_tile("gene_window1", T, tag="neg_a")]
-
-        def weigh(b):
-            root = last_root[:] if b == PACK - 1 else block(inv, b)
-            neg_q = q_banks[b][:].rearrange("j (s p) -> j p s", s=PACK)
-            nc.scalar.activation(block(inv, b).rearrange("j (p s) -> j p s", s=PACK), neg_q, ACT.Square)
-            nc.vector.scalar_tensor_tensor(block(num, b).rearrange("j (p s) -> j p s", s=PACK), neg_q, neg_ts[:, b:b + 1],
-                                           us_all[:].rearrange("j (p s) -> j p s", s=PACK), MULT, MULT)
-            nc.scalar.activation(root, block(inv, b), ACT.Abs_reciprocal_sqrt, bias=1.0)
-            nc.scalar.activation(block(inv, b), root, ACT.Square)
+        def weigh_far(b):
+            turned_q = q_banks[b][:].rearrange("j (s p) -> j p s", s=PACK)
+            if b == PACK - 1:
+                damping(b, turned_q)
+            nc.vector.scalar_tensor_tensor(woven(block(num, b)), turned_q, neg_ts[:, b:b + 1], woven(us_all[:]), MULT, MULT)
+            if b < PACK - 1:
+                damping(b, turned_q)
             nc.vector.tensor_tensor(block(h_cells, b), block(num, b), block(inv, b), MULT)
             words = block(h_cells[:].bitcast(F32), b, half)
-            bank = banks[b % 2]
             for u in range(2):
-                nc.tensor.transpose(block(bank, u, P), words[:, u:half:2], ident[:])
+                nc.tensor.transpose(block(banks[b], u, P), words[:, u:half:2], ident[:])
             nc.scalar.copy(block(h_r[:].bitcast(F32), b, half).rearrange("q (j u) -> q j u", u=2),
-                           bank[:, 0:half].rearrange("q (u j) -> q j u", u=2))
+                           banks[b][:, 0:half].rearrange("q (u j) -> q j u", u=2))
 
-        dv = [f32_tile(f"dv{t}", L) for t in range(3)]
+        dv = [f32_tile(f"dv{t}", L // 2) for t in range(3)]
         du = [f32_tile(f"du{t}", L) for t in range(PACK)]
         out_0_rows = out_0.rearrange("(p t) c -> p t c", t=PACK)
         out_1_rows = out_1.rearrange("(p t) c -> p t c", t=PACK)
@@ -201,35 +236,47 @@ def tile_attend_gmf_cau_vu_kernel(tc, uT, vT, y, us, ts, offs, uoffs, out_0, out
             product(bank[:], wq_i[t // 2], E4M3, (t % 2) * P, hq_i, E5M2, 0, L)
             place(gene_windows[t % 2], gene_list, bank, du[t][:], out_1_rows[:, t, :])
 
-        weigh(0)
-        weigh(1)
-        for window in gene_windows:
-            nc.vector.memset(window[:].bitcast(I32), 0)
+        def cell_block(t, bank, stage):
+            product(bank[:], xq_r, E4M3, t * P, hq_r, E5M2, half, half + L)
+            place(cell_windows[t % 3], cell_list, bank, stage, out_0_rows[:, t, :])
+
+        for b in range(NEAR):
+            scale_near(b)
+        for b in range(NEAR):
+            residual_near(b)
+        for b in range(NEAR, PACK):
+            scale_far(b)
+        for b in range(2):
+            if b < NEAR:
+                weigh_near(b)
+            else:
+                weigh_far(b)
         quantize(hq_r, h_r, E5M2, 0, half, half)
-        cell_half(0, 0, banks[2], dv[0][:, 0:half])
-        weigh(2)
-        weigh(3)
-        cell_half(1, 0, banks[3], last_root[:, 0:half])
+        weigh_far(2)
+        weigh_far(3)
+        wq_i = [mx_tiles("wq_i0", L // 2, tag="us_all"), mx_tiles("wq_i1", L // 2)]
+        quantize(wq_i[0], w_i, E4M3, 0, half)
+        cell_half(0, 0, banks[0], block(root, 1)[:, 0:half])
         quantize(hq_r, h_r, E5M2, half, L, half)
-        cell_half(2, 0, banks[1], dv[2][:, 0:half])
+        cell_half(1, 0, banks[1], block(h_cells[:].bitcast(F32), 3, half))
+        cell_half(2, 0, banks[3], block(num, 3)[:, 0:half])
 
         h_i = bf16_tile("h_i")
         hq_i = mx_tiles("hq_i")
         for t in range(2):
-            cell_half(t, 1, banks[2 + t], dv[t][:, half:L])
+            cell_half(t, 1, banks[t], dv[t][:])
             nc.sync.dma_start(out_0_rows[:, t, :], cell_windows[t][:])
         for u in range(2):
-            turned = turn(h_r[:].bitcast(F32), u, banks[4 + u])
+            turned = turn(h_r[:].bitcast(F32), u, banks[u])
             nc.scalar.copy(h_i[:].rearrange("q (p u e s) -> q u p e s", u=2, e=2, s=PACK)[:, u],
                            turned.rearrange("q (s p e) -> q p e s", s=PACK, e=2))
         quantize(hq_i, h_i, E5M2)
-        cell_half(2, 1, banks[5], dv[2][:, half:L])
+        cell_half(2, 1, banks[1], dv[2][:])
         nc.sync.dma_start(out_0_rows[:, 2, :], cell_windows[2][:])
         gene_block(0, banks[6])
         gene_block(1, banks[7])
-        product(banks[0][:], xq_r, E4M3, 3 * P, hq_r, E5M2, half, half + L)
-        place(cell_windows[0], cell_list, banks[0], du[0][:], out_0_rows[:, 3, :])
-        turn_table(w_i, w_d, 1, banks[4])
+        turn_table(w_i, w_d, 1, banks[6])
         quantize(wq_i[1], w_i, E4M3, half, L, -half)
-        gene_block(2, banks[2])
-        gene_block(3, banks[3])
+        cell_block(3, banks[6], block(neg_a, 0))
+        gene_block(2, banks[3])
+        gene_block(3, banks[5])

@@ -116,17 +116,17 @@ def tile_attend_gmf_cau_vu_kernel(tc, uT, vT, y, us, ts, offs, uoffs, out_0, out
         for b in range(NEAR):
             nc.scalar.copy(block(neg_sc_woven, b).rearrange("p (j s) -> p j s", s=PACK), block(neg_sc, b).rearrange("p (s j) -> p j s", s=PACK))
 
-        x_planes = bf16_tile("x_planes")
+        x_planes = [f32_tile(f"x_planes{u}", 2 * L) for u in range(2)]
         x_d = bf16_tile("x_d")
         x_r = bf16_tile("x_r")
         for t in range(PACK):
-            if t < 2:
-                nc.vector.tensor_copy(block(x_planes, t), u_planes[t][:].indirect(gene_list[:]))
+            if t >= 2:
+                nc.vector.tensor_copy(block(x_planes[t // 2], t % 2), u_planes[t][:].indirect(gene_list[:]))
             else:
                 nc.vector.tensor_copy(x_d[:].rearrange("p (s m t) -> p m s t", s=PACK, t=PACK)[:, :, :, t], u_planes[t][:].indirect(gene_list[:]))
-            if t == 1:
+            if t % 2 == 1 and t >= 2:
                 nc.scalar.copy(x_d[:].rearrange("p (s m t) -> p s m t", s=PACK, t=PACK)[:, :, :, t - 1:t + 1],
-                               block(x_planes, t // 2, 2 * L).rearrange("p (e m s) -> p s m e", e=2, s=PACK))
+                               x_planes[t // 2][:].rearrange("p (e m s) -> p s m e", e=2, s=PACK))
             if t % 2 == 1:
                 turn_table(x_r, x_d, t // 2, banks[4 + t // 2], dealt=True)
 
@@ -152,7 +152,7 @@ def tile_attend_gmf_cau_vu_kernel(tc, uT, vT, y, us, ts, offs, uoffs, out_0, out
         quantize(xq_r, x_r, E4M3)
 
         cell_windows = [f32_tile(f"cell_window{k}", T) for k in range(3)]
-        gene_windows = [f32_tile(f"gene_window{k}", T, tag=f"u_plane{k + 1}") for k in range(2)]
+        gene_windows = [f32_tile(f"gene_window{k}", T, tag=f"u_plane{2 * k + 1}") for k in range(2)]
         for window in cell_windows + gene_windows:
             nc.vector.memset(window[:].bitcast(I32), 0)
 
@@ -187,7 +187,8 @@ def tile_attend_gmf_cau_vu_kernel(tc, uT, vT, y, us, ts, offs, uoffs, out_0, out
         def damping(b, first):
             nc.scalar.activation(woven(block(square, b % 2)), first, ACT.Square)
             nc.scalar.activation(block(root, b % 2), block(square, b % 2), ACT.Abs_reciprocal_sqrt, bias=1.0)
-            nc.scalar.activation(block(inv, b), block(root, b % 2), ACT.Square)
+            if b != 2:
+                nc.scalar.activation(block(inv, b), block(root, b % 2), ACT.Square)
 
         def weigh_near(b):
             damping(b, woven(block(neg_q, b)))
@@ -210,7 +211,11 @@ def tile_attend_gmf_cau_vu_kernel(tc, uT, vT, y, us, ts, offs, uoffs, out_0, out
             nc.vector.scalar_tensor_tensor(woven(block(num, b)), turned_q, neg_ts[:, b:b + 1], woven(us_all[:]), MULT, MULT)
             if b < PACK - 1:
                 damping(b, turned_q)
-            nc.vector.tensor_tensor(block(h_cells, b), block(num, b), block(inv, b), MULT)
+            if b == 2:
+                nc.vector.tensor_tensor(block(inv, b), block(num, b), block(root, b % 2), MULT)
+                nc.vector.tensor_tensor(block(h_cells, b), block(inv, b), block(root, b % 2), MULT)
+            else:
+                nc.vector.tensor_tensor(block(h_cells, b), block(num, b), block(inv, b), MULT)
             words = block(h_cells[:].bitcast(F32), b, half)
             for u in range(2):
                 nc.tensor.transpose(block(banks[b], u, P), words[:, u:half:2], ident[:])

@@ -116,17 +116,10 @@ def tile_attend_gmf_cau_vu_kernel(tc, uT, vT, y, us, ts, offs, uoffs, out_0, out
         for b in range(NEAR):
             nc.scalar.copy(block(neg_sc_woven, b).rearrange("p (j s) -> p j s", s=PACK), block(neg_sc, b).rearrange("p (s j) -> p j s", s=PACK))
 
-        x_planes = [f32_tile(f"x_planes{u}", 2 * L) for u in range(2)]
         x_d = bf16_tile("x_d")
         x_r = bf16_tile("x_r")
         for t in range(PACK):
-            if t >= 2:
-                nc.vector.tensor_copy(block(x_planes[t // 2], t % 2), u_planes[t][:].indirect(gene_list[:]))
-            else:
-                nc.vector.tensor_copy(x_d[:].rearrange("p (s m t) -> p m s t", s=PACK, t=PACK)[:, :, :, t], u_planes[t][:].indirect(gene_list[:]))
-            if t % 2 == 1 and t >= 2:
-                nc.scalar.copy(x_d[:].rearrange("p (s m t) -> p s m t", s=PACK, t=PACK)[:, :, :, t - 1:t + 1],
-                               x_planes[t // 2][:].rearrange("p (e m s) -> p s m e", e=2, s=PACK))
+            nc.vector.tensor_copy(x_d[:].rearrange("p (s m t) -> p m s t", s=PACK, t=PACK)[:, :, :, t], u_planes[t][:].indirect(gene_list[:]))
             if t % 2 == 1:
                 turn_table(x_r, x_d, t // 2, banks[4 + t // 2], dealt=True)
 
@@ -152,9 +145,11 @@ def tile_attend_gmf_cau_vu_kernel(tc, uT, vT, y, us, ts, offs, uoffs, out_0, out
         quantize(xq_r, x_r, E4M3)
 
         cell_windows = [f32_tile(f"cell_window{k}", T) for k in range(3)]
-        gene_windows = [f32_tile(f"gene_window{k}", T, tag=f"u_plane{2 * k + 1}") for k in range(2)]
-        for window in cell_windows + gene_windows:
+        gene_windows = [f32_tile(f"gene_window{k}", T, tag=f"u_plane{k}") for k in range(2)]
+        for window in cell_windows:
             nc.vector.memset(window[:].bitcast(I32), 0)
+        for window in gene_windows:
+            nc.gpsimd.memset(window[:].bitcast(I32), 0)
 
         neg_a = f32_tile("neg_a", PACK * L)
         num = f32_tile("num", PACK * L)

@@ -155,7 +155,7 @@ def tile_attend_gmf_cau_vu_kernel(tc, uT, vT, y, us, ts, offs, uoffs, out_0, out
         num = f32_tile("num", PACK * L)
         inv = f32_tile("inv", PACK * L)
         square = f32_tile("square", 2 * L)
-        root = f32_tile("root", 2 * L)
+        root = f32_tile("root", PACK * L)
         h_cells = bf16_tile("h_cells")
         h_r = bf16_tile("h_r")
         hq_r = mx_tiles("hq_r", half + L)
@@ -181,14 +181,15 @@ def tile_attend_gmf_cau_vu_kernel(tc, uT, vT, y, us, ts, offs, uoffs, out_0, out
 
         def damping(b, first):
             nc.scalar.activation(woven(block(square, b % 2)), first, ACT.Square)
-            nc.scalar.activation(block(root, b % 2), block(square, b % 2), ACT.Abs_reciprocal_sqrt, bias=1.0)
-            if b != 2:
-                nc.scalar.activation(block(inv, b), block(root, b % 2), ACT.Square)
+            nc.scalar.activation(block(root, b), block(square, b % 2), ACT.Abs_reciprocal_sqrt, bias=1.0)
+            if b >= NEAR:
+                nc.scalar.activation(block(inv, b), block(root, b), ACT.Square)
 
         def weigh_near(b):
             damping(b, woven(block(neg_q, b)))
-            nc.vector.tensor_tensor(block(num, b), block(neg_q, b), block(neg_sc_woven, b), MULT)
-            nc.vector.tensor_tensor(block(h_r, b), block(num, b), block(inv, b), MULT)
+            nc.gpsimd.tensor_tensor(block(num, b), block(neg_q, b), block(neg_sc_woven, b), MULT)
+            nc.vector.tensor_tensor(block(inv, b), block(num, b), block(root, b), MULT)
+            nc.vector.tensor_tensor(block(h_r, b), block(inv, b), block(root, b), MULT)
 
         def scale_far(b):
             nc.vector.tensor_tensor(block(neg_a, b), banks[b][:], block(neg_sc, b), MULT)
@@ -206,11 +207,7 @@ def tile_attend_gmf_cau_vu_kernel(tc, uT, vT, y, us, ts, offs, uoffs, out_0, out
             nc.vector.scalar_tensor_tensor(woven(block(num, b)), turned_q, neg_ts[:, b:b + 1], woven(us_all[:]), MULT, MULT)
             if b < PACK - 1:
                 damping(b, turned_q)
-            if b == 2:
-                nc.vector.tensor_tensor(block(inv, b), block(num, b), block(root, b % 2), MULT)
-                nc.vector.tensor_tensor(block(h_cells, b), block(inv, b), block(root, b % 2), MULT)
-            else:
-                nc.vector.tensor_tensor(block(h_cells, b), block(num, b), block(inv, b), MULT)
+            nc.vector.tensor_tensor(block(h_cells, b), block(num, b), block(inv, b), MULT)
             words = block(h_cells[:].bitcast(F32), b, half)
             for u in range(2):
                 nc.tensor.transpose(block(banks[b], u, P), words[:, u:half:2], ident[:])
@@ -256,7 +253,7 @@ def tile_attend_gmf_cau_vu_kernel(tc, uT, vT, y, us, ts, offs, uoffs, out_0, out
         weigh_far(3)
         wq_i = [mx_tiles("wq_i0", L // 2, tag="us_all"), mx_tiles("wq_i1", L // 2)]
         quantize(wq_i[0], w_i, E4M3, 0, half)
-        cell_half(0, 0, banks[0], block(root, 1)[:, 0:half])
+        cell_half(0, 0, banks[0], block(root, 3)[:, 0:half])
         quantize(hq_r, h_r, E5M2, half, L, half)
         cell_half(1, 0, banks[1], block(h_cells[:].bitcast(F32), 3, half))
         cell_half(2, 0, banks[3], block(num, 3)[:, 0:half])
@@ -271,7 +268,7 @@ def tile_attend_gmf_cau_vu_kernel(tc, uT, vT, y, us, ts, offs, uoffs, out_0, out
             nc.scalar.copy(h_i[:].rearrange("q (p u e s) -> q u p e s", u=2, e=2, s=PACK)[:, u],
                            turned.rearrange("q (s p e) -> q p e s", s=PACK, e=2))
         quantize(hq_i, h_i, E5M2)
-        cell_half(2, 1, banks[1], dv[2][:])
+        cell_half(2, 1, banks[0], dv[2][:])
         nc.sync.dma_start(out_0_rows[:, 2, :], cell_windows[2][:])
         gene_block(0, banks[6])
         gene_block(1, banks[7])

@@ -62,7 +62,7 @@ def tile_attend_gmf_cau_vu_kernel(tc, uT, vT, y, us, ts, offs, uoffs, out_0, out
         u_planes = [f32_tile(f"u_plane{t}", T) for t in range(PACK)]
         v_planes = [f32_tile(f"v_plane{t}", T) for t in range(PACK)]
         us_rows = f32_tile("us_rows", PACK)
-        y_halves = [f32_tile(f"y_half{k}", 2 * L) for k in range(2)]
+        y_rows = f32_tile("y_rows", PACK * L)
         uT_rows = uT.rearrange("(p t) c -> p t c", t=PACK)
         vT_rows = vT.rearrange("(p t) c -> p t c", t=PACK)
         nc.sync.dma_start(u_planes[0][:], uT_rows[:, 0, :])
@@ -75,9 +75,7 @@ def tile_attend_gmf_cau_vu_kernel(tc, uT, vT, y, us, ts, offs, uoffs, out_0, out
             nc.sync.dma_start(u_planes[t][:], uT_rows[:, t, :])
         for t in range(PACK):
             nc.sync.dma_start(v_planes[t][:], vT_rows[:, t, :])
-        y_rows = y.rearrange("b (p s) i -> p (b s) i", s=PACK)
-        for k in range(2):
-            nc.sync.dma_start(y_halves[k][:].rearrange("p (s i) -> p s i", s=PACK), y_rows[:, :, k * L // 2:(k + 1) * L // 2])
+        nc.sync.dma_start(y_rows[:], y.rearrange("b (p s) i -> p (b s i)", s=PACK))
 
         warm = f32_tile("warm", 8)
         nc.scalar.activation(warm[:, 0:1], ident[:, 0:1], ACT.Abs_reciprocal_sqrt, bias=1.0)
@@ -145,11 +143,10 @@ def tile_attend_gmf_cau_vu_kernel(tc, uT, vT, y, us, ts, offs, uoffs, out_0, out
         quantize(xq_r, x_r, E4M3)
 
         cell_windows = [f32_tile(f"cell_window{k}", T) for k in range(3)]
-        gene_windows = [f32_tile(f"gene_window{k}", T, tag=f"u_plane{k}") for k in range(2)]
         for window in cell_windows:
             nc.vector.memset(window[:].bitcast(I32), 0)
-        for window in gene_windows:
-            nc.gpsimd.memset(window[:].bitcast(I32), 0)
+        gene_windows = [f32_tile("gene_window0", T, tag="x_r")]
+        nc.gpsimd.memset(gene_windows[0][:].bitcast(I32), 0)
 
         neg_a = f32_tile("neg_a", PACK * L)
         num = f32_tile("num", PACK * L)
@@ -166,7 +163,7 @@ def tile_attend_gmf_cau_vu_kernel(tc, uT, vT, y, us, ts, offs, uoffs, out_0, out
         neg_q = f32_tile("neg_q", NEAR * L)
 
         def y_chunk(b):
-            return y_halves[b // 2][:].rearrange("p (s b j) -> p b s j", s=PACK, b=2)[:, b % 2]
+            return y_rows[:].rearrange("p (s b j) -> p b s j", s=PACK, b=PACK)[:, b]
 
         def woven(ap):
             return ap.rearrange("p (j s) -> p j s", s=PACK)
@@ -248,6 +245,8 @@ def tile_attend_gmf_cau_vu_kernel(tc, uT, vT, y, us, ts, offs, uoffs, out_0, out
                 weigh_near(b)
             else:
                 weigh_far(b)
+        gene_windows.append(f32_tile("gene_window1", T, tag="neg_sc_woven"))
+        nc.gpsimd.memset(gene_windows[1][:].bitcast(I32), 0)
         quantize(hq_r, h_r, E5M2, 0, half, half)
         weigh_far(2)
         weigh_far(3)

@@ -62,7 +62,7 @@ def tile_attend_gmf_cau_vu_kernel(tc, uT, vT, y, us, ts, offs, uoffs, out_0, out
         u_planes = [f32_tile(f"u_plane{t}", T) for t in range(PACK)]
         v_planes = [f32_tile(f"v_plane{t}", T) for t in range(PACK)]
         us_rows = f32_tile("us_rows", PACK)
-        y_rows = f32_tile("y_rows", PACK * L)
+        y_halves = [f32_tile(f"y_half{k}", 2 * L) for k in range(2)]
         uT_rows = uT.rearrange("(p t) c -> p t c", t=PACK)
         vT_rows = vT.rearrange("(p t) c -> p t c", t=PACK)
         nc.sync.dma_start(u_planes[0][:], uT_rows[:, 0, :])
@@ -75,7 +75,9 @@ def tile_attend_gmf_cau_vu_kernel(tc, uT, vT, y, us, ts, offs, uoffs, out_0, out
             nc.sync.dma_start(u_planes[t][:], uT_rows[:, t, :])
         for t in range(PACK):
             nc.sync.dma_start(v_planes[t][:], vT_rows[:, t, :])
-        nc.sync.dma_start(y_rows[:], y.rearrange("b (p s) i -> p (b s i)", s=PACK))
+        y_rows = y.rearrange("b (p s) i -> p (b s) i", s=PACK)
+        for k in range(2):
+            nc.sync.dma_start(y_halves[k][:].rearrange("p (s i) -> p s i", s=PACK), y_rows[:, :, k * L // 2:(k + 1) * L // 2])
 
         warm = f32_tile("warm", 8)
         nc.scalar.activation(warm[:, 0:1], ident[:, 0:1], ACT.Abs_reciprocal_sqrt, bias=1.0)
@@ -163,7 +165,7 @@ def tile_attend_gmf_cau_vu_kernel(tc, uT, vT, y, us, ts, offs, uoffs, out_0, out
         neg_q = f32_tile("neg_q", NEAR * L)
 
         def y_chunk(b):
-            return y_rows[:].rearrange("p (s b j) -> p b s j", s=PACK, b=PACK)[:, b]
+            return y_halves[b // 2][:].rearrange("p (s b j) -> p b s j", s=PACK, b=2)[:, b % 2]
 
         def woven(ap):
             return ap.rearrange("p (j s) -> p j s", s=PACK)

@@ -56,7 +56,7 @@ def tile_attend_gmf_cau_vu_kernel(tc, uT, vT, y, us, ts, offs, uoffs, out_0, out
 
         ident = f32_tile("ident", P)
         ts_table = f32_tile("ts_table", T)
-        nc.vector.memset(ts_table[:].bitcast(I32), 0)
+        nc.vector.memset(ts_table[0:P - 1, :].bitcast(I32), 0)
         make_identity(nc, ident[:])
 
         u_planes = [f32_tile(f"u_plane{t}", T) for t in range(PACK)]
@@ -70,7 +70,7 @@ def tile_attend_gmf_cau_vu_kernel(tc, uT, vT, y, us, ts, offs, uoffs, out_0, out
         nc.sync.dma_start(cell_list[:], offs)
         nc.sync.dma_start(us_rows[:], us.rearrange("b (p s) o -> p (b s o)", s=PACK))
         nc.sync.dma_start(u_planes[1][:], uT_rows[:, 1, :])
-        nc.scalar.dma_start(ts_table[0:1, :], ts[0:1, :])
+        nc.scalar.dma_start(ts_table[P - 1:P, :], ts[0:1, :])
         for t in range(2, PACK):
             nc.sync.dma_start(u_planes[t][:], uT_rows[:, t, :])
         for t in range(PACK):
@@ -106,7 +106,7 @@ def tile_attend_gmf_cau_vu_kernel(tc, uT, vT, y, us, ts, offs, uoffs, out_0, out
         nc.scalar.copy(us_all[:].rearrange("q (p s) -> q p s", s=PACK), banks[0][:].rearrange("q (s p) -> q p s", s=PACK))
         for b in range(PACK):
             nc.tensor.transpose(block(banks[6], b, P), block(ts_listed, b, P), ident[:])
-        nc.scalar.activation(neg_ts[:], banks[6][:, 0:L:P], ACT.Copy, scale=-1.0)
+        nc.scalar.activation(neg_ts[:], banks[6][:, P - 1:L:P], ACT.Copy, scale=-1.0)
         for b in range(PACK):
             nc.tensor.transpose(block(banks[7], b, P), neg_ts[:, b:b + 1].to_broadcast([P, P]), ident[:])
         for m in range(PACK):
@@ -123,10 +123,19 @@ def tile_attend_gmf_cau_vu_kernel(tc, uT, vT, y, us, ts, offs, uoffs, out_0, out
             if t % 2 == 1:
                 turn_table(x_r, x_d, t // 2, banks[4 + t // 2], dealt=True)
 
+        hq_r = mx_tiles("hq_r", L // 2 + L)
+        nc.gpsimd.memset(hq_r[0][:, 0:L // 2], 0)
+        nc.gpsimd.memset(hq_r[1][:, 0:L // 2], 0)
+        cell_windows = [f32_tile(f"cell_window{k}", T) for k in range(3)] + [f32_tile("cell_window3", T, tag="u_plane0")]
+        gene_windows = [f32_tile(f"gene_window{k}", T, tag=f"u_plane{k + 1}") for k in range(2)]
+        nc.vector.memset(cell_windows[0][:].bitcast(I32), 0)
+        for window in cell_windows[1:] + gene_windows:
+            nc.gpsimd.memset(window[:].bitcast(I32), 0)
+
         w_d = bf16_tile("w_d")
         w_i = bf16_tile("w_i")
         xq_d = mx_tiles("xq_d", tag="v_plane0")
-        xq_r = mx_tiles("xq_r", tag="v_plane3")
+        xq_r = mx_tiles("xq_r", tag="v_plane1")
         wq_d = mx_tiles("wq_d")
         half = L // 2
         for t in range(2):
@@ -134,6 +143,7 @@ def tile_attend_gmf_cau_vu_kernel(tc, uT, vT, y, us, ts, offs, uoffs, out_0, out
         turn_table(w_i, w_d, 0, banks[4])
         quantize(xq_d, x_d, E4M3)
         nc.vector.tensor_copy(w_d[:, 2:L * PACK:PACK], v_planes[2][:].indirect(cell_list[:]))
+        quantize(xq_r, x_r, E4M3)
         for k in range(2):
             nc.vector.tensor_copy(w_d[:, k * 1024 + 3:(k + 1) * 1024:PACK],
                                   v_planes[3][:].indirect(cell_list[:, k * 16:(k + 1) * 16]))
@@ -142,13 +152,8 @@ def tile_attend_gmf_cau_vu_kernel(tc, uT, vT, y, us, ts, offs, uoffs, out_0, out
             for m in range(PACK):
                 product(block(banks[b], m, P), xq_d, E4M3, m * P, wq_d, E4M3, b * P, (b + 1) * P)
 
-        quantize(xq_r, x_r, E4M3)
-
-        cell_windows = [f32_tile(f"cell_window{k}", T) for k in range(3)]
-        for window in cell_windows:
-            nc.vector.memset(window[:].bitcast(I32), 0)
-        gene_windows = [f32_tile("gene_window0", T, tag="x_r")]
-        nc.gpsimd.memset(gene_windows[0][:].bitcast(I32), 0)
+        wq_i = [mx_tiles("wq_i0", L // 2, tag="v_plane3"), mx_tiles("wq_i1", L // 2)]
+        quantize(wq_i[0], w_i, E4M3, 0, half)
 
         neg_a = f32_tile("neg_a", PACK * L)
         num = f32_tile("num", PACK * L)
@@ -157,9 +162,6 @@ def tile_attend_gmf_cau_vu_kernel(tc, uT, vT, y, us, ts, offs, uoffs, out_0, out
         root = f32_tile("root", PACK * L)
         h_cells = bf16_tile("h_cells")
         h_r = bf16_tile("h_r")
-        hq_r = mx_tiles("hq_r", half + L)
-        nc.gpsimd.memset(hq_r[0][:, 0:half], 0)
-        nc.gpsimd.memset(hq_r[1][:, 0:half], 0)
         q_banks = banks[4:8]
 
         neg_q = f32_tile("neg_q", NEAR * L)
@@ -230,11 +232,7 @@ def tile_attend_gmf_cau_vu_kernel(tc, uT, vT, y, us, ts, offs, uoffs, out_0, out
 
         def gene_block(t, bank):
             product(bank[:], wq_i[t // 2], E4M3, (t % 2) * P, hq_i, E5M2, 0, L)
-            place(gene_windows[t % 2], gene_list, bank, du[t][:], out_1_rows[:, t, :])
-
-        def cell_block(t, bank, stage):
-            product(bank[:], xq_r, E4M3, t * P, hq_r, E5M2, half, half + L)
-            place(cell_windows[t % 3], cell_list, bank, stage, out_0_rows[:, t, :])
+            place(gene_windows[t % 3], gene_list, bank, du[t][:], out_1_rows[:, t, :])
 
         for b in range(NEAR):
             scale_near(b)
@@ -247,13 +245,9 @@ def tile_attend_gmf_cau_vu_kernel(tc, uT, vT, y, us, ts, offs, uoffs, out_0, out
                 weigh_near(b)
             else:
                 weigh_far(b)
-        gene_windows.append(f32_tile("gene_window1", T, tag="neg_sc_woven"))
-        nc.gpsimd.memset(gene_windows[1][:].bitcast(I32), 0)
         quantize(hq_r, h_r, E5M2, 0, half, half)
         weigh_far(2)
         weigh_far(3)
-        wq_i = [mx_tiles("wq_i0", L // 2, tag="us_all"), mx_tiles("wq_i1", L // 2)]
-        quantize(wq_i[0], w_i, E4M3, 0, half)
         cell_half(0, 0, banks[0], block(root, 3)[:, 0:half])
         quantize(hq_r, h_r, E5M2, half, L, half)
         cell_half(1, 0, banks[1], block(h_cells[:].bitcast(F32), 3, half))
@@ -261,20 +255,21 @@ def tile_attend_gmf_cau_vu_kernel(tc, uT, vT, y, us, ts, offs, uoffs, out_0, out
 
         h_i = bf16_tile("h_i")
         hq_i = mx_tiles("hq_i")
-        for t in range(2):
+        for t in range(3):
             cell_half(t, 1, banks[t], dv[t][:])
             nc.sync.dma_start(out_0_rows[:, t, :], cell_windows[t][:])
         for u in range(2):
-            turned = turn(h_r[:].bitcast(F32), u, banks[u])
+            turned = turn(h_r[:].bitcast(F32), u, banks[4 + u])
             nc.scalar.copy(h_i[:].rearrange("q (p u e s) -> q u p e s", u=2, e=2, s=PACK)[:, u],
                            turned.rearrange("q (s p e) -> q p e s", s=PACK, e=2))
+        turn_table(w_i, w_d, 1, banks[4])
         quantize(hq_i, h_i, E5M2)
-        cell_half(2, 1, banks[0], dv[2][:])
-        nc.sync.dma_start(out_0_rows[:, 2, :], cell_windows[2][:])
-        gene_block(0, banks[6])
-        gene_block(1, banks[7])
-        turn_table(w_i, w_d, 1, banks[6])
         quantize(wq_i[1], w_i, E4M3, half, L, -half)
-        cell_block(3, banks[6], block(neg_a, 0))
-        gene_block(2, banks[3])
-        gene_block(3, banks[5])
+        product(banks[3][:], xq_r, E4M3, 3 * P, hq_r, E5M2, half, half + L)
+        place(cell_windows[3], cell_list, banks[3], w_d[:].bitcast(F32)[:, 0:L], out_0_rows[:, 3, :])
+        gene_windows.append(f32_tile("gene_window2", T, tag="cell_window0"))
+        nc.gpsimd.memset(gene_windows[2][:].bitcast(I32), 0)
+        gene_block(0, banks[7])
+        gene_block(1, banks[2])
+        gene_block(2, banks[0])
+        gene_block(3, banks[1])

@@ -232,7 +232,7 @@ def tile_attend_gmf_cau_vu_kernel(tc, uT, vT, y, us, ts, offs, uoffs, out_0, out
 
         def gene_block(t, bank):
             product(bank[:], wq_i[t // 2], E4M3, (t % 2) * P, hq_i, E5M2, 0, L)
-            place(gene_windows[t % 3], gene_list, bank, du[t][:], out_1_rows[:, t, :])
+            place(gene_windows[t % 2], gene_list, bank, du[t][:], out_1_rows[:, t, :])
 
         for b in range(NEAR):
             scale_near(b)
@@ -259,17 +259,22 @@ def tile_attend_gmf_cau_vu_kernel(tc, uT, vT, y, us, ts, offs, uoffs, out_0, out
             cell_half(t, 1, banks[t], dv[t][:])
             nc.sync.dma_start(out_0_rows[:, t, :], cell_windows[t][:])
         for u in range(2):
-            turned = turn(h_r[:].bitcast(F32), u, banks[4 + u])
+            turned = turn(h_r[:].bitcast(F32), u, banks[u])
             nc.scalar.copy(h_i[:].rearrange("q (p u e s) -> q u p e s", u=2, e=2, s=PACK)[:, u],
                            turned.rearrange("q (s p e) -> q p e s", s=PACK, e=2))
-        turn_table(w_i, w_d, 1, banks[4])
         quantize(hq_i, h_i, E5M2)
-        quantize(wq_i[1], w_i, E4M3, half, L, -half)
         product(banks[3][:], xq_r, E4M3, 3 * P, hq_r, E5M2, half, half + L)
-        place(cell_windows[3], cell_list, banks[3], w_d[:].bitcast(F32)[:, 0:L], out_0_rows[:, 3, :])
-        gene_windows.append(f32_tile("gene_window2", T, tag="cell_window0"))
-        nc.gpsimd.memset(gene_windows[2][:].bitcast(I32), 0)
-        gene_block(0, banks[7])
-        gene_block(1, banks[2])
-        gene_block(2, banks[0])
-        gene_block(3, banks[1])
+
+        def last_plane_half(k, stage):
+            nc.scalar.copy(stage, block(banks[3], k, half))
+            nc.vector.tensor_copy(cell_windows[3][:].indirect(cell_list[:, k * 16:(k + 1) * 16]), stage)
+
+        last_plane_half(0, h_r[:].bitcast(F32)[:, 0:half])
+        turn_table(w_i, w_d, 1, banks[2])
+        quantize(wq_i[1], w_i, E4M3, half, L, -half)
+        gene_block(0, banks[4])
+        gene_block(1, banks[5])
+        last_plane_half(1, du[0][:, 0:half])
+        nc.sync.dma_start(out_0_rows[:, 3, :], cell_windows[3][:])
+        gene_block(2, banks[6])
+        gene_block(3, banks[7])

@@ -186,11 +186,12 @@ def tile_attend_gmf_cau_vu_kernel(tc, uT, vT, y, us, ts, offs, uoffs, out_0, out
             if b >= NEAR:
                 nc.scalar.activation(block(inv, b), block(root, b), ACT.Square)
 
+        part = [f32_tile(f"part{b}", L) for b in range(NEAR)]
+
         def weigh_near(b):
             damping(b, woven(block(neg_q, b)))
-            nc.gpsimd.tensor_tensor(block(num, b), block(neg_q, b), block(neg_sc_woven, b), MULT)
-            nc.vector.tensor_tensor(block(inv, b), block(num, b), block(root, b), MULT)
-            nc.vector.tensor_tensor(block(h_r, b), block(inv, b), block(root, b), MULT)
+            nc.vector.tensor_tensor(part[b][:], block(num, b), block(root, b), MULT)
+            nc.vector.tensor_tensor(block(h_r, b), part[b][:], block(root, b), MULT)
 
         def scale_far(b):
             nc.vector.tensor_tensor(block(neg_a, b), banks[b][:], block(neg_sc, b), MULT)
@@ -203,12 +204,10 @@ def tile_attend_gmf_cau_vu_kernel(tc, uT, vT, y, us, ts, offs, uoffs, out_0, out
 
         def weigh_far(b):
             turned_q = q_banks[b][:].rearrange("j (s p) -> j p s", s=PACK)
-            if b == PACK - 1:
-                damping(b, turned_q)
-            nc.vector.scalar_tensor_tensor(woven(block(num, b)), turned_q, neg_ts[:, b:b + 1], woven(us_all[:]), MULT, MULT)
-            if b < PACK - 1:
-                damping(b, turned_q)
-            nc.vector.tensor_tensor(block(h_cells, b), block(num, b), block(inv, b), MULT)
+            far_num = part[1][:] if b == NEAR else block(root, 1)
+            damping(b, turned_q)
+            nc.vector.scalar_tensor_tensor(woven(far_num), turned_q, neg_ts[:, b:b + 1], woven(us_all[:]), MULT, MULT)
+            nc.gpsimd.tensor_tensor(block(h_cells, b), far_num, block(inv, b), MULT)
             words = block(h_cells[:].bitcast(F32), b, half)
             for u in range(2):
                 nc.tensor.transpose(block(banks[b], u, P), words[:, u:half:2], ident[:])
@@ -238,20 +237,20 @@ def tile_attend_gmf_cau_vu_kernel(tc, uT, vT, y, us, ts, offs, uoffs, out_0, out
             scale_near(b)
         for b in range(NEAR):
             residual_near(b)
+        nc.gpsimd.tensor_tensor(block(num, 0), block(neg_q, 0), block(neg_sc_woven, 0), MULT)
         for b in range(NEAR, PACK):
             scale_far(b)
-        for b in range(2):
-            if b < NEAR:
-                weigh_near(b)
-            else:
-                weigh_far(b)
-        quantize(hq_r, h_r, E5M2, 0, half, half)
+        nc.vector.tensor_tensor(block(num, 1), block(neg_q, 1), block(neg_sc_woven, 1), MULT)
+        for b in range(NEAR):
+            weigh_near(b)
+        for b in range(NEAR):
+            quantize(hq_r, h_r, E5M2, b * P, (b + 1) * P, half)
         weigh_far(2)
         weigh_far(3)
         cell_half(0, 0, banks[0], block(root, 3)[:, 0:half])
+        cell_half(1, 0, banks[1], block(root, 3)[:, half:L])
         quantize(hq_r, h_r, E5M2, half, L, half)
-        cell_half(1, 0, banks[1], block(h_cells[:].bitcast(F32), 3, half))
-        cell_half(2, 0, banks[3], block(num, 3)[:, 0:half])
+        cell_half(2, 0, banks[4], block(h_cells[:].bitcast(F32), 3, half))
 
         h_i = bf16_tile("h_i")
         hq_i = mx_tiles("hq_i")

@@ -135,7 +135,7 @@ def tile_attend_gmf_cau_vu_kernel(tc, uT, vT, y, us, ts, offs, uoffs, out_0, out
         w_d = bf16_tile("w_d")
         w_i = bf16_tile("w_i")
         xq_d = mx_tiles("xq_d", tag="v_plane0")
-        xq_r = mx_tiles("xq_r", tag="v_plane1")
+        xq_r = mx_tiles("xq_r", L + L // 2, tag="v_plane3")
         wq_d = mx_tiles("wq_d")
         half = L // 2
         for t in range(2):
@@ -143,21 +143,22 @@ def tile_attend_gmf_cau_vu_kernel(tc, uT, vT, y, us, ts, offs, uoffs, out_0, out
         turn_table(w_i, w_d, 0, banks[4])
         quantize(xq_d, x_d, E4M3)
         nc.vector.tensor_copy(w_d[:, 2:L * PACK:PACK], v_planes[2][:].indirect(cell_list[:]))
-        quantize(xq_r, x_r, E4M3)
         for k in range(2):
             nc.vector.tensor_copy(w_d[:, k * 1024 + 3:(k + 1) * 1024:PACK],
                                   v_planes[3][:].indirect(cell_list[:, k * 16:(k + 1) * 16]))
-            quantize(wq_d, w_d, E4M3, k * half, (k + 1) * half)
+            for c0, c1 in (((0, P), (P, half)), ((half, L),))[k]:
+                quantize(wq_d, w_d, E4M3, c0, c1)
         for b in range(PACK):
             for m in range(PACK):
                 product(block(banks[b], m, P), xq_d, E4M3, m * P, wq_d, E4M3, b * P, (b + 1) * P)
 
-        wq_i = [mx_tiles("wq_i0", L // 2, tag="v_plane3"), mx_tiles("wq_i1", L // 2)]
+        quantize(xq_r, x_r, E4M3)
+        wq_i = [(xq_r[0][:, L:L + half], xq_r[1][:, L:L + half]), mx_tiles("wq_i1", half)]
         quantize(wq_i[0], w_i, E4M3, 0, half)
 
         neg_a = f32_tile("neg_a", PACK * L)
-        num = f32_tile("num", PACK * L)
-        inv = f32_tile("inv", PACK * L)
+        num = f32_tile("num", NEAR * L)
+        inv = f32_tile("inv", (PACK - NEAR) * L)
         square = f32_tile("square", 2 * L)
         root = f32_tile("root", PACK * L)
         h_cells = bf16_tile("h_cells")
@@ -184,7 +185,7 @@ def tile_attend_gmf_cau_vu_kernel(tc, uT, vT, y, us, ts, offs, uoffs, out_0, out
             nc.scalar.activation(woven(block(square, b % 2)), first, ACT.Square)
             nc.scalar.activation(block(root, b), block(square, b % 2), ACT.Abs_reciprocal_sqrt, bias=1.0)
             if b >= NEAR:
-                nc.scalar.activation(block(inv, b), block(root, b), ACT.Square)
+                nc.scalar.activation(block(inv, b - NEAR), block(root, b), ACT.Square)
 
         part = [f32_tile(f"part{b}", L) for b in range(NEAR)]
 
@@ -207,7 +208,7 @@ def tile_attend_gmf_cau_vu_kernel(tc, uT, vT, y, us, ts, offs, uoffs, out_0, out
             far_num = part[1][:] if b == NEAR else block(root, 1)
             damping(b, turned_q)
             nc.vector.scalar_tensor_tensor(woven(far_num), turned_q, neg_ts[:, b:b + 1], woven(us_all[:]), MULT, MULT)
-            nc.gpsimd.tensor_tensor(block(h_cells, b), far_num, block(inv, b), MULT)
+            nc.gpsimd.tensor_tensor(block(h_cells, b), far_num, block(inv, b - NEAR), MULT)
             words = block(h_cells[:].bitcast(F32), b, half)
             for u in range(2):
                 nc.tensor.transpose(block(banks[b], u, P), words[:, u:half:2], ident[:])

@@ -127,21 +127,21 @@ def tile_attend_gmf_cau_vu_kernel(tc, uT, vT, y, us, ts, offs, uoffs, out_0, out
         nc.gpsimd.memset(hq_r[0][:, 0:L // 2], 0)
         nc.gpsimd.memset(hq_r[1][:, 0:L // 2], 0)
         cell_windows = [f32_tile(f"cell_window{k}", T) for k in range(3)] + [f32_tile("cell_window3", T, tag="u_plane0")]
-        gene_windows = [f32_tile(f"gene_window{k}", T, tag=f"u_plane{k + 1}") for k in range(2)]
+        gene_windows = [f32_tile("gene_window0", T, tag="u_plane1")]
         nc.vector.memset(cell_windows[0][:].bitcast(I32), 0)
         for window in cell_windows[1:] + gene_windows:
             nc.gpsimd.memset(window[:].bitcast(I32), 0)
 
         w_d = bf16_tile("w_d")
         w_i = bf16_tile("w_i")
-        xq_d = mx_tiles("xq_d", tag="v_plane0")
+        xq_d = mx_tiles("xq_d")
         xq_r = mx_tiles("xq_r", L + L // 2, tag="v_plane3")
         wq_d = mx_tiles("wq_d")
         half = L // 2
+        quantize(xq_d, x_d, E4M3)
         for t in range(2):
             nc.vector.tensor_copy(w_d[:, t:L * PACK:PACK], v_planes[t][:].indirect(cell_list[:]))
         turn_table(w_i, w_d, 0, banks[4])
-        quantize(xq_d, x_d, E4M3)
         nc.vector.tensor_copy(w_d[:, 2:L * PACK:PACK], v_planes[2][:].indirect(cell_list[:]))
         for k in range(2):
             nc.vector.tensor_copy(w_d[:, k * 1024 + 3:(k + 1) * 1024:PACK],
@@ -208,7 +208,7 @@ def tile_attend_gmf_cau_vu_kernel(tc, uT, vT, y, us, ts, offs, uoffs, out_0, out
             far_num = part[1][:] if b == NEAR else block(root, 1)
             damping(b, turned_q)
             nc.vector.scalar_tensor_tensor(woven(far_num), turned_q, neg_ts[:, b:b + 1], woven(us_all[:]), MULT, MULT)
-            nc.gpsimd.tensor_tensor(block(h_cells, b), far_num, block(inv, b - NEAR), MULT)
+            (nc.vector if b == NEAR else nc.gpsimd).tensor_tensor(block(h_cells, b), far_num, block(inv, b - NEAR), MULT)
             words = block(h_cells[:].bitcast(F32), b, half)
             for u in range(2):
                 nc.tensor.transpose(block(banks[b], u, P), words[:, u:half:2], ident[:])
@@ -238,10 +238,10 @@ def tile_attend_gmf_cau_vu_kernel(tc, uT, vT, y, us, ts, offs, uoffs, out_0, out
             scale_near(b)
         for b in range(NEAR):
             residual_near(b)
-        nc.gpsimd.tensor_tensor(block(num, 0), block(neg_q, 0), block(neg_sc_woven, 0), MULT)
+        nc.gpsimd.tensor_tensor(num[:, 0:L], neg_q[:, 0:L], neg_sc_woven[:, 0:L], MULT)
         for b in range(NEAR, PACK):
             scale_far(b)
-        nc.vector.tensor_tensor(block(num, 1), block(neg_q, 1), block(neg_sc_woven, 1), MULT)
+        nc.vector.tensor_tensor(num[:, L:NEAR * L], neg_q[:, L:NEAR * L], neg_sc_woven[:, L:NEAR * L], MULT)
         for b in range(NEAR):
             weigh_near(b)
         for b in range(NEAR):
@@ -252,6 +252,9 @@ def tile_attend_gmf_cau_vu_kernel(tc, uT, vT, y, us, ts, offs, uoffs, out_0, out
         cell_half(1, 0, banks[1], block(root, 3)[:, half:L])
         quantize(hq_r, h_r, E5M2, half, L, half)
         cell_half(2, 0, banks[4], block(h_cells[:].bitcast(F32), 3, half))
+
+        gene_windows.append(f32_tile("gene_window1", T, tag="h_cells"))
+        nc.gpsimd.memset(gene_windows[1][:].bitcast(I32), 0)
 
         h_i = bf16_tile("h_i")
         hq_i = mx_tiles("hq_i")

@@ -18,8 +18,12 @@ ADD = mybir.AluOpType.add
 P = 128
 PACK = 4
 L = 512
+HALF = L // 2
 T = 2048
-NEAR = 2
+LIST_HALF = HALF // 16
+PAIR = 2 * L
+GENE_MAJOR = 2
+EARLY_PLANES = 3
 FLOPS = 3 * 2 * L * L * L
 BYTES = 4 * (4 * L * T + L * L + L + T) + 2 * 2 * P * 32
 
@@ -38,7 +42,7 @@ def tile_attend_gmf_cau_vu_kernel(tc, uT, vT, y, us, ts, offs, uoffs, out_0, out
         def f32_tile(name, width, tag=None):
             return sb.tile([P, width], F32, name=name, tag=tag or name, align_bytes=64)
 
-        def bf16_tile(name):
+        def woven_tile(name):
             return sb.tile([P, L * PACK], BF16, name=name, align_bytes=64)
 
         def mx_tiles(name, width=L, tag=None):
@@ -54,230 +58,256 @@ def tile_attend_gmf_cau_vu_kernel(tc, uT, vT, y, us, ts, offs, uoffs, out_0, out
                                 rhs=rhs[0][:, n0:n1].bitcast(rhs_fmt), rhs_scale=rhs[1][:, n0:n1],
                                 start=True, stop=True)
 
+        def block(tile_, b, width=L):
+            return tile_[:, b * width:(b + 1) * width]
+
+        def list_half(offsets, k):
+            return block(offsets, k, LIST_HALF)
+
         ident = f32_tile("ident", P)
         ts_table = f32_tile("ts_table", T)
+        us_table = f32_tile("us_table", L)
+        nc.vector.memset(us_table[0:P - 1, :].bitcast(I32), 0)
         nc.vector.memset(ts_table[0:P - 1, :].bitcast(I32), 0)
         make_identity(nc, ident[:])
 
         u_planes = [f32_tile(f"u_plane{t}", T) for t in range(PACK)]
         v_planes = [f32_tile(f"v_plane{t}", T) for t in range(PACK)]
-        us_rows = f32_tile("us_rows", PACK)
-        y_halves = [f32_tile(f"y_half{k}", 2 * L) for k in range(2)]
+        y_chunks = [f32_tile(f"y_chunk{c}", L) for c in range(PACK)]
         uT_rows = uT.rearrange("(p t) c -> p t c", t=PACK)
         vT_rows = vT.rearrange("(p t) c -> p t c", t=PACK)
-        nc.sync.dma_start(u_planes[0][:], uT_rows[:, 0, :])
-        nc.sync.dma_start(gene_list[:], uoffs)
+        nc.sync.dma_start(v_planes[0][:], vT_rows[:, 0, :])
         nc.sync.dma_start(cell_list[:], offs)
-        nc.sync.dma_start(us_rows[:], us.rearrange("b (p s) o -> p (b s o)", s=PACK))
-        nc.sync.dma_start(u_planes[1][:], uT_rows[:, 1, :])
+        nc.sync.dma_start(gene_list[:], uoffs)
+        nc.sync.dma_start(v_planes[1][:], vT_rows[:, 1, :])
         nc.scalar.dma_start(ts_table[P - 1:P, :], ts[0:1, :])
+        nc.scalar.dma_start(us_table[P - 1:P, :], us.rearrange("b r o -> b (r o)"))
         for t in range(2, PACK):
-            nc.sync.dma_start(u_planes[t][:], uT_rows[:, t, :])
-        for t in range(PACK):
             nc.sync.dma_start(v_planes[t][:], vT_rows[:, t, :])
-        y_rows = y.rearrange("b (p s) i -> p (b s) i", s=PACK)
-        for k in range(2):
-            nc.sync.dma_start(y_halves[k][:].rearrange("p (s i) -> p s i", s=PACK), y_rows[:, :, k * L // 2:(k + 1) * L // 2])
+        for t in range(PACK):
+            nc.sync.dma_start(u_planes[t][:], uT_rows[:, t, :])
+        y_rows = y.rearrange("b (c p) i -> p (b c) i", p=P)
+        for c in (1, 0, 2, 3):
+            nc.sync.dma_start(y_chunks[c][:], y_rows[:, c, :])
 
         warm = f32_tile("warm", 8)
         nc.scalar.activation(warm[:, 0:1], ident[:, 0:1], ACT.Abs_reciprocal_sqrt, bias=1.0)
 
-        def block(tile_, b, width=L):
-            return tile_[:, b * width:(b + 1) * width]
-
-        def turn(src_words, u, bank, dealt=False):
+        def turn(src, u, bank):
+            words = src[:].bitcast(F32)
             for s in range(PACK):
-                a, step = (2 * P * s + u, 2) if dealt else (2 * s + u, 8)
-                nc.tensor.transpose(block(bank, s, P), src_words[:, a:a + step * (P - 1) + 1:step], ident[:])
+                nc.tensor.transpose(block(bank, s, P), words[:, 2 * s + u:2 * L:2 * PACK], ident[:])
             return bank[:].bitcast(BF16)
 
-        def turn_table(dst, src, u, bank, dealt=False):
-            turned = turn(src[:].bitcast(F32), u, bank, dealt)
-            nc.scalar.copy(block(dst, u, 1024).rearrange("q (e p s) -> q e p s", e=2, s=PACK),
+        def turn_table(dst, src, u, bank):
+            turned = turn(src, u, bank)
+            nc.scalar.copy(block(dst, u, PAIR).rearrange("q (e p s) -> q e p s", e=2, s=PACK),
                            turned.rearrange("q (s p e) -> q e p s", s=PACK, e=2))
 
         ts_listed = f32_tile("ts_listed", L)
-        neg_ts = f32_tile("neg_ts", PACK)
-        us_all = f32_tile("us_all", L)
+        neg_us = [f32_tile(f"neg_us{c}", 1) for c in range(PACK)]
+        ts_cols = f32_tile("ts_cols", PACK)
+        ts_all = f32_tile("ts_all", L)
         neg_sc = f32_tile("neg_sc", PACK * L)
+        neg_sc_woven = f32_tile("neg_sc_woven", PACK * L)
         nc.vector.tensor_copy(ts_listed[:], ts_table[:].indirect(cell_list[:]))
-        for s in range(PACK):
-            nc.tensor.transpose(block(banks[0], s, P), us_rows[:, s:s + 1].to_broadcast([P, P]), ident[:])
-        nc.scalar.copy(us_all[:].rearrange("q (p s) -> q p s", s=PACK), banks[0][:].rearrange("q (s p) -> q p s", s=PACK))
-        for b in range(PACK):
-            nc.tensor.transpose(block(banks[6], b, P), block(ts_listed, b, P), ident[:])
-        nc.scalar.activation(neg_ts[:], banks[6][:, P - 1:L:P], ACT.Copy, scale=-1.0)
-        for b in range(PACK):
-            nc.tensor.transpose(block(banks[7], b, P), neg_ts[:, b:b + 1].to_broadcast([P, P]), ident[:])
-        for m in range(PACK):
-            nc.scalar.activation(neg_sc[:].rearrange("p (b m j) -> p b m j", b=PACK, m=PACK)[:, :, m, :],
-                                 banks[7][:].rearrange("p (b j) -> p b j", b=PACK), ACT.Copy, scale=us_rows[:, m:m + 1])
-        neg_sc_woven = f32_tile("neg_sc_woven", NEAR * L)
-        for b in range(NEAR):
-            nc.scalar.copy(block(neg_sc_woven, b).rearrange("p (j s) -> p j s", s=PACK), block(neg_sc, b).rearrange("p (s j) -> p j s", s=PACK))
+        for c in range(PACK):
+            nc.tensor.transpose(block(banks[0], c, P), block(us_table, c, P), ident[:])
+        for c in range(PACK):
+            nc.scalar.activation(neg_us[c][:], block(banks[0], c, P)[:, P - 1:P], ACT.Copy, scale=-1.0)
 
-        x_d = bf16_tile("x_d")
-        x_r = bf16_tile("x_r")
+        for c in range(PACK):
+            nc.tensor.transpose(block(banks[2], c, P), neg_us[c][:].to_broadcast([P, P]), ident[:])
         for t in range(PACK):
-            nc.vector.tensor_copy(x_d[:].rearrange("p (s m t) -> p m s t", s=PACK, t=PACK)[:, :, :, t], u_planes[t][:].indirect(gene_list[:]))
-            if t % 2 == 1:
-                turn_table(x_r, x_d, t // 2, banks[4 + t // 2], dealt=True)
+            nc.tensor.transpose(block(banks[1], t, P), ts_listed[:, t:L:PACK], ident[:])
+        nc.scalar.copy(ts_cols[:], banks[1][:, P - 1:L:P])
+        for t in range(PACK):
+            nc.tensor.transpose(block(banks[3], t, P), ts_cols[:, t:t + 1].to_broadcast([P, P]), ident[:])
+        nc.scalar.copy(ts_all[:], banks[3][:])
+        for t in range(PACK):
+            nc.scalar.activation(block(neg_sc, t), banks[2][:], ACT.Copy, scale=ts_cols[:, t:t + 1])
+        for c in range(PACK):
+            nc.scalar.copy(block(neg_sc_woven, c).rearrange("q (g t) -> q g t", t=PACK),
+                           neg_sc[:].rearrange("q (t c g) -> q c g t", t=PACK, c=PACK)[:, c])
 
-        hq_r = mx_tiles("hq_r", L // 2 + L)
-        nc.gpsimd.memset(hq_r[0][:, 0:L // 2], 0)
-        nc.gpsimd.memset(hq_r[1][:, 0:L // 2], 0)
-        cell_windows = [f32_tile(f"cell_window{k}", T) for k in range(3)] + [f32_tile("cell_window3", T, tag="u_plane0")]
-        gene_windows = [f32_tile("gene_window0", T, tag="u_plane1")]
-        nc.vector.memset(cell_windows[0][:].bitcast(I32), 0)
-        for window in cell_windows[1:] + gene_windows:
+        w_d = woven_tile("w_d")
+        w_i = woven_tile("w_i")
+        for t in range(PACK):
+            nc.vector.tensor_copy(w_d[:, t:L * PACK:PACK], v_planes[t][:].indirect(cell_list[:]))
+            if t % 2 == 1:
+                turn_table(w_i, w_d, t // 2, banks[4 + t // 2])
+
+        hq_i = mx_tiles("hq_i", HALF + L)
+        nc.gpsimd.memset(hq_i[0][:, 0:HALF], 0)
+        nc.gpsimd.memset(hq_i[1][:, 0:HALF], 0)
+        gene_windows = [f32_tile(f"gene_window{k}", T) for k in range(PACK - 1)] + [f32_tile("gene_window3", T, tag="v_plane0")]
+        nc.vector.memset(gene_windows[0][:].bitcast(I32), 0)
+        for window in gene_windows[1:]:
             nc.gpsimd.memset(window[:].bitcast(I32), 0)
 
-        w_d = bf16_tile("w_d")
-        w_i = bf16_tile("w_i")
-        xq_d = mx_tiles("xq_d")
-        xq_r = mx_tiles("xq_r", L + L // 2, tag="v_plane3")
+        x_d = woven_tile("x_d")
+        x_r = woven_tile("x_r")
         wq_d = mx_tiles("wq_d")
-        half = L // 2
-        quantize(xq_d, x_d, E4M3)
-        for t in range(2):
-            nc.vector.tensor_copy(w_d[:, t:L * PACK:PACK], v_planes[t][:].indirect(cell_list[:]))
-        turn_table(w_i, w_d, 0, banks[4])
-        nc.vector.tensor_copy(w_d[:, 2:L * PACK:PACK], v_planes[2][:].indirect(cell_list[:]))
-        for k in range(2):
-            nc.vector.tensor_copy(w_d[:, k * 1024 + 3:(k + 1) * 1024:PACK],
-                                  v_planes[3][:].indirect(cell_list[:, k * 16:(k + 1) * 16]))
-            for c0, c1 in (((0, P), (P, half)), ((half, L),))[k]:
-                quantize(wq_d, w_d, E4M3, c0, c1)
-        for b in range(PACK):
-            for m in range(PACK):
-                product(block(banks[b], m, P), xq_d, E4M3, m * P, wq_d, E4M3, b * P, (b + 1) * P)
+        quantize(wq_d, w_d, E4M3)
+        nc.vector.tensor_copy(x_d[:, 0:L * PACK:PACK], u_planes[0][:].indirect(gene_list[:]))
+        nc.vector.tensor_copy(x_d[:, 1:L * PACK:PACK], u_planes[1][:].indirect(gene_list[:]))
+        turn_table(x_r, x_d, 0, banks[6])
+        nc.vector.tensor_copy(x_d[:, 2:L * PACK:PACK], u_planes[2][:].indirect(gene_list[:]))
+        nc.vector.tensor_copy(x_d[:, PACK - 1:PAIR:PACK], u_planes[3][:].indirect(list_half(gene_list, 0)))
 
-        quantize(xq_r, x_r, E4M3)
-        wq_i = [(xq_r[0][:, L:L + half], xq_r[1][:, L:L + half]), mx_tiles("wq_i1", half)]
-        quantize(wq_i[0], w_i, E4M3, 0, half)
-
+        y_dealt = f32_tile("y_dealt", PACK * L, tag="neg_sc")
         neg_a = f32_tile("neg_a", PACK * L)
-        num = f32_tile("num", NEAR * L)
-        inv = f32_tile("inv", (PACK - NEAR) * L)
+        num = f32_tile("num", 2 * L)
+        inv = f32_tile("inv", 3 * L)
+        inv_second = f32_tile("inv_second", L)
+        invs = [inv_second[:]] + [block(inv, c) for c in range(3)]
         square = f32_tile("square", 2 * L)
-        root = f32_tile("root", PACK * L)
-        h_cells = bf16_tile("h_cells")
-        h_r = bf16_tile("h_r")
-        q_banks = banks[4:8]
-
-        neg_q = f32_tile("neg_q", NEAR * L)
-
-        def y_chunk(b):
-            return y_halves[b // 2][:].rearrange("p (s b j) -> p b s j", s=PACK, b=2)[:, b % 2]
+        root = f32_tile("root", 3 * L)
+        h_i = woven_tile("h_i")
+        score_banks = [banks[0], banks[1], banks[2], banks[3]]
+        q_banks = [banks[4], banks[5], banks[0], banks[2]]
 
         def woven(ap):
-            return ap.rearrange("p (j s) -> p j s", s=PACK)
+            return ap.rearrange("q (g t) -> q g t", t=PACK)
 
-        def scale_near(b):
-            nc.scalar.copy(woven(block(neg_q, b)), y_chunk(b).rearrange("p s j -> p j s"))
-            nc.vector.tensor_tensor(woven(block(neg_a, b)), banks[b][:].rearrange("p (s j) -> p j s", s=PACK),
-                                    woven(block(neg_sc_woven, b)), MULT)
+        def scores(c, xq_d):
+            product(score_banks[c][:], xq_d, E4M3, (c % 2) * P, wq_d, E4M3, 0, L)
 
-        def residual_near(b):
-            nc.vector.tensor_tensor(block(neg_q, b), block(neg_a, b), block(neg_q, b), ADD)
+        def deal_targets(c):
+            nc.scalar.copy(block(y_dealt, c).rearrange("p (t q) -> p q t", t=PACK), y_chunks[c][:].rearrange("p (q t) -> p q t", t=PACK))
 
-        def damping(b, first):
-            nc.scalar.activation(woven(block(square, b % 2)), first, ACT.Square)
-            nc.scalar.activation(block(root, b), block(square, b % 2), ACT.Abs_reciprocal_sqrt, bias=1.0)
-            if b >= NEAR:
-                nc.scalar.activation(block(inv, b - NEAR), block(root, b), ACT.Square)
+        def targets(c):
+            for t in range(PACK):
+                nc.tensor.matmul(block(q_banks[c], t, P), block(block(y_dealt, c), t, P), ident[:],
+                                 start=(t == 0), stop=False, is_transpose=True)
 
-        part = [f32_tile(f"part{b}", L) for b in range(NEAR)]
+        def scale(c):
+            nc.vector.scalar_tensor_tensor(block(neg_a, c).rearrange("p (t q) -> p t q", t=PACK),
+                                           score_banks[c][:].rearrange("p (q t) -> p t q", t=PACK), neg_us[c][:],
+                                           ts_all[:].rearrange("p (t q) -> p t q", t=PACK), MULT, MULT)
 
-        def weigh_near(b):
-            damping(b, woven(block(neg_q, b)))
-            nc.vector.tensor_tensor(part[b][:], block(num, b), block(root, b), MULT)
-            nc.vector.tensor_tensor(block(h_r, b), part[b][:], block(root, b), MULT)
+        def residual(c):
+            for t in range(PACK):
+                nc.tensor.matmul(block(q_banks[c], t, P), block(block(neg_a, c), t, P), ident[:],
+                                 start=False, stop=(t == PACK - 1), is_transpose=True)
 
-        def scale_far(b):
-            nc.vector.tensor_tensor(block(neg_a, b), banks[b][:], block(neg_sc, b), MULT)
-            for m in range(PACK):
-                nc.tensor.matmul(block(q_banks[b], m, P), y_chunk(b)[:, m, :], ident[:],
-                                 start=(m == 0), stop=False, is_transpose=True)
-            for m in range(PACK):
-                nc.tensor.matmul(block(q_banks[b], m, P), neg_a[:, b * L + m * P:b * L + (m + 1) * P], ident[:],
-                                 start=False, stop=(m == PACK - 1), is_transpose=True)
+        def neg_q(c):
+            return q_banks[c][:].rearrange("q (t g) -> q g t", t=PACK)
 
-        def weigh_far(b):
-            turned_q = q_banks[b][:].rearrange("j (s p) -> j p s", s=PACK)
-            far_num = part[1][:] if b == NEAR else block(root, 1)
-            damping(b, turned_q)
-            nc.vector.scalar_tensor_tensor(woven(far_num), turned_q, neg_ts[:, b:b + 1], woven(us_all[:]), MULT, MULT)
-            (nc.vector if b == NEAR else nc.gpsimd).tensor_tensor(block(h_cells, b), far_num, block(inv, b - NEAR), MULT)
-            words = block(h_cells[:].bitcast(F32), b, half)
-            for u in range(2):
-                nc.tensor.transpose(block(banks[b], u, P), words[:, u:half:2], ident[:])
-            nc.scalar.copy(block(h_r[:].bitcast(F32), b, half).rearrange("q (j u) -> q j u", u=2),
-                           banks[b][:, 0:half].rearrange("q (u j) -> q j u", u=2))
+        roots = [block(root, c) for c in range(3)] + [block(neg_sc_woven, 2)]
 
-        dv = [f32_tile(f"dv{t}", L // 2) for t in range(3)]
-        du = [f32_tile(f"du{t}", L) for t in range(PACK)]
+        def squares(c, sq):
+            nc.scalar.activation(woven(sq), neg_q(c), ACT.Square)
+
+        def inverse_root(c, sq):
+            nc.scalar.activation(roots[c], sq, ACT.Abs_reciprocal_sqrt, bias=1.0)
+
+        def damping(c, sq):
+            squares(c, sq)
+            inverse_root(c, sq)
+
+        def numerator(c, dst):
+            nc.vector.tensor_tensor(woven(dst), neg_q(c), woven(block(neg_sc_woven, c)), MULT)
+
+        def weigh(c, src, engine):
+            nc.scalar.activation(invs[c], roots[c], ACT.Square)
+            engine.tensor_tensor(block(h_i, c), src, invs[c], MULT)
+
+        du = [f32_tile(f"du{t}", HALF) for t in range(EARLY_PLANES)]
+        dv = [f32_tile(f"dv{t}", L) for t in range(PACK)]
         out_0_rows = out_0.rearrange("(p t) c -> p t c", t=PACK)
         out_1_rows = out_1.rearrange("(p t) c -> p t c", t=PACK)
 
-        def cell_half(t, k, bank, stage):
-            product(bank[:], xq_r, E4M3, t * P, hq_r, E5M2, k * half, k * half + L)
-            nc.scalar.copy(stage, bank[:, half:L])
-            nc.vector.tensor_copy(cell_windows[t][:].indirect(cell_list[:, k * 16:(k + 1) * 16]), stage)
+        def gene_half(t, k, bank, stage):
+            product(bank[:], wq_i, E4M3, t * P, hq_i, E5M2, k * HALF, k * HALF + L)
+            nc.scalar.copy(stage, bank[:, HALF:L])
+            nc.vector.tensor_copy(gene_windows[t][:].indirect(list_half(gene_list, k)), stage)
 
-        def place(window, offsets, bank, stage, rows):
-            nc.scalar.copy(stage, bank[:])
-            nc.vector.tensor_copy(window[:].indirect(offsets[:]), stage)
-            nc.sync.dma_start(rows, window[:])
+        def cell_plane(t, bank):
+            product(bank[:], xq_r[t // 2], E4M3, (t % 2) * P, hq_r, E5M2, 0, L)
+            nc.scalar.copy(dv[t][:], bank[:])
+            nc.vector.tensor_copy(cell_windows[t % 2][:].indirect(cell_list[:]), dv[t][:])
+            nc.sync.dma_start(out_0_rows[:, t, :], cell_windows[t % 2][:])
 
-        def gene_block(t, bank):
-            product(bank[:], wq_i[t // 2], E4M3, (t % 2) * P, hq_i, E5M2, 0, L)
-            place(gene_windows[t % 2], gene_list, bank, du[t][:], out_1_rows[:, t, :])
+        first, second = 1, 0
+        for c in (first, second, 2, 3):
+            deal_targets(c)
+        targets(first)
+        xq_d = mx_tiles("xq_d", HALF, tag=f"y_chunk{first}")
+        for c in (first, second):
+            quantize(xq_d, x_d, E4M3, c * P, (c + 1) * P)
+        lap = 2
+        nc.vector.tensor_copy(x_d[:, PACK * (HALF - 16 * lap) + PACK - 1:L * PACK:PACK],
+                              u_planes[3][:].indirect(gene_list[:, LIST_HALF - lap:2 * LIST_HALF]))
+        for c in (first, second):
+            scores(c, xq_d)
+        targets(second)
+        for c in (first, second):
+            scale(c)
+            residual(c)
+        xq_far = mx_tiles("xq_far", 2 * L, tag=f"neg_us{first}")
+        wq_i = (xq_far[0][:, L:2 * L], xq_far[1][:, L:2 * L])
+        xq_r = [(xq_far[0][:, HALF:L], xq_far[1][:, HALF:L]), mx_tiles("xq_r1", HALF)]
+        quantize(xq_far, x_d, E4M3, HALF, L, -HALF)
+        quantize(wq_i, w_i, E4M3)
+        quantize(xq_r[0], x_r, E4M3, 0, HALF)
+        for c in (2, 3):
+            scores(c, xq_far)
+        for c in (first, second):
+            squares(c, block(square, c))
+        for c in (first, second):
+            inverse_root(c, block(square, c))
+        numerator(first, block(num, first))
+        targets(2)
+        scale(2)
+        residual(2)
+        numerator(second, block(num, second))
+        targets(3)
+        scale(3)
+        residual(3)
+        for c in (first, second):
+            weigh(c, block(num, c), nc.vector)
+        for c in (first, second):
+            quantize(hq_i, h_i, E5M2, c * P, (c + 1) * P, HALF)
+        damping(2, block(square, 0))
+        squares(3, block(square, 1))
+        numerator(2, block(num, second))
+        numerator(3, inv_second[:])
+        weigh(2, block(num, second), nc.gpsimd)
+        gene_half(0, 0, banks[6], du[0][:])
+        inverse_root(3, block(square, 1))
+        gene_half(1, 0, banks[1], invs[first][:, 0:HALF])
+        weigh(3, inv_second[:], nc.gpsimd)
+        quantize(hq_i, h_i, E5M2, HALF, L, HALF)
+        gene_half(2, 0, banks[3], inv_second[:, 0:HALF])
+        cell_windows = [f32_tile(f"cell_window{k}", T, tag=tag) for k, tag in enumerate(("inv", "inv_second"))]
+        for window in cell_windows:
+            nc.gpsimd.memset(window[:].bitcast(I32), 0)
 
-        for b in range(NEAR):
-            scale_near(b)
-        for b in range(NEAR):
-            residual_near(b)
-        nc.gpsimd.tensor_tensor(num[:, 0:L], neg_q[:, 0:L], neg_sc_woven[:, 0:L], MULT)
-        for b in range(NEAR, PACK):
-            scale_far(b)
-        nc.vector.tensor_tensor(num[:, L:NEAR * L], neg_q[:, L:NEAR * L], neg_sc_woven[:, L:NEAR * L], MULT)
-        for b in range(NEAR):
-            weigh_near(b)
-        for b in range(NEAR):
-            quantize(hq_r, h_r, E5M2, b * P, (b + 1) * P, half)
-        weigh_far(2)
-        weigh_far(3)
-        cell_half(0, 0, banks[0], block(root, 3)[:, 0:half])
-        cell_half(1, 0, banks[1], block(root, 3)[:, half:L])
-        quantize(hq_r, h_r, E5M2, half, L, half)
-        cell_half(2, 0, banks[4], block(h_cells[:].bitcast(F32), 3, half))
-
-        gene_windows.append(f32_tile("gene_window1", T, tag="h_cells"))
-        nc.gpsimd.memset(gene_windows[1][:].bitcast(I32), 0)
-
-        h_i = bf16_tile("h_i")
-        hq_i = mx_tiles("hq_i")
-        for t in range(3):
-            cell_half(t, 1, banks[t], dv[t][:])
-            nc.sync.dma_start(out_0_rows[:, t, :], cell_windows[t][:])
+        h_r = woven_tile("h_r")
+        hq_r = mx_tiles("hq_r")
+        for t in range(EARLY_PLANES):
+            gene_half(t, 1, banks[t], du[t][:])
+            nc.sync.dma_start(out_1_rows[:, t, :], gene_windows[t][:])
         for u in range(2):
-            turned = turn(h_r[:].bitcast(F32), u, banks[u])
-            nc.scalar.copy(h_i[:].rearrange("q (p u e s) -> q u p e s", u=2, e=2, s=PACK)[:, u],
-                           turned.rearrange("q (s p e) -> q p e s", s=PACK, e=2))
-        quantize(hq_i, h_i, E5M2)
-        product(banks[3][:], xq_r, E4M3, 3 * P, hq_r, E5M2, half, half + L)
+            turned = turn(h_i, u, banks[u])
+            nc.scalar.copy(h_r[:].rearrange("p (q u e s) -> p u q e s", u=2, e=2, s=PACK)[:, u],
+                           turned.rearrange("p (s q e) -> p q e s", s=PACK, e=2))
+        quantize(hq_r, h_r, E5M2)
+
+        last = PACK - 1
+        product(banks[last][:], wq_i, E4M3, last * P, hq_i, E5M2, HALF, HALF + L)
 
         def last_plane_half(k, stage):
-            nc.scalar.copy(stage, block(banks[3], k, half))
-            nc.vector.tensor_copy(cell_windows[3][:].indirect(cell_list[:, k * 16:(k + 1) * 16]), stage)
+            nc.scalar.copy(stage, block(banks[last], k, HALF))
+            nc.vector.tensor_copy(gene_windows[last][:].indirect(list_half(gene_list, k)), stage)
 
-        last_plane_half(0, h_r[:].bitcast(F32)[:, 0:half])
-        turn_table(w_i, w_d, 1, banks[2])
-        quantize(wq_i[1], w_i, E4M3, half, L, -half)
-        gene_block(0, banks[4])
-        gene_block(1, banks[5])
-        last_plane_half(1, du[0][:, 0:half])
-        nc.sync.dma_start(out_0_rows[:, 3, :], cell_windows[3][:])
-        gene_block(2, banks[6])
-        gene_block(3, banks[7])
+        last_plane_half(0, h_i[:].bitcast(F32)[:, 0:HALF])
+        turn_table(x_r, x_d, 1, banks[2])
+        quantize(xq_r[1], x_r, E4M3, HALF, L, -HALF)
+        cell_plane(0, banks[4])
+        cell_plane(1, banks[5])
+        last_plane_half(1, dv[0][:, 0:HALF])
+        nc.sync.dma_start(out_1_rows[:, last, :], gene_windows[last][:])
+        cell_plane(2, banks[6])
+        cell_plane(3, banks[7])

@@ -76,8 +76,8 @@ def tile_attend_gmf_cau_vu_kernel(tc, uT, vT, y, us, ts, offs, uoffs, out_0, out
         y_chunks = [f32_tile(f"y_chunk{c}", L) for c in range(PACK)]
         uT_rows = uT.rearrange("(p t) c -> p t c", t=PACK)
         vT_rows = vT.rearrange("(p t) c -> p t c", t=PACK)
-        nc.sync.dma_start(v_planes[0][:], vT_rows[:, 0, :])
         nc.sync.dma_start(cell_list[:], offs)
+        nc.sync.dma_start(v_planes[0][:], vT_rows[:, 0, :])
         nc.sync.dma_start(gene_list[:], uoffs)
         nc.sync.dma_start(v_planes[1][:], vT_rows[:, 1, :])
         nc.scalar.dma_start(ts_table[P - 1:P, :], ts[0:1, :])
@@ -138,9 +138,9 @@ def tile_attend_gmf_cau_vu_kernel(tc, uT, vT, y, us, ts, offs, uoffs, out_0, out
                 turn_table(w_i, w_d, t // 2, banks[4 + t // 2])
 
         hq_i = mx_tiles("hq_i", HALF + L)
-        nc.gpsimd.memset(hq_i[0][:, 0:HALF], 0)
-        nc.gpsimd.memset(hq_i[1][:, 0:HALF], 0)
-        gene_windows = [f32_tile(f"gene_window{k}", T) for k in range(PACK - 1)] + [f32_tile("gene_window3", T, tag="v_plane0")]
+        nc.vector.memset(hq_i[0][:, 0:HALF], 0)
+        nc.vector.memset(hq_i[1][:, 0:HALF].bitcast(U32), 0)
+        gene_windows = [f32_tile(f"gene_window{k}", T, tag=tag) for k, tag in enumerate((None, "ts_table", "v_plane0", "v_plane1"))]
         nc.vector.memset(gene_windows[0][:].bitcast(I32), 0)
         for window in gene_windows[1:]:
             nc.gpsimd.memset(window[:].bitcast(I32), 0)
@@ -173,8 +173,9 @@ def tile_attend_gmf_cau_vu_kernel(tc, uT, vT, y, us, ts, offs, uoffs, out_0, out
         def scores(c, xq_d):
             product(score_banks[c][:], xq_d, E4M3, (c % 2) * P, wq_d, E4M3, 0, L)
 
-        def deal_targets(c):
-            nc.scalar.copy(block(y_dealt, c).rearrange("p (t q) -> p q t", t=PACK), y_chunks[c][:].rearrange("p (q t) -> p q t", t=PACK))
+        def deal_targets(c, t0=0, t1=PACK):
+            nc.scalar.copy(block(y_dealt, c).rearrange("p (t q) -> p q t", t=PACK)[:, :, t0:t1],
+                           y_chunks[c][:].rearrange("p (q t) -> p q t", t=PACK)[:, :, t0:t1])
 
         def targets(c):
             for t in range(PACK):
@@ -230,7 +231,9 @@ def tile_attend_gmf_cau_vu_kernel(tc, uT, vT, y, us, ts, offs, uoffs, out_0, out
             nc.sync.dma_start(out_0_rows[:, t, :], cell_windows[t % 2][:])
 
         first, second = 1, 0
-        for c in (first, second, 2, 3):
+        deal_targets(first, 0, 2)
+        deal_targets(first, 2, PACK)
+        for c in (second, 2, 3):
             deal_targets(c)
         targets(first)
         xq_d = mx_tiles("xq_d", HALF, tag=f"y_chunk{first}")

@@ -45,9 +45,9 @@ def tile_attend_gmf_cau_vu_kernel(tc, uT, vT, y, us, ts, offs, uoffs, out_0, out
         def woven_tile(name):
             return sb.tile([P, L * PACK], BF16, name=name, align_bytes=64)
 
-        def mx_tiles(name, width=L, tag=None):
+        def mx_tiles(name, width=L, tag=None, scale_tag=None):
             return (sb.tile([P, width], U32, name=name + "_codes", tag=tag or name + "_codes", align_bytes=64),
-                    sb.tile([P, width], U8, name=name + "_scales", align_bytes=64))
+                    sb.tile([P, width], U8, name=name + "_scales", tag=scale_tag or name + "_scales", align_bytes=64))
 
         def quantize(dst, src, fmt, c0=0, c1=L, shift=0):
             nc.vector.quantize_mx(out=dst[0][:, shift + c0:shift + c1].bitcast(fmt), scales=dst[1][:, shift + c0:shift + c1],
@@ -137,20 +137,24 @@ def tile_attend_gmf_cau_vu_kernel(tc, uT, vT, y, us, ts, offs, uoffs, out_0, out
             if t % 2 == 1:
                 turn_table(w_i, w_d, t // 2, banks[4 + t // 2])
 
-        hq_i = mx_tiles("hq_i", HALF + L)
-        nc.vector.memset(hq_i[0][:, 0:HALF], 0)
-        nc.vector.memset(hq_i[1][:, 0:HALF].bitcast(U32), 0)
-        gene_windows = [f32_tile(f"gene_window{k}", T, tag=tag) for k, tag in enumerate((None, "ts_table", "v_plane0", "v_plane1"))]
-        nc.vector.memset(gene_windows[0][:].bitcast(I32), 0)
-        for window in gene_windows[1:]:
+        hq_i = mx_tiles("hq_i", HALF + L, tag="v_plane2", scale_tag="v_plane3")
+        gene_windows = [f32_tile(f"gene_window{k}", T, tag=tag) for k, tag in enumerate(("ts_table", "v_plane0", "v_plane1"))]
+        for window in gene_windows:
             nc.gpsimd.memset(window[:].bitcast(I32), 0)
+        nc.gpsimd.memset(hq_i[0][:, 0:HALF], 0)
+        nc.gpsimd.memset(hq_i[1][:, 0:HALF].bitcast(U32), 0)
 
         x_d = woven_tile("x_d")
         x_r = woven_tile("x_r")
-        wq_d = mx_tiles("wq_d")
-        quantize(wq_d, w_d, E4M3)
+        w_dealt = woven_tile("w_dealt")
+        nc.scalar.copy(w_dealt[:].bitcast(U32).rearrange("p (s q u) -> p s q u", s=PACK, u=2),
+                       w_d[:].bitcast(U32).rearrange("p (q s u) -> p s q u", s=PACK, u=2))
         nc.vector.tensor_copy(x_d[:, 0:L * PACK:PACK], u_planes[0][:].indirect(gene_list[:]))
+        wq_d = mx_tiles("wq_d", tag="u_plane0")
+        quantize(wq_d, w_dealt, E4M3)
         nc.vector.tensor_copy(x_d[:, 1:L * PACK:PACK], u_planes[1][:].indirect(gene_list[:]))
+        gene_windows.append(f32_tile("gene_window3", T, tag="u_plane1"))
+        nc.gpsimd.memset(gene_windows[3][:].bitcast(I32), 0)
         turn_table(x_r, x_d, 0, banks[6])
         nc.vector.tensor_copy(x_d[:, 2:L * PACK:PACK], u_planes[2][:].indirect(gene_list[:]))
         nc.vector.tensor_copy(x_d[:, PACK - 1:PAIR:PACK], u_planes[3][:].indirect(list_half(gene_list, 0)))
@@ -183,9 +187,7 @@ def tile_attend_gmf_cau_vu_kernel(tc, uT, vT, y, us, ts, offs, uoffs, out_0, out
                                  start=(t == 0), stop=False, is_transpose=True)
 
         def scale(c):
-            nc.vector.scalar_tensor_tensor(block(neg_a, c).rearrange("p (t q) -> p t q", t=PACK),
-                                           score_banks[c][:].rearrange("p (q t) -> p t q", t=PACK), neg_us[c][:],
-                                           ts_all[:].rearrange("p (t q) -> p t q", t=PACK), MULT, MULT)
+            nc.vector.scalar_tensor_tensor(block(neg_a, c), score_banks[c][:], neg_us[c][:], ts_all[:], MULT, MULT)
 
         def residual(c):
             for t in range(PACK):

@@ -137,8 +137,8 @@ def tile_attend_gmf_cau_vu_kernel(tc, uT, vT, y, us, ts, offs, uoffs, out_0, out
             if t % 2 == 1:
                 turn_table(w_i, w_d, t // 2, banks[4 + t // 2])
 
-        hq_i = mx_tiles("hq_i", HALF + L, tag="v_plane2", scale_tag="v_plane3")
-        gene_windows = [f32_tile(f"gene_window{k}", T, tag=tag) for k, tag in enumerate(("ts_table", "v_plane0", "v_plane1"))]
+        hq_i = mx_tiles("hq_i", HALF + L, tag="v_plane3", scale_tag="warm")
+        gene_windows = [f32_tile(f"gene_window{k}", T, tag=tag) for k, tag in enumerate(("ts_table", "v_plane0", "v_plane1", "v_plane2"))]
         for window in gene_windows:
             nc.gpsimd.memset(window[:].bitcast(I32), 0)
         nc.gpsimd.memset(hq_i[0][:, 0:HALF], 0)
@@ -153,8 +153,8 @@ def tile_attend_gmf_cau_vu_kernel(tc, uT, vT, y, us, ts, offs, uoffs, out_0, out
         wq_d = mx_tiles("wq_d", tag="u_plane0")
         quantize(wq_d, w_dealt, E4M3)
         nc.vector.tensor_copy(x_d[:, 1:L * PACK:PACK], u_planes[1][:].indirect(gene_list[:]))
-        gene_windows.append(f32_tile("gene_window3", T, tag="u_plane1"))
-        nc.gpsimd.memset(gene_windows[3][:].bitcast(I32), 0)
+        cell_windows = [f32_tile("cell_window0", T, tag="u_plane1")]
+        nc.gpsimd.memset(cell_windows[0][:].bitcast(I32), 0)
         turn_table(x_r, x_d, 0, banks[6])
         nc.vector.tensor_copy(x_d[:, 2:L * PACK:PACK], u_planes[2][:].indirect(gene_list[:]))
         nc.vector.tensor_copy(x_d[:, PACK - 1:PAIR:PACK], u_planes[3][:].indirect(list_half(gene_list, 0)))
@@ -229,8 +229,8 @@ def tile_attend_gmf_cau_vu_kernel(tc, uT, vT, y, us, ts, offs, uoffs, out_0, out
         def cell_plane(t, bank):
             product(bank[:], xq_r[t // 2], E4M3, (t % 2) * P, hq_r, E5M2, 0, L)
             nc.scalar.copy(dv[t][:], bank[:])
-            nc.vector.tensor_copy(cell_windows[t % 2][:].indirect(cell_list[:]), dv[t][:])
-            nc.sync.dma_start(out_0_rows[:, t, :], cell_windows[t % 2][:])
+            nc.vector.tensor_copy(cell_windows[t % 3][:].indirect(cell_list[:]), dv[t][:])
+            nc.sync.dma_start(out_0_rows[:, t, :], cell_windows[t % 3][:])
 
         first, second = 1, 0
         deal_targets(first, 0, 2)
@@ -252,7 +252,7 @@ def tile_attend_gmf_cau_vu_kernel(tc, uT, vT, y, us, ts, offs, uoffs, out_0, out
             residual(c)
         xq_far = mx_tiles("xq_far", 2 * L, tag=f"neg_us{first}")
         wq_i = (xq_far[0][:, L:2 * L], xq_far[1][:, L:2 * L])
-        xq_r = [(xq_far[0][:, HALF:L], xq_far[1][:, HALF:L]), mx_tiles("xq_r1", HALF)]
+        xq_r = [(xq_far[0][:, HALF:L], xq_far[1][:, HALF:L])]
         quantize(xq_far, x_d, E4M3, HALF, L, -HALF)
         quantize(wq_i, w_i, E4M3)
         quantize(xq_r[0], x_r, E4M3, 0, HALF)
@@ -281,13 +281,13 @@ def tile_attend_gmf_cau_vu_kernel(tc, uT, vT, y, us, ts, offs, uoffs, out_0, out
         weigh(2, block(num, second), nc.gpsimd)
         gene_half(0, 0, banks[6], du[0][:])
         inverse_root(3, block(square, 1))
-        gene_half(1, 0, banks[1], invs[first][:, 0:HALF])
+        gene_half(1, 0, banks[1], du[1][:])
         weigh(3, inv_second[:], nc.gpsimd)
+        turn_table(x_r, x_d, 1, banks[2])
         quantize(hq_i, h_i, E5M2, HALF, L, HALF)
+        xq_r.append(mx_tiles("xq_r1", HALF, tag="inv"))
+        quantize(xq_r[1], x_r, E4M3, HALF, L, -HALF)
         gene_half(2, 0, banks[3], inv_second[:, 0:HALF])
-        cell_windows = [f32_tile(f"cell_window{k}", T, tag=tag) for k, tag in enumerate(("inv", "inv_second"))]
-        for window in cell_windows:
-            nc.gpsimd.memset(window[:].bitcast(I32), 0)
 
         h_r = woven_tile("h_r")
         hq_r = mx_tiles("hq_r")
@@ -303,16 +303,14 @@ def tile_attend_gmf_cau_vu_kernel(tc, uT, vT, y, us, ts, offs, uoffs, out_0, out
         last = PACK - 1
         product(banks[last][:], wq_i, E4M3, last * P, hq_i, E5M2, HALF, HALF + L)
 
-        def last_plane_half(k, stage):
-            nc.scalar.copy(stage, block(banks[last], k, HALF))
-            nc.vector.tensor_copy(gene_windows[last][:].indirect(list_half(gene_list, k)), stage)
-
-        last_plane_half(0, h_i[:].bitcast(F32)[:, 0:HALF])
-        turn_table(x_r, x_d, 1, banks[2])
-        quantize(xq_r[1], x_r, E4M3, HALF, L, -HALF)
+        stage = h_i[:].bitcast(F32)[:, 0:L]
+        nc.scalar.copy(stage, banks[last][:])
+        nc.vector.tensor_copy(gene_windows[last][:].indirect(gene_list[:]), stage)
+        nc.sync.dma_start(out_1_rows[:, last, :], gene_windows[last][:])
+        for k, tag in ((1, "h_r"), (2, "h_i")):
+            cell_windows.append(f32_tile(f"cell_window{k}", T, tag=tag))
+            nc.gpsimd.memset(cell_windows[k][:].bitcast(I32), 0)
         cell_plane(0, banks[4])
         cell_plane(1, banks[5])
-        last_plane_half(1, dv[0][:, 0:HALF])
-        nc.sync.dma_start(out_1_rows[:, last, :], gene_windows[last][:])
         cell_plane(2, banks[6])
         cell_plane(3, banks[7])

@@ -160,7 +160,8 @@ def tile_attend_gmf_cau_vu_kernel(tc, uT, vT, y, us, ts, offs, uoffs, out_0, out
         nc.vector.tensor_copy(x_d[:, PACK - 1:PAIR:PACK], u_planes[3][:].indirect(list_half(gene_list, 0)))
 
         y_dealt = f32_tile("y_dealt", PACK * L, tag="neg_sc")
-        neg_a = f32_tile("neg_a", PACK * L)
+        neg_a = f32_tile("neg_a", 3 * L)
+        scaled = [block(neg_a, 0), block(neg_a, 1), block(neg_sc_woven, 1), block(neg_sc_woven, 0)]
         num = f32_tile("num", 2 * L)
         inv = f32_tile("inv", 3 * L)
         inv_second = f32_tile("inv_second", L)
@@ -181,17 +182,17 @@ def tile_attend_gmf_cau_vu_kernel(tc, uT, vT, y, us, ts, offs, uoffs, out_0, out
             nc.scalar.copy(block(y_dealt, c).rearrange("p (t q) -> p q t", t=PACK)[:, :, t0:t1],
                            y_chunks[c][:].rearrange("p (q t) -> p q t", t=PACK)[:, :, t0:t1])
 
-        def targets(c):
-            for t in range(PACK):
+        def targets(c, t0=0):
+            for t in range(t0, PACK):
                 nc.tensor.matmul(block(q_banks[c], t, P), block(block(y_dealt, c), t, P), ident[:],
                                  start=(t == 0), stop=False, is_transpose=True)
 
         def scale(c):
-            nc.vector.scalar_tensor_tensor(block(neg_a, c), score_banks[c][:], neg_us[c][:], ts_all[:], MULT, MULT)
+            nc.vector.scalar_tensor_tensor(scaled[c], score_banks[c][:], neg_us[c][:], ts_all[:], MULT, MULT)
 
         def residual(c):
             for t in range(PACK):
-                nc.tensor.matmul(block(q_banks[c], t, P), block(block(neg_a, c), t, P), ident[:],
+                nc.tensor.matmul(block(q_banks[c], t, P), block(scaled[c], t, P), ident[:],
                                  start=False, stop=(t == PACK - 1), is_transpose=True)
 
         def neg_q(c):
@@ -233,12 +234,14 @@ def tile_attend_gmf_cau_vu_kernel(tc, uT, vT, y, us, ts, offs, uoffs, out_0, out
             nc.sync.dma_start(out_0_rows[:, t, :], cell_windows[t % 3][:])
 
         first, second = 1, 0
-        deal_targets(first, 0, 2)
-        deal_targets(first, 2, PACK)
+        direct = 3
+        for t in range(direct):
+            nc.tensor.matmul(block(q_banks[first], t, P), y_chunks[first][:, t:L:PACK], ident[:],
+                             start=(t == 0), stop=False, is_transpose=True)
+        deal_targets(first, direct, PACK)
         for c in (second, 2, 3):
             deal_targets(c)
-        targets(first)
-        xq_d = mx_tiles("xq_d", HALF, tag=f"y_chunk{first}")
+        xq_d = mx_tiles("xq_d", HALF)
         for c in (first, second):
             quantize(xq_d, x_d, E4M3, c * P, (c + 1) * P)
         lap = 2
@@ -246,6 +249,7 @@ def tile_attend_gmf_cau_vu_kernel(tc, uT, vT, y, us, ts, offs, uoffs, out_0, out
                               u_planes[3][:].indirect(gene_list[:, LIST_HALF - lap:2 * LIST_HALF]))
         for c in (first, second):
             scores(c, xq_d)
+        targets(first, direct)
         targets(second)
         for c in (first, second):
             scale(c)
@@ -263,10 +267,10 @@ def tile_attend_gmf_cau_vu_kernel(tc, uT, vT, y, us, ts, offs, uoffs, out_0, out
         for c in (first, second):
             inverse_root(c, block(square, c))
         numerator(first, block(num, first))
+        numerator(second, block(num, second))
         targets(2)
         scale(2)
         residual(2)
-        numerator(second, block(num, second))
         targets(3)
         scale(3)
         residual(3)

@@ -131,14 +131,14 @@ def tile_attend_gmf_cau_vu_kernel(tc, uT, vT, y, us, ts, offs, uoffs, out_0, out
                            neg_sc[:].rearrange("q (t c g) -> q c g t", t=PACK, c=PACK)[:, c])
 
         w_d = woven_tile("w_d")
-        w_i = woven_tile("w_i")
+        w_i = sb.tile([P, L * PACK], BF16, name="w_i", tag="neg_sc", align_bytes=64)
         for t in range(PACK):
             nc.vector.tensor_copy(w_d[:, t:L * PACK:PACK], v_planes[t][:].indirect(cell_list[:]))
             if t % 2 == 1:
-                turn_table(w_i, w_d, t // 2, banks[4 + t // 2])
+                turn_table(w_i, w_d, t // 2, banks[3 + t // 2])
 
-        hq_i = mx_tiles("hq_i", HALF + L, tag="v_plane3", scale_tag="warm")
-        gene_windows = [f32_tile(f"gene_window{k}", T, tag=tag) for k, tag in enumerate(("ts_table", "v_plane0", "v_plane1", "v_plane2"))]
+        hq_i = mx_tiles("hq_i", HALF + L, tag="v_plane2", scale_tag="warm")
+        gene_windows = [f32_tile(f"gene_window{k}", T, tag=tag) for k, tag in enumerate(("ts_table", "v_plane0", "v_plane1"))]
         for window in gene_windows:
             nc.gpsimd.memset(window[:].bitcast(I32), 0)
         nc.gpsimd.memset(hq_i[0][:, 0:HALF], 0)
@@ -146,20 +146,17 @@ def tile_attend_gmf_cau_vu_kernel(tc, uT, vT, y, us, ts, offs, uoffs, out_0, out
 
         x_d = woven_tile("x_d")
         x_r = woven_tile("x_r")
-        w_dealt = woven_tile("w_dealt")
-        nc.scalar.copy(w_dealt[:].bitcast(U32).rearrange("p (s q u) -> p s q u", s=PACK, u=2),
-                       w_d[:].bitcast(U32).rearrange("p (q s u) -> p s q u", s=PACK, u=2))
+        wq_d = mx_tiles("wq_d")
+        quantize(wq_d, w_d, E4M3)
         nc.vector.tensor_copy(x_d[:, 0:L * PACK:PACK], u_planes[0][:].indirect(gene_list[:]))
-        wq_d = mx_tiles("wq_d", tag="u_plane0")
-        quantize(wq_d, w_dealt, E4M3)
+        wq_i = mx_tiles("wq_i", tag="u_plane0")
+        quantize(wq_i, w_i, E4M3)
         nc.vector.tensor_copy(x_d[:, 1:L * PACK:PACK], u_planes[1][:].indirect(gene_list[:]))
-        cell_windows = [f32_tile("cell_window0", T, tag="u_plane1")]
-        nc.gpsimd.memset(cell_windows[0][:].bitcast(I32), 0)
         turn_table(x_r, x_d, 0, banks[6])
         nc.vector.tensor_copy(x_d[:, 2:L * PACK:PACK], u_planes[2][:].indirect(gene_list[:]))
         nc.vector.tensor_copy(x_d[:, PACK - 1:PAIR:PACK], u_planes[3][:].indirect(list_half(gene_list, 0)))
 
-        y_dealt = f32_tile("y_dealt", PACK * L, tag="neg_sc")
+        y_dealt = f32_tile("y_dealt", PACK * L)
         neg_a = f32_tile("neg_a", 3 * L)
         scaled = [block(neg_a, 0), block(neg_a, 1), block(neg_sc_woven, 1), block(neg_sc_woven, 0)]
         num = f32_tile("num", 2 * L)
@@ -188,7 +185,9 @@ def tile_attend_gmf_cau_vu_kernel(tc, uT, vT, y, us, ts, offs, uoffs, out_0, out
                                  start=(t == 0), stop=False, is_transpose=True)
 
         def scale(c):
-            nc.vector.scalar_tensor_tensor(scaled[c], score_banks[c][:], neg_us[c][:], ts_all[:], MULT, MULT)
+            nc.vector.scalar_tensor_tensor(scaled[c].rearrange("p (t q) -> p t q", t=PACK),
+                                           score_banks[c][:].rearrange("p (q t) -> p t q", t=PACK), neg_us[c][:],
+                                           ts_all[:].rearrange("p (t q) -> p t q", t=PACK), MULT, MULT)
 
         def residual(c):
             for t in range(PACK):
@@ -213,9 +212,11 @@ def tile_attend_gmf_cau_vu_kernel(tc, uT, vT, y, us, ts, offs, uoffs, out_0, out
         def numerator(c, dst):
             nc.vector.tensor_tensor(woven(dst), neg_q(c), woven(block(neg_sc_woven, c)), MULT)
 
-        def weigh(c, src, engine):
-            nc.scalar.activation(invs[c], roots[c], ACT.Square)
-            engine.tensor_tensor(block(h_i, c), src, invs[c], MULT)
+        def weigh(c, src, engine, parts=1):
+            for k in range(parts):
+                cols = slice(k * L // parts, (k + 1) * L // parts)
+                nc.scalar.activation(invs[c][:, cols], roots[c][:, cols], ACT.Square)
+                engine.tensor_tensor(block(h_i, c)[:, cols], src[:, cols], invs[c][:, cols], MULT)
 
         du = [f32_tile(f"du{t}", HALF) for t in range(EARLY_PLANES)]
         dv = [f32_tile(f"dv{t}", L) for t in range(PACK)]
@@ -254,11 +255,9 @@ def tile_attend_gmf_cau_vu_kernel(tc, uT, vT, y, us, ts, offs, uoffs, out_0, out
         for c in (first, second):
             scale(c)
             residual(c)
-        xq_far = mx_tiles("xq_far", 2 * L, tag=f"neg_us{first}")
-        wq_i = (xq_far[0][:, L:2 * L], xq_far[1][:, L:2 * L])
+        xq_far = mx_tiles("xq_far", L, tag=f"neg_us{first}")
         xq_r = [(xq_far[0][:, HALF:L], xq_far[1][:, HALF:L])]
         quantize(xq_far, x_d, E4M3, HALF, L, -HALF)
-        quantize(wq_i, w_i, E4M3)
         quantize(xq_r[0], x_r, E4M3, 0, HALF)
         for c in (2, 3):
             scores(c, xq_far)
@@ -274,8 +273,8 @@ def tile_attend_gmf_cau_vu_kernel(tc, uT, vT, y, us, ts, offs, uoffs, out_0, out
         targets(3)
         scale(3)
         residual(3)
-        for c in (first, second):
-            weigh(c, block(num, c), nc.vector)
+        weigh(first, block(num, first), nc.vector)
+        weigh(second, block(num, second), nc.vector, 2)
         for c in (first, second):
             quantize(hq_i, h_i, E5M2, c * P, (c + 1) * P, HALF)
         damping(2, block(square, 0))
@@ -286,11 +285,13 @@ def tile_attend_gmf_cau_vu_kernel(tc, uT, vT, y, us, ts, offs, uoffs, out_0, out
         gene_half(0, 0, banks[6], du[0][:])
         inverse_root(3, block(square, 1))
         gene_half(1, 0, banks[1], du[1][:])
-        weigh(3, inv_second[:], nc.gpsimd)
+        weigh(3, inv_second[:], nc.gpsimd, 2)
         turn_table(x_r, x_d, 1, banks[2])
         quantize(hq_i, h_i, E5M2, HALF, L, HALF)
         xq_r.append(mx_tiles("xq_r1", HALF, tag="inv"))
         quantize(xq_r[1], x_r, E4M3, HALF, L, -HALF)
+        gene_windows.append(f32_tile("gene_window3", T, tag="x_r"))
+        nc.gpsimd.memset(gene_windows[3][:].bitcast(I32), 0)
         gene_half(2, 0, banks[3], inv_second[:, 0:HALF])
 
         h_r = woven_tile("h_r")
@@ -311,10 +312,16 @@ def tile_attend_gmf_cau_vu_kernel(tc, uT, vT, y, us, ts, offs, uoffs, out_0, out
         nc.scalar.copy(stage, banks[last][:])
         nc.vector.tensor_copy(gene_windows[last][:].indirect(gene_list[:]), stage)
         nc.sync.dma_start(out_1_rows[:, last, :], gene_windows[last][:])
-        for k, tag in ((1, "h_r"), (2, "h_i")):
-            cell_windows.append(f32_tile(f"cell_window{k}", T, tag=tag))
-            nc.gpsimd.memset(cell_windows[k][:].bitcast(I32), 0)
+        cell_windows = []
+
+        def cell_window(tag):
+            cell_windows.append(f32_tile(f"cell_window{len(cell_windows)}", T, tag=tag))
+            nc.gpsimd.memset(cell_windows[-1][:].bitcast(I32), 0)
+
+        cell_window("h_r")
+        cell_window("h_i")
         cell_plane(0, banks[4])
+        cell_window("dv0")
         cell_plane(1, banks[5])
         cell_plane(2, banks[6])
         cell_plane(3, banks[7])

@@ -13,7 +13,6 @@ E4M3 = mybir.dt.float8_e4m3fn_x4
 E5M2 = mybir.dt.float8_e5m2_x4
 ACT = mybir.ActivationFunctionType
 MULT = mybir.AluOpType.mult
-ADD = mybir.AluOpType.add
 
 P = 128
 PACK = 4
@@ -22,8 +21,12 @@ HALF = L // 2
 T = 2048
 LIST_HALF = HALF // 16
 PAIR = 2 * L
-GENE_MAJOR = 2
+LAST = PACK - 1
+FIRST, SECOND = 1, 0
+LAP = 2
+DIRECT = 3
 EARLY_PLANES = 3
+CELL_WINDOWS = 3
 FLOPS = 3 * 2 * L * L * L
 BYTES = 4 * (4 * L * T + L * L + L + T) + 2 * 2 * P * 32
 
@@ -42,20 +45,20 @@ def tile_attend_gmf_cau_vu_kernel(tc, uT, vT, y, us, ts, offs, uoffs, out_0, out
         def f32_tile(name, width, tag=None):
             return sb.tile([P, width], F32, name=name, tag=tag or name, align_bytes=64)
 
-        def woven_tile(name):
-            return sb.tile([P, L * PACK], BF16, name=name, align_bytes=64)
+        def woven_tile(name, tag=None):
+            return sb.tile([P, L * PACK], BF16, name=name, tag=tag or name, align_bytes=64)
 
         def mx_tiles(name, width=L, tag=None, scale_tag=None):
             return (sb.tile([P, width], U32, name=name + "_codes", tag=tag or name + "_codes", align_bytes=64),
                     sb.tile([P, width], U8, name=name + "_scales", tag=scale_tag or name + "_scales", align_bytes=64))
 
         def quantize(dst, src, fmt, c0=0, c1=L, shift=0):
-            nc.vector.quantize_mx(out=dst[0][:, shift + c0:shift + c1].bitcast(fmt), scales=dst[1][:, shift + c0:shift + c1],
-                                  in_=src[:, PACK * c0:PACK * c1])
+            nc.vector.quantize_mx(out=dst[0][:, shift + c0:shift + c1].bitcast(fmt),
+                                  scales=dst[1][:, shift + c0:shift + c1], in_=src[:, PACK * c0:PACK * c1])
 
-        def product(out, lhs, lhs_fmt, m0, rhs, rhs_fmt, n0, n1):
-            nc.tensor.matmul_mx(out=out, lhsT=lhs[0][:, m0:m0 + P].bitcast(lhs_fmt), lhsT_scale=lhs[1][:, m0:m0 + P],
-                                rhs=rhs[0][:, n0:n1].bitcast(rhs_fmt), rhs_scale=rhs[1][:, n0:n1],
+        def product(out, lhs, m0, rhs, rhs_fmt, n0):
+            nc.tensor.matmul_mx(out=out, lhsT=lhs[0][:, m0:m0 + P].bitcast(E4M3), lhsT_scale=lhs[1][:, m0:m0 + P],
+                                rhs=rhs[0][:, n0:n0 + L].bitcast(rhs_fmt), rhs_scale=rhs[1][:, n0:n0 + L],
                                 start=True, stop=True)
 
         def block(tile_, b, width=L):
@@ -87,7 +90,7 @@ def tile_attend_gmf_cau_vu_kernel(tc, uT, vT, y, us, ts, offs, uoffs, out_0, out
         for t in range(PACK):
             nc.sync.dma_start(u_planes[t][:], uT_rows[:, t, :])
         y_rows = y.rearrange("b (c p) i -> p (b c) i", p=P)
-        for c in (1, 0, 2, 3):
+        for c in (FIRST, SECOND, 2, LAST):
             nc.sync.dma_start(y_chunks[c][:], y_rows[:, c, :])
 
         warm = f32_tile("warm", 8)
@@ -115,7 +118,6 @@ def tile_attend_gmf_cau_vu_kernel(tc, uT, vT, y, us, ts, offs, uoffs, out_0, out
             nc.tensor.transpose(block(banks[0], c, P), block(us_table, c, P), ident[:])
         for c in range(PACK):
             nc.scalar.activation(neg_us[c][:], block(banks[0], c, P)[:, P - 1:P], ACT.Copy, scale=-1.0)
-
         for c in range(PACK):
             nc.tensor.transpose(block(banks[2], c, P), neg_us[c][:].to_broadcast([P, P]), ident[:])
         for t in range(PACK):
@@ -131,14 +133,15 @@ def tile_attend_gmf_cau_vu_kernel(tc, uT, vT, y, us, ts, offs, uoffs, out_0, out
                            neg_sc[:].rearrange("q (t c g) -> q c g t", t=PACK, c=PACK)[:, c])
 
         w_d = woven_tile("w_d")
-        w_i = sb.tile([P, L * PACK], BF16, name="w_i", tag="neg_sc", align_bytes=64)
+        w_i = woven_tile("w_i", tag="neg_sc")
         for t in range(PACK):
             nc.vector.tensor_copy(w_d[:, t:L * PACK:PACK], v_planes[t][:].indirect(cell_list[:]))
             if t % 2 == 1:
                 turn_table(w_i, w_d, t // 2, banks[3 + t // 2])
 
         hq_i = mx_tiles("hq_i", HALF + L, tag="v_plane2", scale_tag="warm")
-        gene_windows = [f32_tile(f"gene_window{k}", T, tag=tag) for k, tag in enumerate(("ts_table", "v_plane0", "v_plane1"))]
+        gene_windows = [f32_tile(f"gene_window{t}", T, tag=tag)
+                        for t, tag in enumerate(("ts_table", "v_plane0", "v_plane1"))]
         for window in gene_windows:
             nc.gpsimd.memset(window[:].bitcast(I32), 0)
         nc.gpsimd.memset(hq_i[0][:, 0:HALF], 0)
@@ -154,30 +157,30 @@ def tile_attend_gmf_cau_vu_kernel(tc, uT, vT, y, us, ts, offs, uoffs, out_0, out
         nc.vector.tensor_copy(x_d[:, 1:L * PACK:PACK], u_planes[1][:].indirect(gene_list[:]))
         turn_table(x_r, x_d, 0, banks[6])
         nc.vector.tensor_copy(x_d[:, 2:L * PACK:PACK], u_planes[2][:].indirect(gene_list[:]))
-        nc.vector.tensor_copy(x_d[:, PACK - 1:PAIR:PACK], u_planes[3][:].indirect(list_half(gene_list, 0)))
+        nc.vector.tensor_copy(x_d[:, LAST:PAIR:PACK], u_planes[LAST][:].indirect(list_half(gene_list, 0)))
 
         y_dealt = f32_tile("y_dealt", PACK * L)
-        neg_a = f32_tile("neg_a", 3 * L)
-        scaled = [block(neg_a, 0), block(neg_a, 1), block(neg_sc_woven, 1), block(neg_sc_woven, 0)]
+        neg_a = f32_tile("neg_a", 2 * L)
+        scaled = [block(neg_a, 0), block(neg_a, 1), block(neg_sc_woven, FIRST), block(neg_sc_woven, SECOND)]
         num = f32_tile("num", 2 * L)
         inv = f32_tile("inv", 3 * L)
         inv_second = f32_tile("inv_second", L)
         invs = [inv_second[:]] + [block(inv, c) for c in range(3)]
         square = f32_tile("square", 2 * L)
         root = f32_tile("root", 3 * L)
+        roots = [block(root, c) for c in range(3)] + [block(neg_sc_woven, 2)]
         h_i = woven_tile("h_i")
-        score_banks = [banks[0], banks[1], banks[2], banks[3]]
         q_banks = [banks[4], banks[5], banks[0], banks[2]]
 
         def woven(ap):
             return ap.rearrange("q (g t) -> q g t", t=PACK)
 
-        def scores(c, xq_d):
-            product(score_banks[c][:], xq_d, E4M3, (c % 2) * P, wq_d, E4M3, 0, L)
+        def scores(c, xq_half):
+            product(banks[c][:], xq_half, (c % 2) * P, wq_d, E4M3, 0)
 
-        def deal_targets(c, t0=0, t1=PACK):
-            nc.scalar.copy(block(y_dealt, c).rearrange("p (t q) -> p q t", t=PACK)[:, :, t0:t1],
-                           y_chunks[c][:].rearrange("p (q t) -> p q t", t=PACK)[:, :, t0:t1])
+        def deal_targets(c, t0=0):
+            nc.scalar.copy(block(y_dealt, c).rearrange("p (t q) -> p q t", t=PACK)[:, :, t0:PACK],
+                           y_chunks[c][:].rearrange("p (q t) -> p q t", t=PACK)[:, :, t0:PACK])
 
         def targets(c, t0=0):
             for t in range(t0, PACK):
@@ -186,28 +189,22 @@ def tile_attend_gmf_cau_vu_kernel(tc, uT, vT, y, us, ts, offs, uoffs, out_0, out
 
         def scale(c):
             nc.vector.scalar_tensor_tensor(scaled[c].rearrange("p (t q) -> p t q", t=PACK),
-                                           score_banks[c][:].rearrange("p (q t) -> p t q", t=PACK), neg_us[c][:],
+                                           banks[c][:].rearrange("p (q t) -> p t q", t=PACK), neg_us[c][:],
                                            ts_all[:].rearrange("p (t q) -> p t q", t=PACK), MULT, MULT)
 
         def residual(c):
             for t in range(PACK):
                 nc.tensor.matmul(block(q_banks[c], t, P), block(scaled[c], t, P), ident[:],
-                                 start=False, stop=(t == PACK - 1), is_transpose=True)
+                                 start=False, stop=(t == LAST), is_transpose=True)
 
         def neg_q(c):
             return q_banks[c][:].rearrange("q (t g) -> q g t", t=PACK)
-
-        roots = [block(root, c) for c in range(3)] + [block(neg_sc_woven, 2)]
 
         def squares(c, sq):
             nc.scalar.activation(woven(sq), neg_q(c), ACT.Square)
 
         def inverse_root(c, sq):
             nc.scalar.activation(roots[c], sq, ACT.Abs_reciprocal_sqrt, bias=1.0)
-
-        def damping(c, sq):
-            squares(c, sq)
-            inverse_root(c, sq)
 
         def numerator(c, dst):
             nc.vector.tensor_tensor(woven(dst), neg_q(c), woven(block(neg_sc_woven, c)), MULT)
@@ -224,74 +221,67 @@ def tile_attend_gmf_cau_vu_kernel(tc, uT, vT, y, us, ts, offs, uoffs, out_0, out
         out_1_rows = out_1.rearrange("(p t) c -> p t c", t=PACK)
 
         def gene_half(t, k, bank, stage):
-            product(bank[:], wq_i, E4M3, t * P, hq_i, E5M2, k * HALF, k * HALF + L)
+            product(bank[:], wq_i, t * P, hq_i, E5M2, k * HALF)
             nc.scalar.copy(stage, bank[:, HALF:L])
             nc.vector.tensor_copy(gene_windows[t][:].indirect(list_half(gene_list, k)), stage)
 
-        def cell_plane(t, bank):
-            product(bank[:], xq_r[t // 2], E4M3, (t % 2) * P, hq_r, E5M2, 0, L)
-            nc.scalar.copy(dv[t][:], bank[:])
-            nc.vector.tensor_copy(cell_windows[t % 3][:].indirect(cell_list[:]), dv[t][:])
-            nc.sync.dma_start(out_0_rows[:, t, :], cell_windows[t % 3][:])
-
-        first, second = 1, 0
-        direct = 3
-        for t in range(direct):
-            nc.tensor.matmul(block(q_banks[first], t, P), y_chunks[first][:, t:L:PACK], ident[:],
+        for t in range(DIRECT):
+            nc.tensor.matmul(block(q_banks[FIRST], t, P), y_chunks[FIRST][:, t:L:PACK], ident[:],
                              start=(t == 0), stop=False, is_transpose=True)
-        deal_targets(first, direct, PACK)
-        for c in (second, 2, 3):
+        deal_targets(FIRST, DIRECT)
+        for c in (SECOND, 2, LAST):
             deal_targets(c)
-        xq_d = mx_tiles("xq_d", HALF)
-        for c in (first, second):
-            quantize(xq_d, x_d, E4M3, c * P, (c + 1) * P)
-        lap = 2
-        nc.vector.tensor_copy(x_d[:, PACK * (HALF - 16 * lap) + PACK - 1:L * PACK:PACK],
-                              u_planes[3][:].indirect(gene_list[:, LIST_HALF - lap:2 * LIST_HALF]))
-        for c in (first, second):
-            scores(c, xq_d)
-        targets(first, direct)
-        targets(second)
-        for c in (first, second):
+        xq_near = mx_tiles("xq_near", HALF)
+        for c in (FIRST, SECOND):
+            quantize(xq_near, x_d, E4M3, c * P, (c + 1) * P)
+        nc.vector.tensor_copy(x_d[:, PACK * (HALF - 16 * LAP) + LAST:L * PACK:PACK],
+                              u_planes[LAST][:].indirect(gene_list[:, LIST_HALF - LAP:2 * LIST_HALF]))
+        for c in (FIRST, SECOND):
+            scores(c, xq_near)
+        targets(FIRST, DIRECT)
+        targets(SECOND)
+        for c in (FIRST, SECOND):
             scale(c)
             residual(c)
-        xq_far = mx_tiles("xq_far", L, tag=f"neg_us{first}")
+
+        xq_far = mx_tiles("xq_far", L, tag=f"neg_us{FIRST}")
         xq_r = [(xq_far[0][:, HALF:L], xq_far[1][:, HALF:L])]
         quantize(xq_far, x_d, E4M3, HALF, L, -HALF)
         quantize(xq_r[0], x_r, E4M3, 0, HALF)
-        for c in (2, 3):
+        for c in (2, LAST):
             scores(c, xq_far)
-        for c in (first, second):
+
+        for c in (FIRST, SECOND):
             squares(c, block(square, c))
-        for c in (first, second):
+        for c in (FIRST, SECOND):
             inverse_root(c, block(square, c))
-        numerator(first, block(num, first))
-        numerator(second, block(num, second))
-        targets(2)
-        scale(2)
-        residual(2)
-        targets(3)
-        scale(3)
-        residual(3)
-        weigh(first, block(num, first), nc.vector)
-        weigh(second, block(num, second), nc.vector, 2)
-        for c in (first, second):
+        for c in (FIRST, SECOND):
+            numerator(c, block(num, c))
+        for c in (2, LAST):
+            targets(c)
+            scale(c)
+            residual(c)
+        weigh(FIRST, block(num, FIRST), nc.vector)
+        weigh(SECOND, block(num, SECOND), nc.vector, 2)
+        for c in (FIRST, SECOND):
             quantize(hq_i, h_i, E5M2, c * P, (c + 1) * P, HALF)
-        damping(2, block(square, 0))
-        squares(3, block(square, 1))
-        numerator(2, block(num, second))
-        numerator(3, inv_second[:])
-        weigh(2, block(num, second), nc.gpsimd)
+
+        squares(2, block(square, 0))
+        inverse_root(2, block(square, 0))
+        squares(LAST, block(square, 1))
+        numerator(2, block(num, SECOND))
+        numerator(LAST, inv_second[:])
+        weigh(2, block(num, SECOND), nc.gpsimd)
         gene_half(0, 0, banks[6], du[0][:])
-        inverse_root(3, block(square, 1))
+        inverse_root(LAST, block(square, 1))
         gene_half(1, 0, banks[1], du[1][:])
-        weigh(3, inv_second[:], nc.gpsimd, 2)
-        turn_table(x_r, x_d, 1, banks[2])
+        weigh(LAST, inv_second[:], nc.gpsimd, 2)
+        turn_table(x_r, x_d, 1, q_banks[LAST])
         quantize(hq_i, h_i, E5M2, HALF, L, HALF)
         xq_r.append(mx_tiles("xq_r1", HALF, tag="inv"))
         quantize(xq_r[1], x_r, E4M3, HALF, L, -HALF)
         gene_windows.append(f32_tile("gene_window3", T, tag="x_r"))
-        nc.gpsimd.memset(gene_windows[3][:].bitcast(I32), 0)
+        nc.gpsimd.memset(gene_windows[LAST][:].bitcast(I32), 0)
         gene_half(2, 0, banks[3], inv_second[:, 0:HALF])
 
         h_r = woven_tile("h_r")
@@ -305,23 +295,29 @@ def tile_attend_gmf_cau_vu_kernel(tc, uT, vT, y, us, ts, offs, uoffs, out_0, out
                            turned.rearrange("p (s q e) -> p q e s", s=PACK, e=2))
         quantize(hq_r, h_r, E5M2)
 
-        last = PACK - 1
-        product(banks[last][:], wq_i, E4M3, last * P, hq_i, E5M2, HALF, HALF + L)
+        product(banks[LAST][:], wq_i, LAST * P, hq_i, E5M2, HALF)
+        last_stage = h_i[:].bitcast(F32)[:, 0:L]
+        nc.scalar.copy(last_stage, banks[LAST][:])
+        nc.vector.tensor_copy(gene_windows[LAST][:].indirect(gene_list[:]), last_stage)
+        nc.sync.dma_start(out_1_rows[:, LAST, :], gene_windows[LAST][:])
 
-        stage = h_i[:].bitcast(F32)[:, 0:L]
-        nc.scalar.copy(stage, banks[last][:])
-        nc.vector.tensor_copy(gene_windows[last][:].indirect(gene_list[:]), stage)
-        nc.sync.dma_start(out_1_rows[:, last, :], gene_windows[last][:])
         cell_windows = []
 
         def cell_window(tag):
             cell_windows.append(f32_tile(f"cell_window{len(cell_windows)}", T, tag=tag))
             nc.gpsimd.memset(cell_windows[-1][:].bitcast(I32), 0)
 
+        def cell_plane(t):
+            bank = banks[PACK + t]
+            window = cell_windows[t % CELL_WINDOWS]
+            product(bank[:], xq_r[t // 2], (t % 2) * P, hq_r, E5M2, 0)
+            nc.scalar.copy(dv[t][:], bank[:])
+            nc.vector.tensor_copy(window[:].indirect(cell_list[:]), dv[t][:])
+            nc.sync.dma_start(out_0_rows[:, t, :], window[:])
+
         cell_window("h_r")
         cell_window("h_i")
-        cell_plane(0, banks[4])
+        cell_plane(0)
         cell_window("dv0")
-        cell_plane(1, banks[5])
-        cell_plane(2, banks[6])
-        cell_plane(3, banks[7])
+        for t in range(1, PACK):
+            cell_plane(t)

@@ -25,8 +25,6 @@ LAST = PACK - 1
 FIRST, SECOND = 1, 0
 LAP = 2
 DIRECT = 3
-EARLY_PLANES = 3
-CELL_WINDOWS = 3
 FLOPS = 3 * 2 * L * L * L
 BYTES = 4 * (4 * L * T + L * L + L + T) + 2 * 2 * P * 32
 
@@ -56,9 +54,9 @@ def tile_attend_gmf_cau_vu_kernel(tc, uT, vT, y, us, ts, offs, uoffs, out_0, out
             nc.vector.quantize_mx(out=dst[0][:, shift + c0:shift + c1].bitcast(fmt),
                                   scales=dst[1][:, shift + c0:shift + c1], in_=src[:, PACK * c0:PACK * c1])
 
-        def product(out, lhs, m0, rhs, rhs_fmt, n0):
+        def product(out, lhs, m0, rhs, rhs_fmt, n0=0, n1=L):
             nc.tensor.matmul_mx(out=out, lhsT=lhs[0][:, m0:m0 + P].bitcast(E4M3), lhsT_scale=lhs[1][:, m0:m0 + P],
-                                rhs=rhs[0][:, n0:n0 + L].bitcast(rhs_fmt), rhs_scale=rhs[1][:, n0:n0 + L],
+                                rhs=rhs[0][:, n0:n1].bitcast(rhs_fmt), rhs_scale=rhs[1][:, n0:n1],
                                 start=True, stop=True)
 
         def block(tile_, b, width=L):
@@ -73,6 +71,9 @@ def tile_attend_gmf_cau_vu_kernel(tc, uT, vT, y, us, ts, offs, uoffs, out_0, out
         nc.vector.memset(us_table[0:P - 1, :].bitcast(I32), 0)
         nc.vector.memset(ts_table[0:P - 1, :].bitcast(I32), 0)
         make_identity(nc, ident[:])
+        windows = [f32_tile(f"window{k}", T) for k in range(2)]
+        for window in windows:
+            nc.vector.memset(window[:].bitcast(I32), 0)
 
         u_planes = [f32_tile(f"u_plane{t}", T) for t in range(PACK)]
         v_planes = [f32_tile(f"v_plane{t}", T) for t in range(PACK)]
@@ -104,7 +105,7 @@ def tile_attend_gmf_cau_vu_kernel(tc, uT, vT, y, us, ts, offs, uoffs, out_0, out
 
         def turn_table(dst, src, u, bank):
             turned = turn(src, u, bank)
-            nc.scalar.copy(block(dst, u, PAIR).rearrange("q (e p s) -> q e p s", e=2, s=PACK),
+            nc.scalar.copy(dst.rearrange("q (e p s) -> q e p s", e=2, s=PACK),
                            turned.rearrange("q (s p e) -> q e p s", s=PACK, e=2))
 
         ts_listed = f32_tile("ts_listed", L)
@@ -113,7 +114,7 @@ def tile_attend_gmf_cau_vu_kernel(tc, uT, vT, y, us, ts, offs, uoffs, out_0, out
         ts_all = f32_tile("ts_all", L)
         neg_sc = f32_tile("neg_sc", PACK * L)
         neg_sc_woven = f32_tile("neg_sc_woven", PACK * L)
-        nc.vector.tensor_copy(ts_listed[:], ts_table[:].indirect(cell_list[:]))
+        nc.scalar.activation(ts_listed[:], ts_table[:].indirect(cell_list[:]), ACT.Copy)
         for c in range(PACK):
             nc.tensor.transpose(block(banks[0], c, P), block(us_table, c, P), ident[:])
         for c in range(PACK):
@@ -137,25 +138,27 @@ def tile_attend_gmf_cau_vu_kernel(tc, uT, vT, y, us, ts, offs, uoffs, out_0, out
         for t in range(PACK):
             nc.vector.tensor_copy(w_d[:, t:L * PACK:PACK], v_planes[t][:].indirect(cell_list[:]))
             if t % 2 == 1:
-                turn_table(w_i, w_d, t // 2, banks[3 + t // 2])
+                turn_table(block(w_i, t // 2, PAIR), w_d, t // 2, banks[3 + t // 2])
 
-        hq_i = mx_tiles("hq_i", HALF + L, tag="v_plane2", scale_tag="warm")
-        gene_windows = [f32_tile(f"gene_window{t}", T, tag=tag)
-                        for t, tag in enumerate(("ts_table", "v_plane0", "v_plane1"))]
-        for window in gene_windows:
-            nc.gpsimd.memset(window[:].bitcast(I32), 0)
-        nc.gpsimd.memset(hq_i[0][:, 0:HALF], 0)
-        nc.gpsimd.memset(hq_i[1][:, 0:HALF].bitcast(U32), 0)
+        hq_i = mx_tiles("hq_i")
+
+        def zeroed_window(tag):
+            windows.append(f32_tile(f"window{len(windows)}", T, tag=tag))
+            nc.gpsimd.memset(windows[-1][:].bitcast(I32), 0)
+
+        for tag in ("ts_table", "v_plane0", "v_plane1"):
+            zeroed_window(tag)
 
         x_d = woven_tile("x_d")
-        x_r = woven_tile("x_r")
+        x_r = [sb.tile([P, PAIR], BF16, name=f"x_r{u}", align_bytes=64) for u in range(2)]
         wq_d = mx_tiles("wq_d")
         quantize(wq_d, w_d, E4M3)
         nc.vector.tensor_copy(x_d[:, 0:L * PACK:PACK], u_planes[0][:].indirect(gene_list[:]))
         wq_i = mx_tiles("wq_i", tag="u_plane0")
         quantize(wq_i, w_i, E4M3)
+        zeroed_window("neg_sc")
         nc.vector.tensor_copy(x_d[:, 1:L * PACK:PACK], u_planes[1][:].indirect(gene_list[:]))
-        turn_table(x_r, x_d, 0, banks[6])
+        turn_table(x_r[0][:], x_d, 0, banks[6])
         nc.vector.tensor_copy(x_d[:, 2:L * PACK:PACK], u_planes[2][:].indirect(gene_list[:]))
         nc.vector.tensor_copy(x_d[:, LAST:PAIR:PACK], u_planes[LAST][:].indirect(list_half(gene_list, 0)))
 
@@ -176,7 +179,7 @@ def tile_attend_gmf_cau_vu_kernel(tc, uT, vT, y, us, ts, offs, uoffs, out_0, out
             return ap.rearrange("q (g t) -> q g t", t=PACK)
 
         def scores(c, xq_half):
-            product(banks[c][:], xq_half, (c % 2) * P, wq_d, E4M3, 0)
+            product(banks[c][:], xq_half, (c % 2) * P, wq_d, E4M3)
 
         def deal_targets(c, t0=0):
             nc.scalar.copy(block(y_dealt, c).rearrange("p (t q) -> p q t", t=PACK)[:, :, t0:PACK],
@@ -215,15 +218,28 @@ def tile_attend_gmf_cau_vu_kernel(tc, uT, vT, y, us, ts, offs, uoffs, out_0, out
                 nc.scalar.activation(invs[c][:, cols], roots[c][:, cols], ACT.Square)
                 engine.tensor_tensor(block(h_i, c)[:, cols], src[:, cols], invs[c][:, cols], MULT)
 
-        du = [f32_tile(f"du{t}", HALF) for t in range(EARLY_PLANES)]
-        dv = [f32_tile(f"dv{t}", L) for t in range(PACK)]
         out_0_rows = out_0.rearrange("(p t) c -> p t c", t=PACK)
         out_1_rows = out_1.rearrange("(p t) c -> p t c", t=PACK)
 
-        def gene_half(t, k, bank, stage):
-            product(bank[:], wq_i, t * P, hq_i, E5M2, k * HALF)
-            nc.scalar.copy(stage, bank[:, HALF:L])
-            nc.vector.tensor_copy(gene_windows[t][:].indirect(list_half(gene_list, k)), stage)
+        def stage_on_vector(stage, bank):
+            nc.vector.tensor_copy(stage, bank)
+
+        def scatter_on_vector(window, offsets, stage):
+            nc.vector.tensor_copy(window[:].indirect(offsets), stage)
+
+        def stage_on_scalar(stage, bank):
+            nc.scalar.copy(stage, bank)
+
+        def scatter_on_scalar(window, offsets, stage):
+            nc.scalar.activation(window[:].indirect(offsets), stage, ACT.Copy)
+
+        def whole_on_scalar(window, offsets, stage):
+            for k in range(2):
+                scatter_on_scalar(window, list_half(offsets, k), block(stage, k, HALF))
+
+        def gene_product(t, bank, n0, n1):
+            product(bank[:, 0:n1 - n0], wq_i, t * P, hq_i, E5M2, n0, n1)
+            return bank[:, 0:n1 - n0]
 
         for t in range(DIRECT):
             nc.tensor.matmul(block(q_banks[FIRST], t, P), y_chunks[FIRST][:, t:L:PACK], ident[:],
@@ -244,10 +260,8 @@ def tile_attend_gmf_cau_vu_kernel(tc, uT, vT, y, us, ts, offs, uoffs, out_0, out
             scale(c)
             residual(c)
 
-        xq_far = mx_tiles("xq_far", L, tag=f"neg_us{FIRST}")
-        xq_r = [(xq_far[0][:, HALF:L], xq_far[1][:, HALF:L])]
+        xq_far = mx_tiles("xq_far", HALF, tag=f"neg_us{FIRST}")
         quantize(xq_far, x_d, E4M3, HALF, L, -HALF)
-        quantize(xq_r[0], x_r, E4M3, 0, HALF)
         for c in (2, LAST):
             scores(c, xq_far)
 
@@ -264,60 +278,75 @@ def tile_attend_gmf_cau_vu_kernel(tc, uT, vT, y, us, ts, offs, uoffs, out_0, out
         weigh(FIRST, block(num, FIRST), nc.vector)
         weigh(SECOND, block(num, SECOND), nc.vector, 2)
         for c in (FIRST, SECOND):
-            quantize(hq_i, h_i, E5M2, c * P, (c + 1) * P, HALF)
+            quantize(hq_i, h_i, E5M2, c * P, (c + 1) * P)
 
+        near0 = gene_product(0, banks[6], 0, HALF)
+        near1 = gene_product(1, banks[7], 0, HALF)
         squares(2, block(square, 0))
         inverse_root(2, block(square, 0))
         squares(LAST, block(square, 1))
         numerator(2, block(num, SECOND))
         numerator(LAST, inv_second[:])
         weigh(2, block(num, SECOND), nc.gpsimd)
-        gene_half(0, 0, banks[6], du[0][:])
+        stage = block(neg_sc_woven, LAST)[:, 0:HALF]
+        stage_on_vector(stage, near0)
+        scatter_on_vector(windows[0], list_half(gene_list, 0), stage)
         inverse_root(LAST, block(square, 1))
-        gene_half(1, 0, banks[1], du[1][:])
         weigh(LAST, inv_second[:], nc.gpsimd, 2)
-        turn_table(x_r, x_d, 1, q_banks[LAST])
-        quantize(hq_i, h_i, E5M2, HALF, L, HALF)
-        xq_r.append(mx_tiles("xq_r1", HALF, tag="inv"))
-        quantize(xq_r[1], x_r, E4M3, HALF, L, -HALF)
-        gene_windows.append(f32_tile("gene_window3", T, tag="x_r"))
-        nc.gpsimd.memset(gene_windows[LAST][:].bitcast(I32), 0)
-        gene_half(2, 0, banks[3], inv_second[:, 0:HALF])
+        stage = roots[LAST][:, HALF:L]
+        stage_on_scalar(stage, near1)
+        scatter_on_scalar(windows[1], list_half(gene_list, 0), stage)
+        quantize(hq_i, h_i, E5M2, HALF, L)
+        xq_r = [mx_tiles("xq_r0", HALF, tag="inv_second")]
+        quantize(xq_r[0], x_r[0], E4M3, 0, HALF)
+        zeroed_window("x_r0")
+
+        far0 = gene_product(0, banks[1], HALF, L)
+        far1 = gene_product(1, banks[3], HALF, L)
+        whole2 = gene_product(2, banks[4], 0, L)
+        whole3 = gene_product(LAST, banks[5], 0, L)
+        du = [f32_tile(f"du{t}", HALF) for t in range(2)]
+        stage_on_vector(du[0][:], far0)
+        scatter_on_vector(windows[0], list_half(gene_list, 1), du[0][:])
+        nc.sync.dma_start(out_1_rows[:, 0, :], windows[0][:])
+        zeroed_window("du0")
+        stage_on_scalar(du[1][:], far1)
+        scatter_on_scalar(windows[1], list_half(gene_list, 1), du[1][:])
+        nc.sync.dma_start(out_1_rows[:, 1, :], windows[1][:])
+        du2 = f32_tile("du2", L)
+        stage_on_vector(du2[:], whole2)
+        scatter_on_vector(windows[2], gene_list[:], du2[:])
+        nc.sync.dma_start(out_1_rows[:, 2, :], windows[2][:])
 
         h_r = woven_tile("h_r")
-        hq_r = mx_tiles("hq_r")
-        for t in range(EARLY_PLANES):
-            gene_half(t, 1, banks[t], du[t][:])
-            nc.sync.dma_start(out_1_rows[:, t, :], gene_windows[t][:])
+        hq_r = mx_tiles("hq_r", tag="du2")
         for u in range(2):
-            turned = turn(h_i, u, banks[u])
+            turned = turn(h_i, u, banks[1 + 2 * u])
             nc.scalar.copy(h_r[:].rearrange("p (q u e s) -> p u q e s", u=2, e=2, s=PACK)[:, u],
                            turned.rearrange("p (s q e) -> p q e s", s=PACK, e=2))
         quantize(hq_r, h_r, E5M2)
 
-        product(banks[LAST][:], wq_i, LAST * P, hq_i, E5M2, HALF)
         last_stage = h_i[:].bitcast(F32)[:, 0:L]
-        nc.scalar.copy(last_stage, banks[LAST][:])
-        nc.vector.tensor_copy(gene_windows[LAST][:].indirect(gene_list[:]), last_stage)
-        nc.sync.dma_start(out_1_rows[:, LAST, :], gene_windows[LAST][:])
+        stage_on_scalar(last_stage, whole3)
+        whole_on_scalar(windows[LAST], gene_list, last_stage)
+        nc.sync.dma_start(out_1_rows[:, LAST, :], windows[LAST][:])
+        turn_table(x_r[1][:], x_d, 1, banks[5])
 
-        cell_windows = []
+        dv = [f32_tile(f"dv{t}", L) for t in range(PACK)]
 
-        def cell_window(tag):
-            cell_windows.append(f32_tile(f"cell_window{len(cell_windows)}", T, tag=tag))
-            nc.gpsimd.memset(cell_windows[-1][:].bitcast(I32), 0)
+        def cell_plane(t, bank):
+            product(bank[:], xq_r[t // 2], (t % 2) * P, hq_r, E5M2)
+            if t % 2 == 0:
+                stage_on_vector(dv[t][:], bank[:])
+                scatter_on_vector(windows[PACK + t], cell_list[:], dv[t][:])
+            else:
+                stage_on_scalar(dv[t][:], bank[:])
+                whole_on_scalar(windows[PACK + t], cell_list, dv[t])
+            nc.sync.dma_start(out_0_rows[:, t, :], windows[PACK + t][:])
 
-        def cell_plane(t):
-            bank = banks[PACK + t]
-            window = cell_windows[t % CELL_WINDOWS]
-            product(bank[:], xq_r[t // 2], (t % 2) * P, hq_r, E5M2, 0)
-            nc.scalar.copy(dv[t][:], bank[:])
-            nc.vector.tensor_copy(window[:].indirect(cell_list[:]), dv[t][:])
-            nc.sync.dma_start(out_0_rows[:, t, :], window[:])
-
-        cell_window("h_r")
-        cell_window("h_i")
-        cell_plane(0)
-        cell_window("dv0")
-        for t in range(1, PACK):
-            cell_plane(t)
+        cell_plane(0, banks[4])
+        cell_plane(1, banks[5])
+        xq_r.append(mx_tiles("xq_r1", HALF, tag="dv0"))
+        quantize(xq_r[1], x_r[1], E4M3, 0, HALF)
+        cell_plane(2, banks[0])
+        cell_plane(LAST, banks[7])

from contextlib import ExitStack

import concourse.mybir as mybir
from concourse.masks import make_identity

F32 = mybir.dt.float32
BF16 = mybir.dt.bfloat16
U32 = mybir.dt.uint32
I32 = mybir.dt.int32
U16 = mybir.dt.uint16
U8 = mybir.dt.uint8
E4M3 = mybir.dt.float8_e4m3fn_x4
E5M2 = mybir.dt.float8_e5m2_x4
ACT = mybir.ActivationFunctionType
MULT = mybir.AluOpType.mult

P = 128
PACK = 4
L = 512
HALF = L // 2
T = 2048
LIST_HALF = HALF // 16
PAIR = 2 * L
LAST = PACK - 1
FIRST, SECOND = 1, 0
LAP = 2
DIRECT = 3
FLOPS = 3 * 2 * L * L * L
BYTES = 4 * (4 * L * T + L * L + L + T) + 2 * 2 * P * 32


def tile_attend_gmf_cau_vu_kernel(tc, uT, vT, y, us, ts, offs, uoffs, out_0, out_1):
    nc = tc.nc
    with ExitStack() as ctx:
        lists = ctx.enter_context(tc.tile_pool(name="lists", bufs=1))
        sb = ctx.enter_context(tc.tile_pool(name="sb", bufs=1))
        ps = ctx.enter_context(tc.psum_pool(name="ps", bufs=1))

        cell_list = lists.tile([P, L // 16], U16, name="cell_list")
        gene_list = lists.tile([P, L // 16], U16, name="gene_list")
        banks = [ps.tile([P, L], F32, name=f"bank{b}") for b in range(8)]

        def f32_tile(name, width, tag=None):
            return sb.tile([P, width], F32, name=name, tag=tag or name, align_bytes=64)

        def woven_tile(name, tag=None):
            return sb.tile([P, L * PACK], BF16, name=name, tag=tag or name, align_bytes=64)

        def mx_tiles(name, width=L, tag=None, scale_tag=None):
            return (sb.tile([P, width], U32, name=name + "_codes", tag=tag or name + "_codes", align_bytes=64),
                    sb.tile([P, width], U8, name=name + "_scales", tag=scale_tag or name + "_scales", align_bytes=64))

        def quantize(dst, src, fmt, c0=0, c1=L, shift=0):
            nc.vector.quantize_mx(out=dst[0][:, shift + c0:shift + c1].bitcast(fmt),
                                  scales=dst[1][:, shift + c0:shift + c1], in_=src[:, PACK * c0:PACK * c1])

        def product(out, lhs, m0, rhs, rhs_fmt, n0=0, n1=L):
            nc.tensor.matmul_mx(out=out, lhsT=lhs[0][:, m0:m0 + P].bitcast(E4M3), lhsT_scale=lhs[1][:, m0:m0 + P],
                                rhs=rhs[0][:, n0:n1].bitcast(rhs_fmt), rhs_scale=rhs[1][:, n0:n1],
                                start=True, stop=True)

        def block(tile_, b, width=L):
            return tile_[:, b * width:(b + 1) * width]

        def list_half(offsets, k):
            return block(offsets, k, LIST_HALF)

        ident = f32_tile("ident", P)
        ts_table = f32_tile("ts_table", T)
        us_table = f32_tile("us_table", L)
        nc.vector.memset(us_table[0:P - 1, :].bitcast(I32), 0)
        nc.vector.memset(ts_table[0:P - 1, :].bitcast(I32), 0)
        make_identity(nc, ident[:])
        windows = [f32_tile(f"window{k}", T) for k in range(2)]
        for window in windows:
            nc.vector.memset(window[:].bitcast(I32), 0)

        u_planes = [f32_tile(f"u_plane{t}", T) for t in range(PACK)]
        v_planes = [f32_tile(f"v_plane{t}", T) for t in range(PACK)]
        y_chunks = [f32_tile(f"y_chunk{c}", L) for c in range(PACK)]
        uT_rows = uT.rearrange("(p t) c -> p t c", t=PACK)
        vT_rows = vT.rearrange("(p t) c -> p t c", t=PACK)
        nc.sync.dma_start(cell_list[:], offs)
        nc.sync.dma_start(v_planes[0][:], vT_rows[:, 0, :])
        nc.sync.dma_start(gene_list[:], uoffs)
        nc.sync.dma_start(v_planes[1][:], vT_rows[:, 1, :])
        nc.scalar.dma_start(ts_table[P - 1:P, :], ts[0:1, :])
        nc.scalar.dma_start(us_table[P - 1:P, :], us.rearrange("b r o -> b (r o)"))
        for t in range(2, PACK):
            nc.sync.dma_start(v_planes[t][:], vT_rows[:, t, :])
        for t in range(PACK):
            nc.sync.dma_start(u_planes[t][:], uT_rows[:, t, :])
        y_rows = y.rearrange("b (c p) i -> p (b c) i", p=P)
        for c in (FIRST, SECOND, 2, LAST):
            nc.sync.dma_start(y_chunks[c][:], y_rows[:, c, :])

        warm = f32_tile("warm", 8)
        nc.scalar.activation(warm[:, 0:1], ident[:, 0:1], ACT.Abs_reciprocal_sqrt, bias=1.0)

        def turn(src, u, bank):
            words = src[:].bitcast(F32)
            for s in range(PACK):
                nc.tensor.transpose(block(bank, s, P), words[:, 2 * s + u:2 * L:2 * PACK], ident[:])
            return bank[:].bitcast(BF16)

        def turn_table(dst, src, u, bank):
            turned = turn(src, u, bank)
            nc.scalar.copy(dst.rearrange("q (e p s) -> q e p s", e=2, s=PACK),
                           turned.rearrange("q (s p e) -> q e p s", s=PACK, e=2))

        ts_listed = f32_tile("ts_listed", L)
        neg_us = [f32_tile(f"neg_us{c}", 1) for c in range(PACK)]
        ts_cols = f32_tile("ts_cols", PACK)
        ts_all = f32_tile("ts_all", L)
        neg_sc = f32_tile("neg_sc", PACK * L)
        neg_sc_woven = f32_tile("neg_sc_woven", PACK * L)
        nc.scalar.activation(ts_listed[:], ts_table[:].indirect(cell_list[:]), ACT.Copy)
        for c in range(PACK):
            nc.tensor.transpose(block(banks[0], c, P), block(us_table, c, P), ident[:])
        for c in range(PACK):
            nc.scalar.activation(neg_us[c][:], block(banks[0], c, P)[:, P - 1:P], ACT.Copy, scale=-1.0)
        for c in range(PACK):
            nc.tensor.transpose(block(banks[2], c, P), neg_us[c][:].to_broadcast([P, P]), ident[:])
        for t in range(PACK):
            nc.tensor.transpose(block(banks[1], t, P), ts_listed[:, t:L:PACK], ident[:])
        nc.scalar.copy(ts_cols[:], banks[1][:, P - 1:L:P])
        for t in range(PACK):
            nc.tensor.transpose(block(banks[3], t, P), ts_cols[:, t:t + 1].to_broadcast([P, P]), ident[:])
        nc.scalar.copy(ts_all[:], banks[3][:])
        for t in range(PACK):
            nc.scalar.activation(block(neg_sc, t), banks[2][:], ACT.Copy, scale=ts_cols[:, t:t + 1])
        for c in range(PACK):
            nc.scalar.copy(block(neg_sc_woven, c).rearrange("q (g t) -> q g t", t=PACK),
                           neg_sc[:].rearrange("q (t c g) -> q c g t", t=PACK, c=PACK)[:, c])

        w_d = woven_tile("w_d")
        w_i = woven_tile("w_i", tag="neg_sc")
        for t in range(PACK):
            nc.vector.tensor_copy(w_d[:, t:L * PACK:PACK], v_planes[t][:].indirect(cell_list[:]))
            if t % 2 == 1:
                turn_table(block(w_i, t // 2, PAIR), w_d, t // 2, banks[3 + t // 2])

        hq_i = mx_tiles("hq_i")

        def zeroed_window(tag):
            windows.append(f32_tile(f"window{len(windows)}", T, tag=tag))
            nc.gpsimd.memset(windows[-1][:].bitcast(I32), 0)

        for tag in ("ts_table", "v_plane0", "v_plane1"):
            zeroed_window(tag)

        x_d = woven_tile("x_d")
        x_r = [sb.tile([P, PAIR], BF16, name=f"x_r{u}", align_bytes=64) for u in range(2)]
        wq_d = mx_tiles("wq_d")
        quantize(wq_d, w_d, E4M3)
        nc.vector.tensor_copy(x_d[:, 0:L * PACK:PACK], u_planes[0][:].indirect(gene_list[:]))
        wq_i = mx_tiles("wq_i", tag="u_plane0")
        quantize(wq_i, w_i, E4M3)
        zeroed_window("neg_sc")
        nc.vector.tensor_copy(x_d[:, 1:L * PACK:PACK], u_planes[1][:].indirect(gene_list[:]))
        turn_table(x_r[0][:], x_d, 0, banks[6])
        nc.vector.tensor_copy(x_d[:, 2:L * PACK:PACK], u_planes[2][:].indirect(gene_list[:]))
        nc.vector.tensor_copy(x_d[:, LAST:PAIR:PACK], u_planes[LAST][:].indirect(list_half(gene_list, 0)))

        y_dealt = f32_tile("y_dealt", PACK * L)
        neg_a = f32_tile("neg_a", 2 * L)
        scaled = [block(neg_a, 0), block(neg_a, 1), block(neg_sc_woven, FIRST), block(neg_sc_woven, SECOND)]
        num = f32_tile("num", 2 * L)
        inv = f32_tile("inv", 3 * L)
        inv_second = f32_tile("inv_second", L)
        invs = [inv_second[:]] + [block(inv, c) for c in range(3)]
        square = f32_tile("square", 2 * L)
        root = f32_tile("root", 3 * L)
        roots = [block(root, c) for c in range(3)] + [block(neg_sc_woven, 2)]
        h_i = woven_tile("h_i")
        q_banks = [banks[4], banks[5], banks[0], banks[2]]

        def woven(ap):
            return ap.rearrange("q (g t) -> q g t", t=PACK)

        def scores(c, xq_half):
            product(banks[c][:], xq_half, (c % 2) * P, wq_d, E4M3)

        def deal_targets(c, t0=0):
            nc.scalar.copy(block(y_dealt, c).rearrange("p (t q) -> p q t", t=PACK)[:, :, t0:PACK],
                           y_chunks[c][:].rearrange("p (q t) -> p q t", t=PACK)[:, :, t0:PACK])

        def targets(c, t0=0):
            for t in range(t0, PACK):
                nc.tensor.matmul(block(q_banks[c], t, P), block(block(y_dealt, c), t, P), ident[:],
                                 start=(t == 0), stop=False, is_transpose=True)

        def scale(c):
            nc.vector.scalar_tensor_tensor(scaled[c].rearrange("p (t q) -> p t q", t=PACK),
                                           banks[c][:].rearrange("p (q t) -> p t q", t=PACK), neg_us[c][:],
                                           ts_all[:].rearrange("p (t q) -> p t q", t=PACK), MULT, MULT)

        def residual(c):
            for t in range(PACK):
                nc.tensor.matmul(block(q_banks[c], t, P), block(scaled[c], t, P), ident[:],
                                 start=False, stop=(t == LAST), is_transpose=True)

        def neg_q(c):
            return q_banks[c][:].rearrange("q (t g) -> q g t", t=PACK)

        def squares(c, sq):
            nc.scalar.activation(woven(sq), neg_q(c), ACT.Square)

        def inverse_root(c, sq):
            nc.scalar.activation(roots[c], sq, ACT.Abs_reciprocal_sqrt, bias=1.0)

        def numerator(c, dst):
            nc.vector.tensor_tensor(woven(dst), neg_q(c), woven(block(neg_sc_woven, c)), MULT)

        def weigh(c, src, engine, parts=1):
            for k in range(parts):
                cols = slice(k * L // parts, (k + 1) * L // parts)
                nc.scalar.activation(invs[c][:, cols], roots[c][:, cols], ACT.Square)
                engine.tensor_tensor(block(h_i, c)[:, cols], src[:, cols], invs[c][:, cols], MULT)

        out_0_rows = out_0.rearrange("(p t) c -> p t c", t=PACK)
        out_1_rows = out_1.rearrange("(p t) c -> p t c", t=PACK)

        def stage_on_vector(stage, bank):
            nc.vector.tensor_copy(stage, bank)

        def scatter_on_vector(window, offsets, stage):
            nc.vector.tensor_copy(window[:].indirect(offsets), stage)

        def stage_on_scalar(stage, bank):
            nc.scalar.copy(stage, bank)

        def scatter_on_scalar(window, offsets, stage):
            nc.scalar.activation(window[:].indirect(offsets), stage, ACT.Copy)

        def whole_on_scalar(window, offsets, stage):
            for k in range(2):
                scatter_on_scalar(window, list_half(offsets, k), block(stage, k, HALF))

        def gene_product(t, bank, n0, n1):
            product(bank[:, 0:n1 - n0], wq_i, t * P, hq_i, E5M2, n0, n1)
            return bank[:, 0:n1 - n0]

        for t in range(DIRECT):
            nc.tensor.matmul(block(q_banks[FIRST], t, P), y_chunks[FIRST][:, t:L:PACK], ident[:],
                             start=(t == 0), stop=False, is_transpose=True)
        deal_targets(FIRST, DIRECT)
        for c in (SECOND, 2, LAST):
            deal_targets(c)
        xq_near = mx_tiles("xq_near", HALF)
        for c in (FIRST, SECOND):
            quantize(xq_near, x_d, E4M3, c * P, (c + 1) * P)
        nc.vector.tensor_copy(x_d[:, PACK * (HALF - 16 * LAP) + LAST:L * PACK:PACK],
                              u_planes[LAST][:].indirect(gene_list[:, LIST_HALF - LAP:2 * LIST_HALF]))
        for c in (FIRST, SECOND):
            scores(c, xq_near)
        targets(FIRST, DIRECT)
        targets(SECOND)
        for c in (FIRST, SECOND):
            scale(c)
            residual(c)

        xq_far = mx_tiles("xq_far", HALF, tag=f"neg_us{FIRST}")
        quantize(xq_far, x_d, E4M3, HALF, L, -HALF)
        for c in (2, LAST):
            scores(c, xq_far)

        for c in (FIRST, SECOND):
            squares(c, block(square, c))
        for c in (FIRST, SECOND):
            inverse_root(c, block(square, c))
        for c in (FIRST, SECOND):
            numerator(c, block(num, c))
        for c in (2, LAST):
            targets(c)
            scale(c)
            residual(c)
        weigh(FIRST, block(num, FIRST), nc.vector)
        weigh(SECOND, block(num, SECOND), nc.vector, 2)
        for c in (FIRST, SECOND):
            quantize(hq_i, h_i, E5M2, c * P, (c + 1) * P)

        near0 = gene_product(0, banks[6], 0, HALF)
        near1 = gene_product(1, banks[7], 0, HALF)
        squares(2, block(square, 0))
        inverse_root(2, block(square, 0))
        squares(LAST, block(square, 1))
        numerator(2, block(num, SECOND))
        numerator(LAST, inv_second[:])
        weigh(2, block(num, SECOND), nc.gpsimd)
        stage = block(neg_sc_woven, LAST)[:, 0:HALF]
        stage_on_vector(stage, near0)
        scatter_on_vector(windows[0], list_half(gene_list, 0), stage)
        inverse_root(LAST, block(square, 1))
        weigh(LAST, inv_second[:], nc.gpsimd, 2)
        stage = roots[LAST][:, HALF:L]
        stage_on_scalar(stage, near1)
        scatter_on_scalar(windows[1], list_half(gene_list, 0), stage)
        quantize(hq_i, h_i, E5M2, HALF, L)
        xq_r = [mx_tiles("xq_r0", HALF, tag="inv_second")]
        quantize(xq_r[0], x_r[0], E4M3, 0, HALF)
        zeroed_window("x_r0")

        far0 = gene_product(0, banks[1], HALF, L)
        far1 = gene_product(1, banks[3], HALF, L)
        whole2 = gene_product(2, banks[4], 0, L)
        whole3 = gene_product(LAST, banks[5], 0, L)
        du = [f32_tile(f"du{t}", HALF) for t in range(2)]
        stage_on_vector(du[0][:], far0)
        scatter_on_vector(windows[0], list_half(gene_list, 1), du[0][:])
        nc.sync.dma_start(out_1_rows[:, 0, :], windows[0][:])
        zeroed_window("du0")
        stage_on_scalar(du[1][:], far1)
        scatter_on_scalar(windows[1], list_half(gene_list, 1), du[1][:])
        nc.sync.dma_start(out_1_rows[:, 1, :], windows[1][:])
        du2 = f32_tile("du2", L)
        stage_on_vector(du2[:], whole2)
        scatter_on_vector(windows[2], gene_list[:], du2[:])
        nc.sync.dma_start(out_1_rows[:, 2, :], windows[2][:])

        h_r = woven_tile("h_r")
        hq_r = mx_tiles("hq_r", tag="du2")
        for u in range(2):
            turned = turn(h_i, u, banks[1 + 2 * u])
            nc.scalar.copy(h_r[:].rearrange("p (q u e s) -> p u q e s", u=2, e=2, s=PACK)[:, u],
                           turned.rearrange("p (s q e) -> p q e s", s=PACK, e=2))
        quantize(hq_r, h_r, E5M2)

        last_stage = h_i[:].bitcast(F32)[:, 0:L]
        stage_on_scalar(last_stage, whole3)
        whole_on_scalar(windows[LAST], gene_list, last_stage)
        nc.sync.dma_start(out_1_rows[:, LAST, :], windows[LAST][:])
        turn_table(x_r[1][:], x_d, 1, banks[5])

        dv = [f32_tile(f"dv{t}", L) for t in range(PACK)]

        def cell_plane(t, bank):
            product(bank[:], xq_r[t // 2], (t % 2) * P, hq_r, E5M2)
            if t % 2 == 0:
                stage_on_vector(dv[t][:], bank[:])
                scatter_on_vector(windows[PACK + t], cell_list[:], dv[t][:])
            else:
                stage_on_scalar(dv[t][:], bank[:])
                whole_on_scalar(windows[PACK + t], cell_list, dv[t])
            nc.sync.dma_start(out_0_rows[:, t, :], windows[PACK + t][:])

        cell_plane(0, banks[4])
        cell_plane(1, banks[5])
        xq_r.append(mx_tiles("xq_r1", HALF, tag="dv0"))
        quantize(xq_r[1], x_r[1], E4M3, 0, HALF)
        cell_plane(2, banks[0])
        cell_plane(LAST, banks[7])
